import numpy as np
import ml_dtypes


def mxq(x, axis, fmt="e4m3"):
    dtype, down = {"e4m3": (ml_dtypes.float8_e4m3fn, 7), "e5m2": (ml_dtypes.float8_e5m2, 14)}[fmt]
    v = np.moveaxis(np.asarray(x, np.float32).astype(ml_dtypes.bfloat16).astype(np.float64), axis, -1)
    blocks = v.reshape(v.shape[:-1] + (-1, 32))
    amax = np.abs(blocks).max(-1, keepdims=True)
    byte = np.maximum(np.where(amax > 0, np.frexp(amax)[1] - 1 + 127, 0) - down, 1)
    scale = np.exp2(byte - 127.0)
    codes = (blocks / scale).astype(np.float32).astype(dtype).astype(np.float64)
    return np.moveaxis((codes * scale).reshape(v.shape), -1, axis)


WIDE = False


def mx_kscale(k):
    if not WIDE:
        return np.ones(k)
    levels = np.array([18, -18])
    if k % 512:
        return np.exp2(np.random.permutation(np.resize(levels, k // 32))).repeat(32)
    a = np.empty((k // 512, 16))
    for p in range(k // 512):
        a[p, :8] = np.random.permutation(np.resize(levels, 8))
        for g in range(8):
            far = levels[np.abs(levels - a[p, g]) >= 10]
            a[p, g + 8] = far[np.random.randint(len(far))]
    return np.exp2(a.ravel()).repeat(32)


def f64(x):
    return np.asarray(x).astype(np.float64)


def striped(idx):
    return np.tile(np.asarray(idx).reshape(-1, 16).T, (8, 1)).astype(np.uint16)


def unstriped(offs):
    return offs[:16].T.reshape(-1).astype(np.int64)

def planes(y):
    n, m = y.shape
    v = y.astype(np.float32).astype(ml_dtypes.bfloat16).astype(np.float64).reshape(n // 32, 32, m)
    top = np.abs(v).max(1)
    byte = np.clip(np.where(top > 0, np.frexp(top)[1] - 1 + 127 - 7, 1), 1, 254)
    codes = (v * np.exp2(127.0 - byte)[:, None, :]).reshape(n, m).astype(np.float32).astype(ml_dtypes.float8_e4m3fn).view(np.uint8)
    words = codes.reshape(n // 512, 128, 4, m).transpose(0, 1, 3, 2)
    return np.ascontiguousarray(words), np.ascontiguousarray(byte.astype(np.uint8).reshape(n // 512, 16, m))


def sig(x):
    return 1.0 / (1.0 + np.exp(-x))


def setup_inputs():
    n = np.random.standard_normal
    uni = np.random.uniform
    ctx = np.random.permutation(2048)[:1024]
    posn = np.random.permutation(np.repeat(np.arange(512), 2))
    slot = np.argsort(posn, kind="stable")
    idx = np.random.permutation(2048)[:512]
    f_d = mx_kscale(512)
    f_i = np.ones(2048)
    f_i[idx] = mx_kscale(512)
    return {
        "eT": (np.round(n((512, 2048)) * 32) / 32 * f_d[:, None]).astype(np.float32),
        "wT": (n((512, 2048)) / np.sqrt(512) / f_d[:, None] * f_i[None, :]).astype(np.float32),
        "ts": np.tile(uni(0.75, 1.3, 2048) / f_i, (128, 1)).astype(np.float32),
        "ux": (uni(0.75, 1.3, (512, 1))).astype(np.float32),
        "y": (np.random.randint(0, 2, (512, 512))).astype(np.float32),
        "coffs": striped(ctx),
        "posnoffs": striped(posn),
        "slotoffs": striped(slot),
        "offs": striped(idx),
    }


def reference(eT, wT, ts, ux, y, coffs, posnoffs, slotoffs, offs):
    ctx = unstriped(coffs)
    posn = unstriped(posnoffs)
    slot = unstriped(slotoffs)
    idx = unstriped(offs)
    eT_c = f64(eT)[:, ctx]
    wT_i = f64(wT)[:, idx]
    ts_i = f64(ts)[:1][:, idx]
    es = eT_c[:, slot]
    s = es.reshape(512, 512, 2).sum(-1)
    h = s / 2.0
    a = mxq(h, 0, "e4m3").T @ mxq(wT_i, 0, "e4m3")
    g = f64(ux) * ts_i * (sig(f64(ux) * ts_i * a) - f64(y))
    dh = mxq(wT_i, 1, "e4m3") @ mxq(g, 1, "e5m2").T
    dc = dh[:, posn]
    de = dc / 2.0
    out_0 = np.zeros((512, 2048))
    out_0[:, ctx] = de
    return (out_0,) + planes(out_0)

@@ -1,0 +1,268 @@
+from contextlib import ExitStack
+
+import concourse.mybir as mybir
+from concourse.masks import make_identity
+
+FLOPS = 2 * 2 * 512 * 512 * 512
+
+F32 = mybir.dt.float32
+BF16 = mybir.dt.bfloat16
+I32 = mybir.dt.int32
+U32 = mybir.dt.uint32
+U16 = mybir.dt.uint16
+U8 = mybir.dt.uint8
+E4M3 = mybir.dt.float8_e4m3fn_x4
+E5M2 = mybir.dt.float8_e5m2_x4
+ALU = mybir.AluOpType
+ACT = mybir.ActivationFunctionType
+
+P = 128
+LANES = 4
+WORDS = 2048
+SLOTS = 1024
+POS = 512
+OUTW = 512
+DH_WINDOW = 1376
+TAIL_CHUNK = 256
+RUN = 4
+
+
+def tile_attend_gcbow_ns_pl_kernel(tc, eT, wT, ts, ux, y, coffs, posnoffs, slotoffs, offs, out_0, out_1, out_2):
+    nc = tc.nc
+    with ExitStack() as ctx:
+        keep = ctx.enter_context(tc.tile_pool(name="keep", bufs=1))
+        ring = ctx.enter_context(tc.tile_pool(name="ring", bufs=2))
+        turn_ps = ctx.enter_context(tc.psum_pool(name="turn", bufs=2))
+        mm_ps = ctx.enter_context(tc.psum_pool(name="mm", bufs=2))
+        dh_pool = ctx.enter_context(tc.psum_pool(name="dh", bufs=1))
+
+        ctx_list = keep.tile([P, SLOTS // 16], U16, name="ctx_list")
+        posn_list = keep.tile([P, SLOTS // 16], U16, name="posn_list")
+        slot_list = keep.tile([P, SLOTS // 16], U16, name="slot_list")
+        idx_list = keep.tile([P, OUTW // 16], U16, name="idx_list")
+        e_rows = eT.rearrange("(p t) c -> p t c", t=LANES)
+        w_rows = wT.rearrange("(p t) c -> p t c", t=LANES)
+        out_rows = out_0.rearrange("(p t) c -> p t c", t=LANES)
+        e_lane = [keep.tile([P, WORDS], F32, name="e_lane%d" % t) for t in range(LANES)]
+        w_half = [[keep.tile([P, WORDS // 2], F32, name="w_half%d%d" % (t, u)) for u in range(2)] for t in range(LANES)]
+        grad = [keep.tile([P, WORDS], F32, name="grad%d" % t, tag="grad%d" % t) for t in range(LANES)]
+        ts_table = keep.tile([P, WORDS], F32, name="ts_table")
+        y_half = [keep.tile([P, 2, OUTW], F32, name="y_half%d" % u) for u in range(2)]
+        ux_rows = keep.tile([P, P], F32, name="ux_rows")
+        ident32 = keep.tile([P, P], F32, name="ident32")
+        ident16 = keep.tile([P, P], BF16, name="ident16")
+        halves = keep.tile([P, SLOTS], F32, name="halves")
+        dh = keep.tile([P, (LANES - 1) * POS + DH_WINDOW], F32, name="dh")
+
+        order = [1, 3, 2, 0]
+
+        make_identity(nc, ident32[:])
+        nc.gpsimd.memset(ux_rows[:], 0.0)
+        nc.gpsimd.memset(ts_table[:], 0.0)
+        make_identity(nc, ident16[:])
+        nc.vector.memset(grad[order[0]][:], 0.0)
+        nc.vector.memset(grad[order[1]][:], 0.0)
+        nc.gpsimd.memset(dh[:, LANES * POS :], 0.0)
+        nc.gpsimd.memset(halves[:], 0.5)
+        nc.gpsimd.memset(grad[order[2]][:], 0.0)
+        nc.gpsimd.memset(grad[order[3]][:], 0.0)
+        warm = keep.tile([P, 1], F32, name="warm")
+        nc.scalar.activation(warm[:], ident32[:, 0:1], ACT.Sigmoid)
+
+        nc.sync.dma_start(ctx_list[:], coffs)
+        nc.sync.dma_start(e_lane[0][:], e_rows[:, 0, :])
+        nc.sync.dma_start(slot_list[:], slotoffs)
+        nc.sync.dma_start(idx_list[:], offs)
+        y_rows = y.rearrange("(q p) i -> p q i", p=P)
+        for t in range(LANES):
+            if t > 0:
+                nc.sync.dma_start(e_lane[t][:], e_rows[:, t, :])
+            if t == 1:
+                nc.sync.dma_start(ux_rows[0:LANES, :], ux.rearrange("(q p) o -> q (p o)", p=P))
+                nc.sync.dma_start(ts_table[0:1, :], ts[0:1, :])
+            if t in (1, 2):
+                nc.sync.dma_start(y_half[t - 1][:], y_rows[:, 2 * (t - 1) : 2 * t, :])
+            for u in range(2):
+                nc.sync.dma_start(w_half[t][u][:], w_rows[:, t, 1024 * u : 1024 * (u + 1)])
+        nc.sync.dma_start(posn_list[:], posnoffs)
+
+        ux_ps = turn_ps.tile([P, P], F32, name="ux_ps", tag="turn")
+        nc.tensor.transpose(ux_ps[:], ux_rows[:], ident32[:])
+        ux_col = keep.tile([P, LANES], F32, name="ux_col", tag="column")
+        m2ux = keep.tile([P, LANES], F32, name="m2ux")
+        nc.scalar.copy(ux_col[:], ux_ps[:, 0:LANES])
+        nc.scalar.activation(m2ux[:], ux_ps[:, 0:LANES], ACT.Copy, scale=-2.0)
+        pairs = keep.tile([P, LANES, SLOTS], F32, name="pairs", tag="pairs_out", align_bytes=64)
+        w_by_d = keep.tile([P, OUTW, LANES], BF16, name="w_by_d", align_bytes=64)
+        w_by_i = keep.tile([P, OUTW, LANES], BF16, name="w_by_i", align_bytes=64)
+        w_i = keep.tile([P, LANES, OUTW], BF16, name="w_i")
+        ts_i = keep.tile([P, OUTW], F32, name="ts_i")
+        signed_ux = keep.tile([P, LANES, LANES, P], F32, name="signed_ux")
+        factor = keep.tile([P, LANES, POS], F32, name="factor")
+
+        def sign_labels(q):
+            nc.scalar.activation(
+                signed_ux[:, q, :, :].rearrange("p r s -> p s r"),
+                y_half[q // 2][:, q % 2, :].rearrange("p (s r) -> p s r", r=LANES),
+                ACT.Identity, bias=ux_col[:, q : q + 1], scale=m2ux[:, q : q + 1])
+
+        def turn_factors():
+            ts_ps = turn_ps.tile([P, LANES, P], F32, name="ts_ps", tag="turn")
+            for r in range(LANES):
+                nc.tensor.transpose(ts_ps[:, r, :], ts_i[:, r:OUTW:LANES], ident32[:])
+            ts_col = keep.tile([P, LANES], F32, name="ts_col", tag="column")
+            nc.scalar.copy(ts_col[:], ts_ps[:, :, 0])
+            for r in range(LANES):
+                f_ps = turn_ps.tile([P, LANES, P], F32, name="f_ps", tag="turn")
+                for q in range(LANES):
+                    nc.tensor.transpose(f_ps[:, q, :], signed_ux[:, q, r, :], ident32[:])
+                nc.scalar.activation(
+                    factor[:, r, :], f_ps[:].rearrange("s q p -> s (q p)"), ACT.Copy, scale=ts_col[:, r : r + 1])
+
+        for t in range(LANES):
+            half_ec = ring.tile([P, SLOTS], F32, name="half_ec", tag="slots")
+            for u in range(2):
+                nc.vector.tensor_scalar(
+                    half_ec[:, 512 * u : 512 * (u + 1)], e_lane[t][:].indirect(ctx_list[:, 32 * u : 32 * (u + 1)]),
+                    0.5, 0.0, ALU.mult, ALU.add)
+            if t == 1:
+                nc.vector.tensor_copy(ts_i[:], ts_table[:].indirect(idx_list[:]))
+            for u in range(2):
+                nc.vector.tensor_copy(
+                    pairs[:, t, 512 * u : 512 * (u + 1)], half_ec[:].indirect(slot_list[:, 32 * u : 32 * (u + 1)]))
+
+            w_bf = ring.tile([P, WORDS], BF16, name="w_bf")
+            for u in range(2):
+                nc.scalar.copy(w_bf[:, 1024 * u : 1024 * (u + 1)], w_half[t][u][:])
+            nc.scalar.activation(
+                w_i[:, t, :].rearrange("p (r s) -> p s r", r=LANES), w_bf[:].indirect(idx_list[:]), ACT.Copy)
+            if t < 2:
+                sign_labels(2 * t)
+                sign_labels(2 * t + 1)
+            if t == 1:
+                turn_factors()
+        nc.scalar.copy(
+            w_by_d[:].rearrange("p (k i) t -> p k t i", i=RUN), w_i[:].rearrange("p t (k i) -> p k t i", i=RUN))
+
+        for t in order:
+            w_ps = turn_ps.tile([P, LANES, P], BF16, name="w_ps", tag="turn")
+            for r in range(LANES):
+                nc.tensor.transpose(w_ps[:, r, :], w_by_d[:, P * r : P * (r + 1), t], ident16[:])
+            nc.scalar.copy(w_by_i[:, P * t : P * (t + 1), :], w_ps[:].rearrange("s r c -> s c r"))
+
+        def mx_tiles(name, width):
+            codes = keep.tile([P, width], U32, name=name + "_codes", align_bytes=64)
+            scales = keep.tile([P, width], U8, name=name + "_scales", align_bytes=64)
+            return codes, scales
+
+        def quantize(operand, grouped, cols, fmt):
+            nc.vector.quantize_mx(
+                out=operand[0][:, cols].bitcast(fmt), scales=operand[1][:, cols],
+                in_=grouped[:, cols, :].rearrange("p c l -> p (c l)"))
+
+        h_mx = mx_tiles("h", POS)
+        g_mx = mx_tiles("g", POS)
+        wd_mx = mx_tiles("wd", OUTW)
+        wi_mx = mx_tiles("wi", OUTW)
+        h_bf = keep.tile([P, POS, LANES], BF16, name="h_bf", align_bytes=64)
+        g_bf = keep.tile([P, POS, LANES], BF16, name="g_bf", align_bytes=64)
+        chunks = [slice(P * c, P * (c + 1)) for c in range(POS // P)]
+        pair_view = pairs[:].rearrange("p t (k i j) -> p k t i j", i=2, j=2)
+
+        def pair_sum(c):
+            ks = slice(64 * c, 64 * (c + 1))
+            nc.vector.tensor_tensor(
+                h_bf[:, chunks[c], :].rearrange("p (k i) t -> p k t i", i=2),
+                pair_view[:, ks, :, :, 0], pair_view[:, ks, :, :, 1], ALU.add)
+
+        sig = {}
+
+        def score(c):
+            a_ps = mm_ps.tile([P, LANES, P], F32, name="a_ps", tag="score")
+            for r in range(LANES):
+                cols = slice(P * r, P * (r + 1))
+                nc.tensor.matmul_mx(
+                    out=a_ps[:, r, :], lhsT=wd_mx[0][:, cols].bitcast(E4M3), lhsT_scale=wd_mx[1][:, cols],
+                    rhs=h_mx[0][:, chunks[c]].bitcast(E4M3), rhs_scale=h_mx[1][:, chunks[c]], start=True, stop=True)
+            z = ring.tile([P, LANES, P], F32, name="z")
+            nc.vector.tensor_tensor(z[:], a_ps[:], factor[:, :, chunks[c]], ALU.mult)
+            sig[c] = ring.tile([P, LANES, P], F32, name="sig")
+            nc.scalar.activation(sig[c][:], z[:], ACT.Sigmoid)
+
+        def loss_gradient(c):
+            nc.vector.tensor_tensor(
+                g_bf[:, chunks[c], :].rearrange("s (k i) r -> s k r i", i=RUN),
+                sig[c][:].rearrange("s r (k i) -> s k r i", i=RUN),
+                factor[:, :, chunks[c]].rearrange("s r (k i) -> s k r i", i=RUN), ALU.mult)
+
+        pair_sum(0)
+        for c in range(4):
+            if c < 3:
+                pair_sum(c + 1)
+            else:
+                quantize(wd_mx, w_by_d, slice(0, OUTW), E4M3)
+            quantize(h_mx, h_bf, chunks[c], E4M3)
+        score(0)
+        score(1)
+        quantize(wi_mx, w_by_i, slice(0, OUTW), E4M3)
+        for c in range(4):
+            loss_gradient(c)
+            if c < 2:
+                score(c + 2)
+            if c > 0:
+                quantize(g_mx, g_bf, chunks[c - 1], E5M2)
+        quantize(g_mx, g_bf, chunks[3], E5M2)
+
+        dh_ps = {}
+        for j in order:
+            cols = slice(P * j, P * (j + 1))
+            dh_ps[j] = dh_pool.tile([P, POS], F32, name="dh_ps%d" % j)
+            nc.tensor.matmul_mx(
+                out=dh_ps[j][:], lhsT=wi_mx[0][:, cols].bitcast(E4M3), lhsT_scale=wi_mx[1][:, cols],
+                rhs=g_mx[0][:].bitcast(E5M2), rhs_scale=g_mx[1][:], start=True, stop=True)
+        start = {j: POS * (LANES - 1 - n) for n, j in enumerate(order)}
+        for j in order:
+            nc.scalar.copy(dh[:, start[j] : start[j] + POS], dh_ps[j][:])
+
+        out_bf = keep.tile([P, WORDS, LANES], BF16, name="out_bf", tag="pairs_out", align_bytes=64)
+        by_slot = {}
+
+        def look_up(j):
+            if j == order[-1]:
+                by_slot[j] = keep.tile([P, SLOTS], F32, name="dc_last", tag="grad%d" % order[0])
+            else:
+                by_slot[j] = ring.tile([P, SLOTS], F32, name="dc", tag="slots")
+            nc.vector.tensor_copy(by_slot[j][:], dh[:, start[j] : start[j] + DH_WINDOW].indirect(posn_list[:]))
+
+        def place(j):
+            nc.vector.tensor_tensor(grad[j][:].indirect(ctx_list[:]), by_slot[j][:], halves[:], ALU.mult)
+            nc.sync.dma_start(out_rows[:, j, :], grad[j][:])
+
+        look_up(order[0])
+        for n, j in enumerate(order[:-1]):
+            if n + 2 < LANES:
+                look_up(order[n + 1])
+            place(j)
+            nc.scalar.copy(out_bf[:, :, j], grad[j][:])
+        look_up(order[-1])
+        place(order[-1])
+
+        last = order[-1]
+        out_codes = keep.tile([P, WORDS], U32, name="out_codes", align_bytes=64)
+        out_scales = keep.tile([P, WORDS], U8, name="out_scales", align_bytes=64)
+        words_hbm = out_1[0].rearrange("p c l -> p (c l)").bitcast(I32)
+        pieces = [slice(TAIL_CHUNK * n, TAIL_CHUNK * (n + 1)) for n in range(WORDS // TAIL_CHUNK)]
+        half = len(pieces) // 2
+        for n in range(half):
+            nc.scalar.copy(out_bf[:, pieces[half + n], last], grad[last][:, pieces[half + n]])
+        nc.vector.tensor_copy(out_bf[:, pieces[0], last], grad[last][:, pieces[0]])
+        for n in range(len(pieces)):
+            if n + 1 < half:
+                nc.vector.tensor_copy(out_bf[:, pieces[n + 1], last], grad[last][:, pieces[n + 1]])
+            quantize((out_codes, out_scales), out_bf, pieces[n], E4M3)
+            if n % 2 == 1:
+                cols = slice(pieces[n - 1].start, pieces[n].stop)
+                nc.sync.dma_start(words_hbm[:, cols], out_codes[:, cols].bitcast(I32))
+        scales_hbm = out_2[0].bitcast(I32)
+        for quad in range(4):
+            nc.scalar.dma_start(scales_hbm[4 * quad : 4 * quad + 4, :], out_scales[32 * quad : 32 * quad + 4, :].bitcast(I32))

@@ -45,27 +45,27 @@ def tile_attend_gcbow_ns_pl_kernel(tc, eT, wT, ts, ux, y, coffs, posnoffs, sloto
         out_rows = out_0.rearrange("(p t) c -> p t c", t=LANES)
         e_lane = [keep.tile([P, WORDS], F32, name="e_lane%d" % t) for t in range(LANES)]
         w_half = [[keep.tile([P, WORDS // 2], F32, name="w_half%d%d" % (t, u)) for u in range(2)] for t in range(LANES)]
-        grad = [keep.tile([P, WORDS], F32, name="grad%d" % t, tag="grad%d" % t) for t in range(LANES)]
         ts_table = keep.tile([P, WORDS], F32, name="ts_table")
         y_half = [keep.tile([P, 2, OUTW], F32, name="y_half%d" % u) for u in range(2)]
         ux_rows = keep.tile([P, P], F32, name="ux_rows")
         ident32 = keep.tile([P, P], F32, name="ident32")
         ident16 = keep.tile([P, P], BF16, name="ident16")
-        halves = keep.tile([P, SLOTS], F32, name="halves")
-        dh = keep.tile([P, (LANES - 1) * POS + DH_WINDOW], F32, name="dh")
+        dh = keep.tile([P, LANES * POS], F32, name="dh")
 
         order = [1, 3, 2, 0]
 
         make_identity(nc, ident32[:])
         nc.gpsimd.memset(ux_rows[:], 0.0)
-        nc.gpsimd.memset(ts_table[:], 0.0)
         make_identity(nc, ident16[:])
-        nc.vector.memset(grad[order[0]][:], 0.0)
-        nc.vector.memset(grad[order[1]][:], 0.0)
-        nc.gpsimd.memset(dh[:, LANES * POS :], 0.0)
-        nc.gpsimd.memset(halves[:], 0.5)
-        nc.gpsimd.memset(grad[order[2]][:], 0.0)
-        nc.gpsimd.memset(grad[order[3]][:], 0.0)
+        nc.vector.memset(ts_table[:].bitcast(I32), 0)
+        grad = {}
+
+        def clear(j, tag):
+            grad[j] = keep.tile([P, WORDS], F32, name="grad%d" % j, tag=tag, align_bytes=64)
+            nc.vector.memset(grad[j][:].bitcast(I32), 0)
+
+        clear(order[0], "first_window")
+        clear(order[1], "second_window")
         warm = keep.tile([P, 1], F32, name="warm")
         nc.scalar.activation(warm[:], ident32[:, 0:1], ACT.Sigmoid)
 
@@ -98,7 +98,7 @@ def tile_attend_gcbow_ns_pl_kernel(tc, eT, wT, ts, ux, y, coffs, posnoffs, sloto
         w_i = keep.tile([P, LANES, OUTW], BF16, name="w_i")
         ts_i = keep.tile([P, OUTW], F32, name="ts_i")
         signed_ux = keep.tile([P, LANES, LANES, P], F32, name="signed_ux")
-        factor = keep.tile([P, LANES, POS], F32, name="factor")
+        factor = keep.tile([P, LANES, POS], F32, name="factor", tag="factor_window", align_bytes=64)
 
         def sign_labels(q):
             nc.scalar.activation(
@@ -165,7 +165,7 @@ def tile_attend_gcbow_ns_pl_kernel(tc, eT, wT, ts, ux, y, coffs, posnoffs, sloto
         wd_mx = mx_tiles("wd", OUTW)
         wi_mx = mx_tiles("wi", OUTW)
         h_bf = keep.tile([P, POS, LANES], BF16, name="h_bf", align_bytes=64)
-        g_bf = keep.tile([P, POS, LANES], BF16, name="g_bf", align_bytes=64)
+        g_bf = keep.tile([P, POS, LANES], BF16, name="g_bf", tag="g_window", align_bytes=64)
         chunks = [slice(P * c, P * (c + 1)) for c in range(POS // P)]
         pair_view = pairs[:].rearrange("p t (k i j) -> p k t i j", i=2, j=2)
 
@@ -213,6 +213,8 @@ def tile_attend_gcbow_ns_pl_kernel(tc, eT, wT, ts, ux, y, coffs, posnoffs, sloto
                 quantize(g_mx, g_bf, chunks[c - 1], E5M2)
         quantize(g_mx, g_bf, chunks[3], E5M2)
 
+        clear(order[2], "g_window")
+        clear(order[3], "factor_window")
         dh_ps = {}
         for j in order:
             cols = slice(P * j, P * (j + 1))
@@ -222,20 +224,25 @@ def tile_attend_gcbow_ns_pl_kernel(tc, eT, wT, ts, ux, y, coffs, posnoffs, sloto
                 rhs=g_mx[0][:].bitcast(E5M2), rhs_scale=g_mx[1][:], start=True, stop=True)
         start = {j: POS * (LANES - 1 - n) for n, j in enumerate(order)}
         for j in order:
-            nc.scalar.copy(dh[:, start[j] : start[j] + POS], dh_ps[j][:])
+            nc.scalar.activation(dh[:, start[j] : start[j] + POS], dh_ps[j][:], ACT.Copy, scale=0.5)
 
         out_bf = keep.tile([P, WORDS, LANES], BF16, name="out_bf", tag="pairs_out", align_bytes=64)
         by_slot = {}
 
         def look_up(j):
             if j == order[-1]:
-                by_slot[j] = keep.tile([P, SLOTS], F32, name="dc_last", tag="grad%d" % order[0])
+                by_slot[j] = keep.tile([P, SLOTS], F32, name="dc_last", tag="first_window", align_bytes=64)
             else:
                 by_slot[j] = ring.tile([P, SLOTS], F32, name="dc", tag="slots")
-            nc.vector.tensor_copy(by_slot[j][:], dh[:, start[j] : start[j] + DH_WINDOW].indirect(posn_list[:]))
+            width = min(LANES * POS - start[j], 3 * POS)
+            piece = SLOTS if width > SLOTS else width // 2
+            for a in range(0, SLOTS, piece):
+                nc.vector.tensor_copy(
+                    by_slot[j][:, a : a + piece],
+                    dh[:, start[j] : start[j] + width].indirect(posn_list[:, a // 16 : (a + piece) // 16]))
 
         def place(j):
-            nc.vector.tensor_tensor(grad[j][:].indirect(ctx_list[:]), by_slot[j][:], halves[:], ALU.mult)
+            nc.vector.tensor_copy(grad[j][:].indirect(ctx_list[:]), by_slot[j][:])
             nc.sync.dma_start(out_rows[:, j, :], grad[j][:])
 
         look_up(order[0])

@@ -25,6 +25,7 @@ OUTW = 512
 DH_WINDOW = 1376
 TAIL_CHUNK = 256
 RUN = 4
+TS_SPLIT = 704
 
 
 def tile_attend_gcbow_ns_pl_kernel(tc, eT, wT, ts, ux, y, coffs, posnoffs, slotoffs, offs, out_0, out_1, out_2):
@@ -44,9 +45,13 @@ def tile_attend_gcbow_ns_pl_kernel(tc, eT, wT, ts, ux, y, coffs, posnoffs, sloto
         w_rows = wT.rearrange("(p t) c -> p t c", t=LANES)
         out_rows = out_0.rearrange("(p t) c -> p t c", t=LANES)
         e_lane = [keep.tile([P, WORDS], F32, name="e_lane%d" % t) for t in range(LANES)]
-        w_half = [[keep.tile([P, WORDS // 2], F32, name="w_half%d%d" % (t, u)) for u in range(2)] for t in range(LANES)]
+        in_halves = [slice(0, WORDS // 2), slice(WORDS // 2, WORDS)]
+        w_cols = [in_halves, [slice(0, WORDS)], [slice(0, WORDS)], in_halves]
+        w_part = [
+            [keep.tile([P, cols.stop - cols.start], F32, name="w%d_%d" % (t, cols.start)) for cols in w_cols[t]]
+            for t in range(LANES)]
         ts_table = keep.tile([P, WORDS], F32, name="ts_table")
-        y_half = [keep.tile([P, 2, OUTW], F32, name="y_half%d" % u) for u in range(2)]
+        y_half = [keep.tile([P, 2, OUTW], F32, name="y_half%d" % u, tag="y_half%d" % u, align_bytes=64) for u in range(2)]
         ux_rows = keep.tile([P, P], F32, name="ux_rows")
         ident32 = keep.tile([P, P], F32, name="ident32")
         ident16 = keep.tile([P, P], BF16, name="ident16")
@@ -54,125 +59,149 @@ def tile_attend_gcbow_ns_pl_kernel(tc, eT, wT, ts, ux, y, coffs, posnoffs, sloto
 
         order = [1, 3, 2, 0]
 
+        nc.gpsimd.memset(ts_table[:, TS_SPLIT:], 0.0)
+        nc.vector.memset(ts_table[:, :TS_SPLIT], 0.0)
+        nc.vector.memset(ux_rows[:], 0.0)
         make_identity(nc, ident32[:])
-        nc.gpsimd.memset(ux_rows[:], 0.0)
         make_identity(nc, ident16[:])
-        nc.vector.memset(ts_table[:].bitcast(I32), 0)
         grad = {}
 
-        def clear(j, tag):
+        def clear(engine, j, tag):
             grad[j] = keep.tile([P, WORDS], F32, name="grad%d" % j, tag=tag, align_bytes=64)
-            nc.vector.memset(grad[j][:].bitcast(I32), 0)
+            engine.memset(grad[j][:], 0.0)
 
-        clear(order[0], "first_window")
-        clear(order[1], "second_window")
+        clear(nc.vector, order[0], "first_window")
+        clear(nc.gpsimd, order[1], "second_window")
+        clear(nc.gpsimd, order[2], "third_window")
         warm = keep.tile([P, 1], F32, name="warm")
         nc.scalar.activation(warm[:], ident32[:, 0:1], ACT.Sigmoid)
 
+        nc.sync.dma_start(idx_list[:], offs)
         nc.sync.dma_start(ctx_list[:], coffs)
         nc.sync.dma_start(e_lane[0][:], e_rows[:, 0, :])
         nc.sync.dma_start(slot_list[:], slotoffs)
-        nc.sync.dma_start(idx_list[:], offs)
+        nc.sync.dma_start(ts_table[0:1, :], ts[0:1, :])
+        nc.sync.dma_start(ux_rows[0:LANES, :], ux.rearrange("(q p) o -> q (p o)", p=P))
         y_rows = y.rearrange("(q p) i -> p q i", p=P)
         for t in range(LANES):
             if t > 0:
                 nc.sync.dma_start(e_lane[t][:], e_rows[:, t, :])
             if t == 1:
-                nc.sync.dma_start(ux_rows[0:LANES, :], ux.rearrange("(q p) o -> q (p o)", p=P))
-                nc.sync.dma_start(ts_table[0:1, :], ts[0:1, :])
-            if t in (1, 2):
-                nc.sync.dma_start(y_half[t - 1][:], y_rows[:, 2 * (t - 1) : 2 * t, :])
-            for u in range(2):
-                nc.sync.dma_start(w_half[t][u][:], w_rows[:, t, 1024 * u : 1024 * (u + 1)])
+                nc.sync.dma_start(y_half[0][:], y_rows[:, 0:2, :])
+            for part, cols in zip(w_part[t], w_cols[t]):
+                nc.sync.dma_start(part[:], w_rows[:, t, cols])
+        nc.sync.dma_start(y_half[1][:], y_rows[:, 2:4, :])
         nc.sync.dma_start(posn_list[:], posnoffs)
 
         ux_ps = turn_ps.tile([P, P], F32, name="ux_ps", tag="turn")
         nc.tensor.transpose(ux_ps[:], ux_rows[:], ident32[:])
-        ux_col = keep.tile([P, LANES], F32, name="ux_col", tag="column")
+        ux_col = keep.tile([P, LANES], F32, name="ux_col")
         m2ux = keep.tile([P, LANES], F32, name="m2ux")
         nc.scalar.copy(ux_col[:], ux_ps[:, 0:LANES])
         nc.scalar.activation(m2ux[:], ux_ps[:, 0:LANES], ACT.Copy, scale=-2.0)
         pairs = keep.tile([P, LANES, SLOTS], F32, name="pairs", tag="pairs_out", align_bytes=64)
-        w_by_d = keep.tile([P, OUTW, LANES], BF16, name="w_by_d", align_bytes=64)
-        w_by_i = keep.tile([P, OUTW, LANES], BF16, name="w_by_i", align_bytes=64)
-        w_i = keep.tile([P, LANES, OUTW], BF16, name="w_i")
+        w_by_d = keep.tile([P, OUTW, LANES], BF16, name="w_by_d", tag="w_by_d", align_bytes=64)
+        w_i = keep.tile([P, LANES - 1, OUTW], BF16, name="w_i")
         ts_i = keep.tile([P, OUTW], F32, name="ts_i")
-        signed_ux = keep.tile([P, LANES, LANES, P], F32, name="signed_ux")
-        factor = keep.tile([P, LANES, POS], F32, name="factor", tag="factor_window", align_bytes=64)
+        signed_ux = [keep.tile([P, OUTW], F32, name="signed_ux%d" % q) for q in range(POS // P)]
+        factor = [keep.tile([P, LANES, POS // 2], F32, name="factor%d" % u) for u in range(2)]
+        w_ps = {}
+        column = {}
 
         def sign_labels(q):
-            nc.scalar.activation(
-                signed_ux[:, q, :, :].rearrange("p r s -> p s r"),
-                y_half[q // 2][:, q % 2, :].rearrange("p (s r) -> p s r", r=LANES),
-                ACT.Identity, bias=ux_col[:, q : q + 1], scale=m2ux[:, q : q + 1])
+            labels = y_half[q // 2][:, q % 2, :]
+            if q < 2:
+                nc.scalar.activation(
+                    signed_ux[q][:], labels, ACT.Identity, bias=ux_col[:, q : q + 1], scale=m2ux[:, q : q + 1])
+            else:
+                nc.vector.tensor_scalar(
+                    signed_ux[q][:], labels, m2ux[:, q : q + 1], ux_col[:, q : q + 1], ALU.mult, ALU.add)
 
-        def turn_factors():
+        def turn_scales():
             ts_ps = turn_ps.tile([P, LANES, P], F32, name="ts_ps", tag="turn")
             for r in range(LANES):
                 nc.tensor.transpose(ts_ps[:, r, :], ts_i[:, r:OUTW:LANES], ident32[:])
-            ts_col = keep.tile([P, LANES], F32, name="ts_col", tag="column")
-            nc.scalar.copy(ts_col[:], ts_ps[:, :, 0])
-            for r in range(LANES):
-                f_ps = turn_ps.tile([P, LANES, P], F32, name="f_ps", tag="turn")
-                for q in range(LANES):
-                    nc.tensor.transpose(f_ps[:, q, :], signed_ux[:, q, r, :], ident32[:])
-                nc.scalar.activation(
-                    factor[:, r, :], f_ps[:].rearrange("s q p -> s (q p)"), ACT.Copy, scale=ts_col[:, r : r + 1])
+            column["ts"] = keep.tile([P, LANES], F32, name="ts_col", tag="y_half0", align_bytes=64)
+            nc.scalar.copy(column["ts"][:], ts_ps[:, :, 0])
 
+        def turn_factors(u):
+            for r0 in range(0, LANES, 2):
+                f_ps = turn_ps.tile([P, 2, 2, P], F32, name="f_ps", tag="turn")
+                for r in range(2):
+                    for q in range(2):
+                        nc.tensor.transpose(f_ps[:, r, q, :], signed_ux[2 * u + q][:, r0 + r : OUTW : LANES], ident32[:])
+                for r in range(2):
+                    nc.scalar.activation(
+                        factor[u][:, r0 + r, :], f_ps[:, r, :, :].rearrange("s q p -> s (q p)"), ACT.Copy,
+                        scale=column["ts"][:, r0 + r : r0 + r + 1])
+
+        nc.vector.tensor_copy(ts_i[:], ts_table[:].indirect(idx_list[:]))
         for t in range(LANES):
             half_ec = ring.tile([P, SLOTS], F32, name="half_ec", tag="slots")
             for u in range(2):
                 nc.vector.tensor_scalar(
                     half_ec[:, 512 * u : 512 * (u + 1)], e_lane[t][:].indirect(ctx_list[:, 32 * u : 32 * (u + 1)]),
                     0.5, 0.0, ALU.mult, ALU.add)
-            if t == 1:
-                nc.vector.tensor_copy(ts_i[:], ts_table[:].indirect(idx_list[:]))
             for u in range(2):
                 nc.vector.tensor_copy(
                     pairs[:, t, 512 * u : 512 * (u + 1)], half_ec[:].indirect(slot_list[:, 32 * u : 32 * (u + 1)]))
 
             w_bf = ring.tile([P, WORDS], BF16, name="w_bf")
-            for u in range(2):
-                nc.scalar.copy(w_bf[:, 1024 * u : 1024 * (u + 1)], w_half[t][u][:])
-            nc.scalar.activation(
-                w_i[:, t, :].rearrange("p (r s) -> p s r", r=LANES), w_bf[:].indirect(idx_list[:]), ACT.Copy)
-            if t < 2:
-                sign_labels(2 * t)
-                sign_labels(2 * t + 1)
-            if t == 1:
-                turn_factors()
-        nc.scalar.copy(
-            w_by_d[:].rearrange("p (k i) t -> p k t i", i=RUN), w_i[:].rearrange("p t (k i) -> p k t i", i=RUN))
+            for part, cols in zip(w_part[t], w_cols[t]):
+                nc.scalar.copy(w_bf[:, cols], part[:])
+            if t < LANES - 1:
+                nc.scalar.activation(w_i[:, t, :], w_bf[:].indirect(idx_list[:]), ACT.Copy)
+                w_ps[t] = dh_pool.tile([P, 2, P], F32, name="w_ps%d" % t, tag="bank%d" % t)
+                for u in range(2):
+                    nc.tensor.transpose(w_ps[t][:, u, :], w_i[:, t, :].bitcast(F32)[:, u : OUTW // 2 : 2], ident32[:])
+            else:
+                nc.scalar.activation(
+                    w_by_d[:, :, t].rearrange("p (r s) -> p s r", r=LANES), w_bf[:].indirect(idx_list[:]), ACT.Copy)
+                w_ps[t] = dh_pool.tile([P, LANES, P], BF16, name="w_ps%d" % t, tag="bank%d" % t)
+                for r in range(LANES):
+                    nc.tensor.transpose(w_ps[t][:, r, :], w_by_d[:, P * r : P * (r + 1), t], ident16[:])
+            if t == LANES - 2:
+                nc.scalar.copy(
+                    w_by_d[:, :, : LANES - 1].rearrange("p (r k i) t -> p k t i r", r=LANES, i=2),
+                    w_i[:].rearrange("p t (k i r) -> p k t i r", i=2, r=LANES))
+            if t in (0, LANES - 1):
+                u = t // (LANES - 1)
+                sign_labels(2 * u)
+                sign_labels(2 * u + 1)
+                if u == 0:
+                    turn_scales()
+                turn_factors(u)
 
+        w_by_i = keep.tile([P, OUTW, LANES], BF16, name="w_by_i", tag="y_half1", align_bytes=64)
         for t in order:
-            w_ps = turn_ps.tile([P, LANES, P], BF16, name="w_ps", tag="turn")
-            for r in range(LANES):
-                nc.tensor.transpose(w_ps[:, r, :], w_by_d[:, P * r : P * (r + 1), t], ident16[:])
-            nc.scalar.copy(w_by_i[:, P * t : P * (t + 1), :], w_ps[:].rearrange("s r c -> s c r"))
+            target = w_by_i[:, P * t : P * (t + 1), :]
+            if t < LANES - 1:
+                target = target.rearrange("s c r -> s (c r)").bitcast(F32).rearrange("s (c u) -> s c u", u=2)
+            nc.scalar.copy(target, w_ps[t][:].rearrange("s r c -> s c r"))
 
         def mx_tiles(name, width):
             codes = keep.tile([P, width], U32, name=name + "_codes", align_bytes=64)
             scales = keep.tile([P, width], U8, name=name + "_scales", align_bytes=64)
             return codes, scales
 
-        def quantize(operand, grouped, cols, fmt):
+        def quantize(operand, cols, grouped, fmt):
             nc.vector.quantize_mx(
-                out=operand[0][:, cols].bitcast(fmt), scales=operand[1][:, cols],
-                in_=grouped[:, cols, :].rearrange("p c l -> p (c l)"))
+                out=operand[0][:, cols].bitcast(fmt), scales=operand[1][:, cols], in_=grouped.rearrange("p c l -> p (c l)"))
 
         h_mx = mx_tiles("h", POS)
         g_mx = mx_tiles("g", POS)
         wd_mx = mx_tiles("wd", OUTW)
         wi_mx = mx_tiles("wi", OUTW)
-        h_bf = keep.tile([P, POS, LANES], BF16, name="h_bf", align_bytes=64)
+        h_bf = {}
         g_bf = keep.tile([P, POS, LANES], BF16, name="g_bf", tag="g_window", align_bytes=64)
         chunks = [slice(P * c, P * (c + 1)) for c in range(POS // P)]
         pair_view = pairs[:].rearrange("p t (k i j) -> p k t i j", i=2, j=2)
 
         def pair_sum(c):
             ks = slice(64 * c, 64 * (c + 1))
+            h_bf[c] = keep.tile([P, P, LANES], BF16, name="h_bf%d" % c, tag="w_by_d" if c == 3 else "h_bf%d" % c, align_bytes=64)
             nc.vector.tensor_tensor(
-                h_bf[:, chunks[c], :].rearrange("p (k i) t -> p k t i", i=2),
+                h_bf[c][:].rearrange("p (k i) t -> p k t i", i=2),
                 pair_view[:, ks, :, :, 0], pair_view[:, ks, :, :, 1], ALU.add)
 
         sig = {}
@@ -185,7 +214,7 @@ def tile_attend_gcbow_ns_pl_kernel(tc, eT, wT, ts, ux, y, coffs, posnoffs, sloto
                     out=a_ps[:, r, :], lhsT=wd_mx[0][:, cols].bitcast(E4M3), lhsT_scale=wd_mx[1][:, cols],
                     rhs=h_mx[0][:, chunks[c]].bitcast(E4M3), rhs_scale=h_mx[1][:, chunks[c]], start=True, stop=True)
             z = ring.tile([P, LANES, P], F32, name="z")
-            nc.vector.tensor_tensor(z[:], a_ps[:], factor[:, :, chunks[c]], ALU.mult)
+            nc.vector.tensor_tensor(z[:], a_ps[:], factor[c // 2][:, :, chunks[c % 2]], ALU.mult)
             sig[c] = ring.tile([P, LANES, P], F32, name="sig")
             nc.scalar.activation(sig[c][:], z[:], ACT.Sigmoid)
 
@@ -193,32 +222,32 @@ def tile_attend_gcbow_ns_pl_kernel(tc, eT, wT, ts, ux, y, coffs, posnoffs, sloto
             nc.vector.tensor_tensor(
                 g_bf[:, chunks[c], :].rearrange("s (k i) r -> s k r i", i=RUN),
                 sig[c][:].rearrange("s r (k i) -> s k r i", i=RUN),
-                factor[:, :, chunks[c]].rearrange("s r (k i) -> s k r i", i=RUN), ALU.mult)
+                factor[c // 2][:, :, chunks[c % 2]].rearrange("s r (k i) -> s k r i", i=RUN), ALU.mult)
 
-        pair_sum(0)
-        for c in range(4):
-            if c < 3:
-                pair_sum(c + 1)
-            else:
-                quantize(wd_mx, w_by_d, slice(0, OUTW), E4M3)
-            quantize(h_mx, h_bf, chunks[c], E4M3)
+        for c in range(3):
+            pair_sum(c)
+            if c > 0:
+                quantize(h_mx, chunks[c - 1], h_bf[c - 1][:], E4M3)
+        quantize(wd_mx, slice(0, OUTW), w_by_d[:], E4M3)
+        quantize(h_mx, chunks[2], h_bf[2][:], E4M3)
+        pair_sum(3)
         score(0)
+        quantize(h_mx, chunks[3], h_bf[3][:], E4M3)
         score(1)
-        quantize(wi_mx, w_by_i, slice(0, OUTW), E4M3)
+        quantize(wi_mx, slice(0, OUTW), w_by_i[:], E4M3)
         for c in range(4):
             loss_gradient(c)
             if c < 2:
                 score(c + 2)
             if c > 0:
-                quantize(g_mx, g_bf, chunks[c - 1], E5M2)
-        quantize(g_mx, g_bf, chunks[3], E5M2)
+                quantize(g_mx, chunks[c - 1], g_bf[:, chunks[c - 1], :], E5M2)
+        quantize(g_mx, chunks[3], g_bf[:, chunks[3], :], E5M2)
 
-        clear(order[2], "g_window")
-        clear(order[3], "factor_window")
+        clear(nc.gpsimd, order[3], "g_window")
         dh_ps = {}
         for j in order:
             cols = slice(P * j, P * (j + 1))
-            dh_ps[j] = dh_pool.tile([P, POS], F32, name="dh_ps%d" % j)
+            dh_ps[j] = dh_pool.tile([P, POS], F32, name="dh_ps%d" % j, tag="bank%d" % j)
             nc.tensor.matmul_mx(
                 out=dh_ps[j][:], lhsT=wi_mx[0][:, cols].bitcast(E4M3), lhsT_scale=wi_mx[1][:, cols],
                 rhs=g_mx[0][:].bitcast(E5M2), rhs_scale=g_mx[1][:], start=True, stop=True)
@@ -266,7 +295,7 @@ def tile_attend_gcbow_ns_pl_kernel(tc, eT, wT, ts, ux, y, coffs, posnoffs, sloto
         for n in range(len(pieces)):
             if n + 1 < half:
                 nc.vector.tensor_copy(out_bf[:, pieces[n + 1], last], grad[last][:, pieces[n + 1]])
-            quantize((out_codes, out_scales), out_bf, pieces[n], E4M3)
+            quantize((out_codes, out_scales), pieces[n], out_bf[:, pieces[n], :], E4M3)
             if n % 2 == 1:
                 cols = slice(pieces[n - 1].start, pieces[n].stop)
                 nc.sync.dma_start(words_hbm[:, cols], out_codes[:, cols].bitcast(I32))

@@ -22,9 +22,10 @@ WORDS = 2048
 SLOTS = 1024
 POS = 512
 OUTW = 512
-DH_WINDOW = 1376
+WINDOW = 1376
 TAIL_CHUNK = 256
 RUN = 4
+ROW = 8
 TS_SPLIT = 704
 
 
@@ -45,83 +46,81 @@ def tile_attend_gcbow_ns_pl_kernel(tc, eT, wT, ts, ux, y, coffs, posnoffs, sloto
         w_rows = wT.rearrange("(p t) c -> p t c", t=LANES)
         out_rows = out_0.rearrange("(p t) c -> p t c", t=LANES)
         e_lane = [keep.tile([P, WORDS], F32, name="e_lane%d" % t) for t in range(LANES)]
-        in_halves = [slice(0, WORDS // 2), slice(WORDS // 2, WORDS)]
-        w_cols = [in_halves, [slice(0, WORDS)], [slice(0, WORDS)], in_halves]
+        halves = [slice(0, WORDS // 2), slice(WORDS // 2, WORDS)]
         w_part = [
-            [keep.tile([P, cols.stop - cols.start], F32, name="w%d_%d" % (t, cols.start)) for cols in w_cols[t]]
+            [keep.tile([P, WORDS // 2], F32, name="w%d_%d" % (t, u), tag="w%d_%d" % (t, u), align_bytes=64) for u in range(2)]
             for t in range(LANES)]
         ts_table = keep.tile([P, WORDS], F32, name="ts_table")
         y_half = [keep.tile([P, 2, OUTW], F32, name="y_half%d" % u, tag="y_half%d" % u, align_bytes=64) for u in range(2)]
-        ux_rows = keep.tile([P, P], F32, name="ux_rows")
+        ux_col = keep.tile([P, LANES], F32, name="ux_col")
+        m2ux = keep.tile([P, LANES], F32, name="m2ux")
         ident32 = keep.tile([P, P], F32, name="ident32")
-        ident16 = keep.tile([P, P], BF16, name="ident16")
-        dh = keep.tile([P, LANES * POS], F32, name="dh")
+        half_ec = keep.tile([P, (LANES - 1) * SLOTS + WINDOW], F32, name="half_ec")
+        dh = keep.tile([P, (LANES - 1) * POS + WINDOW], F32, name="dh")
 
         order = [1, 3, 2, 0]
 
         nc.gpsimd.memset(ts_table[:, TS_SPLIT:], 0.0)
         nc.vector.memset(ts_table[:, :TS_SPLIT], 0.0)
-        nc.vector.memset(ux_rows[:], 0.0)
         make_identity(nc, ident32[:])
-        make_identity(nc, ident16[:])
+        nc.gpsimd.memset(half_ec[:, LANES * SLOTS :], 0.0)
         grad = {}
 
-        def clear(engine, j, tag):
+        def clear(j, tag):
             grad[j] = keep.tile([P, WORDS], F32, name="grad%d" % j, tag=tag, align_bytes=64)
-            engine.memset(grad[j][:], 0.0)
+            nc.gpsimd.memset(grad[j][:], 0.0)
 
-        clear(nc.vector, order[0], "first_window")
-        clear(nc.gpsimd, order[1], "second_window")
-        clear(nc.gpsimd, order[2], "third_window")
+        clear(order[0], "first_window")
+        clear(order[1], "second_window")
+
         warm = keep.tile([P, 1], F32, name="warm")
         nc.scalar.activation(warm[:], ident32[:, 0:1], ACT.Sigmoid)
 
         nc.sync.dma_start(idx_list[:], offs)
         nc.sync.dma_start(ctx_list[:], coffs)
-        nc.sync.dma_start(e_lane[0][:], e_rows[:, 0, :])
+        for a in range(0, WORDS, WORDS // 4):
+            nc.sync.dma_start(e_lane[0][:, a : a + WORDS // 4], e_rows[:, 0, a : a + WORDS // 4])
         nc.sync.dma_start(slot_list[:], slotoffs)
+        nc.sync.dma_start(
+            ux_col[:].rearrange("p (u q) -> p u q", q=2), ux.rearrange("(u p q) o -> p u (q o)", p=P, q=2))
         nc.sync.dma_start(ts_table[0:1, :], ts[0:1, :])
-        nc.sync.dma_start(ux_rows[0:LANES, :], ux.rearrange("(q p) o -> q (p o)", p=P))
-        y_rows = y.rearrange("(q p) i -> p q i", p=P)
+        y_rows = y.rearrange("(u p q) i -> p u q i", p=P, q=2)
         for t in range(LANES):
             if t > 0:
                 nc.sync.dma_start(e_lane[t][:], e_rows[:, t, :])
-            if t == 1:
-                nc.sync.dma_start(y_half[0][:], y_rows[:, 0:2, :])
-            for part, cols in zip(w_part[t], w_cols[t]):
+            for part, cols in zip(w_part[t], halves):
                 nc.sync.dma_start(part[:], w_rows[:, t, cols])
-        nc.sync.dma_start(y_half[1][:], y_rows[:, 2:4, :])
+            if t in (1, 2):
+                nc.sync.dma_start(y_half[t - 1][:], y_rows[:, t - 1, :, :])
         nc.sync.dma_start(posn_list[:], posnoffs)
 
-        ux_ps = turn_ps.tile([P, P], F32, name="ux_ps", tag="turn")
-        nc.tensor.transpose(ux_ps[:], ux_rows[:], ident32[:])
-        ux_col = keep.tile([P, LANES], F32, name="ux_col")
-        m2ux = keep.tile([P, LANES], F32, name="m2ux")
-        nc.scalar.copy(ux_col[:], ux_ps[:, 0:LANES])
-        nc.scalar.activation(m2ux[:], ux_ps[:, 0:LANES], ACT.Copy, scale=-2.0)
+        nc.gpsimd.tensor_scalar(m2ux[:], ux_col[:], -2.0, 0.0, ALU.mult, ALU.add)
+
         pairs = keep.tile([P, LANES, SLOTS], F32, name="pairs", tag="pairs_out", align_bytes=64)
         w_by_d = keep.tile([P, OUTW, LANES], BF16, name="w_by_d", tag="w_by_d", align_bytes=64)
-        w_i = keep.tile([P, LANES - 1, OUTW], BF16, name="w_i")
         ts_i = keep.tile([P, OUTW], F32, name="ts_i")
+        ts_dealt = keep.tile([P, OUTW], F32, name="ts_dealt")
         signed_ux = [keep.tile([P, OUTW], F32, name="signed_ux%d" % q) for q in range(POS // P)]
         factor = [keep.tile([P, LANES, POS // 2], F32, name="factor%d" % u) for u in range(2)]
-        w_ps = {}
         column = {}
 
+        def listed(row):
+            return row.rearrange("p (b r a) -> p b r a", r=LANES, a=ROW)
+
+        def dealt(row):
+            return row.rearrange("p (r b a) -> p b r a", r=LANES, a=ROW)
+
         def sign_labels(q):
-            labels = y_half[q // 2][:, q % 2, :]
-            if q < 2:
-                nc.scalar.activation(
-                    signed_ux[q][:], labels, ACT.Identity, bias=ux_col[:, q : q + 1], scale=m2ux[:, q : q + 1])
-            else:
-                nc.vector.tensor_scalar(
-                    signed_ux[q][:], labels, m2ux[:, q : q + 1], ux_col[:, q : q + 1], ALU.mult, ALU.add)
+            nc.gpsimd.tensor_scalar(
+                dealt(signed_ux[q][:]), listed(y_half[q // 2][:, q % 2, :]), m2ux[:, q : q + 1], ux_col[:, q : q + 1],
+                ALU.mult, ALU.add)
 
         def turn_scales():
+            nc.gpsimd.tensor_scalar(dealt(ts_dealt[:]), listed(ts_i[:]), 1.0, 0.0, ALU.mult, ALU.add)
             ts_ps = turn_ps.tile([P, LANES, P], F32, name="ts_ps", tag="turn")
             for r in range(LANES):
-                nc.tensor.transpose(ts_ps[:, r, :], ts_i[:, r:OUTW:LANES], ident32[:])
-            column["ts"] = keep.tile([P, LANES], F32, name="ts_col", tag="y_half0", align_bytes=64)
+                nc.tensor.transpose(ts_ps[:, r, :], ts_dealt[:, P * r : P * (r + 1)], ident32[:])
+            column["ts"] = keep.tile([P, LANES], F32, name="ts_col", tag="w1_1", align_bytes=64)
             nc.scalar.copy(column["ts"][:], ts_ps[:, :, 0])
 
         def turn_factors(u):
@@ -129,55 +128,48 @@ def tile_attend_gcbow_ns_pl_kernel(tc, eT, wT, ts, ux, y, coffs, posnoffs, sloto
                 f_ps = turn_ps.tile([P, 2, 2, P], F32, name="f_ps", tag="turn")
                 for r in range(2):
                     for q in range(2):
-                        nc.tensor.transpose(f_ps[:, r, q, :], signed_ux[2 * u + q][:, r0 + r : OUTW : LANES], ident32[:])
+                        nc.tensor.transpose(
+                            f_ps[:, r, q, :], signed_ux[2 * u + q][:, P * (r0 + r) : P * (r0 + r + 1)], ident32[:])
                 for r in range(2):
                     nc.scalar.activation(
-                        factor[u][:, r0 + r, :], f_ps[:, r, :, :].rearrange("s q p -> s (q p)"), ACT.Copy,
+                        factor[u][:, r0 + r, :].rearrange("s (p q) -> s p q", q=2), f_ps[:, r, :, :].rearrange("s q p -> s p q"), ACT.Copy,
                         scale=column["ts"][:, r0 + r : r0 + r + 1])
 
         nc.vector.tensor_copy(ts_i[:], ts_table[:].indirect(idx_list[:]))
         for t in range(LANES):
-            half_ec = ring.tile([P, SLOTS], F32, name="half_ec", tag="slots")
+            first = SLOTS * (LANES - 1 - t)
             for u in range(2):
                 nc.vector.tensor_scalar(
-                    half_ec[:, 512 * u : 512 * (u + 1)], e_lane[t][:].indirect(ctx_list[:, 32 * u : 32 * (u + 1)]),
-                    0.5, 0.0, ALU.mult, ALU.add)
-            for u in range(2):
-                nc.vector.tensor_copy(
-                    pairs[:, t, 512 * u : 512 * (u + 1)], half_ec[:].indirect(slot_list[:, 32 * u : 32 * (u + 1)]))
+                    half_ec[:, first + 512 * u : first + 512 * (u + 1)],
+                    e_lane[t][:].indirect(ctx_list[:, 32 * u : 32 * (u + 1)]), 0.5, 0.0, ALU.mult, ALU.add)
+            nc.vector.tensor_copy(pairs[:, t, :], half_ec[:, first : first + WINDOW].indirect(slot_list[:]))
 
             w_bf = ring.tile([P, WORDS], BF16, name="w_bf")
-            for part, cols in zip(w_part[t], w_cols[t]):
+            for part, cols in zip(w_part[t], halves):
                 nc.scalar.copy(w_bf[:, cols], part[:])
-            if t < LANES - 1:
-                nc.scalar.activation(w_i[:, t, :], w_bf[:].indirect(idx_list[:]), ACT.Copy)
-                w_ps[t] = dh_pool.tile([P, 2, P], F32, name="w_ps%d" % t, tag="bank%d" % t)
-                for u in range(2):
-                    nc.tensor.transpose(w_ps[t][:, u, :], w_i[:, t, :].bitcast(F32)[:, u : OUTW // 2 : 2], ident32[:])
-            else:
-                nc.scalar.activation(
-                    w_by_d[:, :, t].rearrange("p (r s) -> p s r", r=LANES), w_bf[:].indirect(idx_list[:]), ACT.Copy)
-                w_ps[t] = dh_pool.tile([P, LANES, P], BF16, name="w_ps%d" % t, tag="bank%d" % t)
-                for r in range(LANES):
-                    nc.tensor.transpose(w_ps[t][:, r, :], w_by_d[:, P * r : P * (r + 1), t], ident16[:])
-            if t == LANES - 2:
-                nc.scalar.copy(
-                    w_by_d[:, :, : LANES - 1].rearrange("p (r k i) t -> p k t i r", r=LANES, i=2),
-                    w_i[:].rearrange("p t (k i r) -> p k t i r", i=2, r=LANES))
-            if t in (0, LANES - 1):
-                u = t // (LANES - 1)
+            nc.scalar.activation(dealt(w_by_d[:, :, t]), w_bf[:].indirect(idx_list[:]), ACT.Copy)
+            if t in (1, 2):
+                u = t - 1
                 sign_labels(2 * u)
                 sign_labels(2 * u + 1)
                 if u == 0:
                     turn_scales()
                 turn_factors(u)
+                clear(order[2 + u], "y_half%d" % u)
 
-        w_by_i = keep.tile([P, OUTW, LANES], BF16, name="w_by_i", tag="y_half1", align_bytes=64)
-        for t in order:
-            target = w_by_i[:, P * t : P * (t + 1), :]
-            if t < LANES - 1:
-                target = target.rearrange("s c r -> s (c r)").bitcast(F32).rearrange("s (c u) -> s c u", u=2)
-            nc.scalar.copy(target, w_ps[t][:].rearrange("s r c -> s c r"))
+        nc.gpsimd.memset(dh[:, LANES * POS :], 0.0)
+
+        w_words = w_by_d[:].rearrange("p c t -> p (c t)").bitcast(F32)
+        w_by_i = keep.tile([P, OUTW, LANES], BF16, name="w_by_i", tag="w3_1", align_bytes=64)
+        w_ps = {}
+        for u in range(2):
+            w_ps[u] = dh_pool.tile([P, LANES, P], F32, name="w_ps%d" % u, tag="bank%d" % order[2 + u])
+            for r in range(LANES):
+                nc.tensor.transpose(w_ps[u][:, r, :], w_words[:, 2 * P * r + u : 2 * P * (r + 1) : 2], ident32[:])
+
+        def lay_w(t):
+            codes = w_ps[t // 2][:].rearrange("s r p -> s (r p)").bitcast(BF16).rearrange("s (r p e) -> s p r e", r=LANES, e=2)
+            nc.scalar.copy(w_by_i[:, P * t : P * (t + 1), :], codes[:, :, :, t % 2])
 
         def mx_tiles(name, width):
             codes = keep.tile([P, width], U32, name=name + "_codes", align_bytes=64)
@@ -193,7 +185,7 @@ def tile_attend_gcbow_ns_pl_kernel(tc, eT, wT, ts, ux, y, coffs, posnoffs, sloto
         wd_mx = mx_tiles("wd", OUTW)
         wi_mx = mx_tiles("wi", OUTW)
         h_bf = {}
-        g_bf = keep.tile([P, POS, LANES], BF16, name="g_bf", tag="g_window", align_bytes=64)
+        g_bf = keep.tile([P, POS, LANES], BF16, name="g_bf", align_bytes=64)
         chunks = [slice(P * c, P * (c + 1)) for c in range(POS // P)]
         pair_view = pairs[:].rearrange("p t (k i j) -> p k t i j", i=2, j=2)
 
@@ -224,26 +216,30 @@ def tile_attend_gcbow_ns_pl_kernel(tc, eT, wT, ts, ux, y, coffs, posnoffs, sloto
                 sig[c][:].rearrange("s r (k i) -> s k r i", i=RUN),
                 factor[c // 2][:, :, chunks[c % 2]].rearrange("s r (k i) -> s k r i", i=RUN), ALU.mult)
 
-        for c in range(3):
-            pair_sum(c)
-            if c > 0:
-                quantize(h_mx, chunks[c - 1], h_bf[c - 1][:], E4M3)
+        pair_sum(0)
+        pair_sum(1)
+        quantize(h_mx, chunks[0], h_bf[0][:], E4M3)
+        pair_sum(2)
+        quantize(h_mx, chunks[1], h_bf[1][:], E4M3)
         quantize(wd_mx, slice(0, OUTW), w_by_d[:], E4M3)
         quantize(h_mx, chunks[2], h_bf[2][:], E4M3)
         pair_sum(3)
         score(0)
         quantize(h_mx, chunks[3], h_bf[3][:], E4M3)
         score(1)
+        loss_gradient(0)
+        score(2)
+        loss_gradient(1)
+        score(3)
+        for t in order:
+            lay_w(t)
+        loss_gradient(2)
+        loss_gradient(3)
+        quantize(g_mx, slice(0, 2 * P), g_bf[:, 0 : 2 * P, :], E5M2)
         quantize(wi_mx, slice(0, OUTW), w_by_i[:], E4M3)
-        for c in range(4):
-            loss_gradient(c)
-            if c < 2:
-                score(c + 2)
-            if c > 0:
-                quantize(g_mx, chunks[c - 1], g_bf[:, chunks[c - 1], :], E5M2)
+        quantize(g_mx, chunks[2], g_bf[:, chunks[2], :], E5M2)
         quantize(g_mx, chunks[3], g_bf[:, chunks[3], :], E5M2)
 
-        clear(nc.gpsimd, order[3], "g_window")
         dh_ps = {}
         for j in order:
             cols = slice(P * j, P * (j + 1))
@@ -259,16 +255,9 @@ def tile_attend_gcbow_ns_pl_kernel(tc, eT, wT, ts, ux, y, coffs, posnoffs, sloto
         by_slot = {}
 
         def look_up(j):
-            if j == order[-1]:
-                by_slot[j] = keep.tile([P, SLOTS], F32, name="dc_last", tag="first_window", align_bytes=64)
-            else:
-                by_slot[j] = ring.tile([P, SLOTS], F32, name="dc", tag="slots")
-            width = min(LANES * POS - start[j], 3 * POS)
-            piece = SLOTS if width > SLOTS else width // 2
-            for a in range(0, SLOTS, piece):
-                nc.vector.tensor_copy(
-                    by_slot[j][:, a : a + piece],
-                    dh[:, start[j] : start[j] + width].indirect(posn_list[:, a // 16 : (a + piece) // 16]))
+            tag = "first_window" if j == order[-1] else "w%d_0" % j
+            by_slot[j] = keep.tile([P, SLOTS], F32, name="dc%d" % j, tag=tag, align_bytes=64)
+            nc.vector.tensor_copy(by_slot[j][:], dh[:, start[j] : start[j] + WINDOW].indirect(posn_list[:]))
 
         def place(j):
             nc.vector.tensor_copy(grad[j][:].indirect(ctx_list[:]), by_slot[j][:])

@@ -34,8 +34,7 @@ def tile_attend_gcbow_ns_pl_kernel(tc, eT, wT, ts, ux, y, coffs, posnoffs, sloto
     with ExitStack() as ctx:
         keep = ctx.enter_context(tc.tile_pool(name="keep", bufs=1))
         ring = ctx.enter_context(tc.tile_pool(name="ring", bufs=2))
-        turn_ps = ctx.enter_context(tc.psum_pool(name="turn", bufs=2))
-        mm_ps = ctx.enter_context(tc.psum_pool(name="mm", bufs=2))
+        turn_ps = ctx.enter_context(tc.psum_pool(name="turn", bufs=4))
         dh_pool = ctx.enter_context(tc.psum_pool(name="dh", bufs=1))
 
         ctx_list = keep.tile([P, SLOTS // 16], U16, name="ctx_list")
@@ -45,7 +44,9 @@ def tile_attend_gcbow_ns_pl_kernel(tc, eT, wT, ts, ux, y, coffs, posnoffs, sloto
         e_rows = eT.rearrange("(p t) c -> p t c", t=LANES)
         w_rows = wT.rearrange("(p t) c -> p t c", t=LANES)
         out_rows = out_0.rearrange("(p t) c -> p t c", t=LANES)
-        e_lane = [keep.tile([P, WORDS], F32, name="e_lane%d" % t) for t in range(LANES)]
+        e_first = [keep.tile([P, WORDS], F32, name="e_lane%d" % t) for t in range(2)]
+        e_last = keep.tile([P, 2 * WORDS], F32, name="e_last")
+        e_lane = [e_first[0][:], e_first[1][:], e_last[:, :WORDS], e_last[:, WORDS:]]
         halves = [slice(0, WORDS // 2), slice(WORDS // 2, WORDS)]
         w_part = [
             [keep.tile([P, WORDS // 2], F32, name="w%d_%d" % (t, u), tag="w%d_%d" % (t, u), align_bytes=64) for u in range(2)]
@@ -55,7 +56,7 @@ def tile_attend_gcbow_ns_pl_kernel(tc, eT, wT, ts, ux, y, coffs, posnoffs, sloto
         ux_col = keep.tile([P, LANES], F32, name="ux_col")
         m2ux = keep.tile([P, LANES], F32, name="m2ux")
         ident32 = keep.tile([P, P], F32, name="ident32")
-        half_ec = keep.tile([P, (LANES - 1) * SLOTS + WINDOW], F32, name="half_ec")
+        e_c = keep.tile([P, (LANES - 1) * SLOTS + WINDOW], F32, name="e_c")
         dh = keep.tile([P, (LANES - 1) * POS + WINDOW], F32, name="dh")
 
         order = [1, 3, 2, 0]
@@ -63,35 +64,44 @@ def tile_attend_gcbow_ns_pl_kernel(tc, eT, wT, ts, ux, y, coffs, posnoffs, sloto
         nc.gpsimd.memset(ts_table[:, TS_SPLIT:], 0.0)
         nc.vector.memset(ts_table[:, :TS_SPLIT], 0.0)
         make_identity(nc, ident32[:])
-        nc.gpsimd.memset(half_ec[:, LANES * SLOTS :], 0.0)
+        nc.gpsimd.memset(e_c[:, LANES * SLOTS :], 0.0)
         grad = {}
 
         def clear(j, tag):
             grad[j] = keep.tile([P, WORDS], F32, name="grad%d" % j, tag=tag, align_bytes=64)
             nc.gpsimd.memset(grad[j][:], 0.0)
 
-        clear(order[0], "first_window")
-        clear(order[1], "second_window")
+        for j in order:
+            clear(j, "window%d" % j)
+        nc.gpsimd.memset(dh[:, LANES * POS :], 0.0)
 
         warm = keep.tile([P, 1], F32, name="warm")
         nc.scalar.activation(warm[:], ident32[:, 0:1], ACT.Sigmoid)
 
-        nc.sync.dma_start(idx_list[:], offs)
         nc.sync.dma_start(ctx_list[:], coffs)
-        for a in range(0, WORDS, WORDS // 4):
-            nc.sync.dma_start(e_lane[0][:, a : a + WORDS // 4], e_rows[:, 0, a : a + WORDS // 4])
+        nc.sync.dma_start(e_lane[0], e_rows[:, 0, :])
+        y_rows = y.rearrange("(u p q) i -> p u q i", p=P, q=2)
+
+        def load_w(t, u):
+            nc.sync.dma_start(w_part[t][u][:], w_rows[:, t, halves[u]])
+
+        nc.sync.dma_start(e_lane[1], e_rows[:, 1, :])
         nc.sync.dma_start(slot_list[:], slotoffs)
+        nc.sync.dma_start(idx_list[:], offs)
+        nc.sync.dma_start(ts_table[0:1, :], ts[0:1, :])
+        load_w(0, 0)
+        load_w(0, 1)
+        load_w(1, 0)
+        load_w(1, 1)
+        nc.sync.dma_start(e_last[:], eT.rearrange("(p u t) c -> p u (t c)", u=2, t=2)[:, 1, :])
+        load_w(2, 0)
+        load_w(2, 1)
+        load_w(3, 0)
         nc.sync.dma_start(
             ux_col[:].rearrange("p (u q) -> p u q", q=2), ux.rearrange("(u p q) o -> p u (q o)", p=P, q=2))
-        nc.sync.dma_start(ts_table[0:1, :], ts[0:1, :])
-        y_rows = y.rearrange("(u p q) i -> p u q i", p=P, q=2)
-        for t in range(LANES):
-            if t > 0:
-                nc.sync.dma_start(e_lane[t][:], e_rows[:, t, :])
-            for part, cols in zip(w_part[t], halves):
-                nc.sync.dma_start(part[:], w_rows[:, t, cols])
-            if t in (1, 2):
-                nc.sync.dma_start(y_half[t - 1][:], y_rows[:, t - 1, :, :])
+        nc.sync.dma_start(y_half[0][:], y_rows[:, 0, :, :])
+        load_w(3, 1)
+        nc.sync.dma_start(y_half[1][:], y_rows[:, 1, :, :])
         nc.sync.dma_start(posn_list[:], posnoffs)
 
         nc.gpsimd.tensor_scalar(m2ux[:], ux_col[:], -2.0, 0.0, ALU.mult, ALU.add)
@@ -99,7 +109,6 @@ def tile_attend_gcbow_ns_pl_kernel(tc, eT, wT, ts, ux, y, coffs, posnoffs, sloto
         pairs = keep.tile([P, LANES, SLOTS], F32, name="pairs", tag="pairs_out", align_bytes=64)
         w_by_d = keep.tile([P, OUTW, LANES], BF16, name="w_by_d", tag="w_by_d", align_bytes=64)
         ts_i = keep.tile([P, OUTW], F32, name="ts_i")
-        ts_dealt = keep.tile([P, OUTW], F32, name="ts_dealt")
         signed_ux = [keep.tile([P, OUTW], F32, name="signed_ux%d" % q) for q in range(POS // P)]
         factor = [keep.tile([P, LANES, POS // 2], F32, name="factor%d" % u) for u in range(2)]
         column = {}
@@ -116,11 +125,12 @@ def tile_attend_gcbow_ns_pl_kernel(tc, eT, wT, ts, ux, y, coffs, posnoffs, sloto
                 ALU.mult, ALU.add)
 
         def turn_scales():
+            ts_dealt = keep.tile([P, OUTW], F32, name="ts_dealt")
             nc.gpsimd.tensor_scalar(dealt(ts_dealt[:]), listed(ts_i[:]), 1.0, 0.0, ALU.mult, ALU.add)
             ts_ps = turn_ps.tile([P, LANES, P], F32, name="ts_ps", tag="turn")
             for r in range(LANES):
                 nc.tensor.transpose(ts_ps[:, r, :], ts_dealt[:, P * r : P * (r + 1)], ident32[:])
-            column["ts"] = keep.tile([P, LANES], F32, name="ts_col", tag="w1_1", align_bytes=64)
+            column["ts"] = keep.tile([P, LANES], F32, name="ts_col", tag="w3_1", align_bytes=64)
             nc.scalar.copy(column["ts"][:], ts_ps[:, :, 0])
 
         def turn_factors(u):
@@ -135,32 +145,43 @@ def tile_attend_gcbow_ns_pl_kernel(tc, eT, wT, ts, ux, y, coffs, posnoffs, sloto
                         factor[u][:, r0 + r, :].rearrange("s (p q) -> s p q", q=2), f_ps[:, r, :, :].rearrange("s q p -> s p q"), ACT.Copy,
                         scale=column["ts"][:, r0 + r : r0 + r + 1])
 
-        nc.vector.tensor_copy(ts_i[:], ts_table[:].indirect(idx_list[:]))
-        for t in range(LANES):
+        def by_context(t):
             first = SLOTS * (LANES - 1 - t)
-            for u in range(2):
-                nc.vector.tensor_scalar(
-                    half_ec[:, first + 512 * u : first + 512 * (u + 1)],
-                    e_lane[t][:].indirect(ctx_list[:, 32 * u : 32 * (u + 1)]), 0.5, 0.0, ALU.mult, ALU.add)
-            nc.vector.tensor_copy(pairs[:, t, :], half_ec[:, first : first + WINDOW].indirect(slot_list[:]))
+            nc.vector.tensor_copy(e_c[:, first : first + SLOTS], e_lane[t].indirect(ctx_list[:]))
 
-            w_bf = ring.tile([P, WORDS], BF16, name="w_bf")
-            for part, cols in zip(w_part[t], halves):
-                nc.scalar.copy(w_bf[:, cols], part[:])
-            nc.scalar.activation(dealt(w_by_d[:, :, t]), w_bf[:].indirect(idx_list[:]), ACT.Copy)
-            if t in (1, 2):
-                u = t - 1
-                sign_labels(2 * u)
-                sign_labels(2 * u + 1)
-                if u == 0:
-                    turn_scales()
-                turn_factors(u)
-                clear(order[2 + u], "y_half%d" % u)
+        def by_position(t):
+            first = SLOTS * (LANES - 1 - t)
+            nc.vector.tensor_copy(pairs[:, t, :], e_c[:, first : first + WINDOW].indirect(slot_list[:]))
 
-        nc.gpsimd.memset(dh[:, LANES * POS :], 0.0)
+        for t in (0, 2):
+            by_context(t)
+            by_context(t + 1)
+            by_position(t)
+            by_position(t + 1)
+            if t == 0:
+                nc.vector.tensor_copy(ts_i[:], ts_table[:].indirect(idx_list[:]))
+        w_bf = {}
+
+        def cast_w(t, u):
+            if u == 0:
+                w_bf[t] = keep.tile([P, WORDS], BF16, name="w_bf%d" % t, tag="w_bf%d" % (t % 2), align_bytes=64)
+            nc.scalar.copy(w_bf[t][:, halves[u]], w_part[t][u][:])
+
+        cast_w(0, 0)
+        for t in range(LANES):
+            cast_w(t, 1)
+            if t + 1 < LANES:
+                cast_w(t + 1, 0)
+            nc.scalar.activation(dealt(w_by_d[:, :, t]), w_bf[t][:].indirect(idx_list[:]), ACT.Copy)
+
+        turn_scales()
+        for u in range(2):
+            sign_labels(2 * u)
+            sign_labels(2 * u + 1)
+            turn_factors(u)
 
         w_words = w_by_d[:].rearrange("p c t -> p (c t)").bitcast(F32)
-        w_by_i = keep.tile([P, OUTW, LANES], BF16, name="w_by_i", tag="w3_1", align_bytes=64)
+        w_by_i = {}
         w_ps = {}
         for u in range(2):
             w_ps[u] = dh_pool.tile([P, LANES, P], F32, name="w_ps%d" % u, tag="bank%d" % order[2 + u])
@@ -169,7 +190,7 @@ def tile_attend_gcbow_ns_pl_kernel(tc, eT, wT, ts, ux, y, coffs, posnoffs, sloto
 
         def lay_w(t):
             codes = w_ps[t // 2][:].rearrange("s r p -> s (r p)").bitcast(BF16).rearrange("s (r p e) -> s p r e", r=LANES, e=2)
-            nc.scalar.copy(w_by_i[:, P * t : P * (t + 1), :], codes[:, :, :, t % 2])
+            nc.scalar.copy(w_by_i[t], codes[:, :, :, t % 2])
 
         def mx_tiles(name, width):
             codes = keep.tile([P, width], U32, name=name + "_codes", align_bytes=64)
@@ -184,31 +205,33 @@ def tile_attend_gcbow_ns_pl_kernel(tc, eT, wT, ts, ux, y, coffs, posnoffs, sloto
         g_mx = mx_tiles("g", POS)
         wd_mx = mx_tiles("wd", OUTW)
         wi_mx = mx_tiles("wi", OUTW)
-        h_bf = {}
+        h_bf = keep.tile([P, POS, LANES], BF16, name="h_bf", tag="w_bf1", align_bytes=64)
         g_bf = keep.tile([P, POS, LANES], BF16, name="g_bf", align_bytes=64)
         chunks = [slice(P * c, P * (c + 1)) for c in range(POS // P)]
         pair_view = pairs[:].rearrange("p t (k i j) -> p k t i j", i=2, j=2)
 
         def pair_sum(c):
             ks = slice(64 * c, 64 * (c + 1))
-            h_bf[c] = keep.tile([P, P, LANES], BF16, name="h_bf%d" % c, tag="w_by_d" if c == 3 else "h_bf%d" % c, align_bytes=64)
             nc.vector.tensor_tensor(
-                h_bf[c][:].rearrange("p (k i) t -> p k t i", i=2),
+                h_bf[:, chunks[c], :].rearrange("p (k i) t -> p k t i", i=2),
                 pair_view[:, ks, :, :, 0], pair_view[:, ks, :, :, 1], ALU.add)
+
+        def quantize_h(c):
+            quantize(h_mx, chunks[c], h_bf[:, chunks[c], :], E4M3)
 
         sig = {}
 
         def score(c):
-            a_ps = mm_ps.tile([P, LANES, P], F32, name="a_ps", tag="score")
+            a_ps = turn_ps.tile([P, LANES, P], F32, name="a_ps", tag="turn")
             for r in range(LANES):
                 cols = slice(P * r, P * (r + 1))
                 nc.tensor.matmul_mx(
                     out=a_ps[:, r, :], lhsT=wd_mx[0][:, cols].bitcast(E4M3), lhsT_scale=wd_mx[1][:, cols],
                     rhs=h_mx[0][:, chunks[c]].bitcast(E4M3), rhs_scale=h_mx[1][:, chunks[c]], start=True, stop=True)
-            z = ring.tile([P, LANES, P], F32, name="z")
+            z = keep.tile([P, LANES, P], F32, name="z%d" % c, tag="z%d" % (c % 2), align_bytes=64)
             nc.vector.tensor_tensor(z[:], a_ps[:], factor[c // 2][:, :, chunks[c % 2]], ALU.mult)
-            sig[c] = ring.tile([P, LANES, P], F32, name="sig")
-            nc.scalar.activation(sig[c][:], z[:], ACT.Sigmoid)
+            sig[c] = keep.tile([P, LANES, P], F32, name="sig%d" % c, tag="w%d_1" % c if c < 3 else "sig3", align_bytes=64)
+            nc.scalar.activation(sig[c][:], z[:], ACT.Sigmoid, scale=0.5)
 
         def loss_gradient(c):
             nc.vector.tensor_tensor(
@@ -216,29 +239,34 @@ def tile_attend_gcbow_ns_pl_kernel(tc, eT, wT, ts, ux, y, coffs, posnoffs, sloto
                 sig[c][:].rearrange("s r (k i) -> s k r i", i=RUN),
                 factor[c // 2][:, :, chunks[c % 2]].rearrange("s r (k i) -> s k r i", i=RUN), ALU.mult)
 
+        quantize(wd_mx, slice(0, OUTW), w_by_d[:], E4M3)
         pair_sum(0)
         pair_sum(1)
-        quantize(h_mx, chunks[0], h_bf[0][:], E4M3)
+        quantize_h(0)
         pair_sum(2)
-        quantize(h_mx, chunks[1], h_bf[1][:], E4M3)
-        quantize(wd_mx, slice(0, OUTW), w_by_d[:], E4M3)
-        quantize(h_mx, chunks[2], h_bf[2][:], E4M3)
+        quantize_h(1)
         pair_sum(3)
+        quantize_h(2)
         score(0)
-        quantize(h_mx, chunks[3], h_bf[3][:], E4M3)
+        quantize_h(3)
         score(1)
         loss_gradient(0)
         score(2)
         loss_gradient(1)
         score(3)
-        for t in order:
+        w_first = keep.tile([P, P, LANES], BF16, name="w_first", tag="w3_1", align_bytes=64)
+        w_rest = keep.tile([P, LANES - 1, P, LANES], BF16, name="w_rest", tag="z1", align_bytes=64)
+        for n, t in enumerate(order):
+            w_by_i[t] = w_first[:] if n == 0 else w_rest[:, n - 1, :, :]
             lay_w(t)
+        quantize(wi_mx, chunks[order[0]], w_by_i[order[0]], E4M3)
         loss_gradient(2)
-        loss_gradient(3)
         quantize(g_mx, slice(0, 2 * P), g_bf[:, 0 : 2 * P, :], E5M2)
-        quantize(wi_mx, slice(0, OUTW), w_by_i[:], E4M3)
+        loss_gradient(3)
         quantize(g_mx, chunks[2], g_bf[:, chunks[2], :], E5M2)
         quantize(g_mx, chunks[3], g_bf[:, chunks[3], :], E5M2)
+        for j in order[1:]:
+            quantize(wi_mx, chunks[j], w_by_i[j], E4M3)
 
         dh_ps = {}
         for j in order:
@@ -255,7 +283,7 @@ def tile_attend_gcbow_ns_pl_kernel(tc, eT, wT, ts, ux, y, coffs, posnoffs, sloto
         by_slot = {}
 
         def look_up(j):
-            tag = "first_window" if j == order[-1] else "w%d_0" % j
+            tag = "window%d" % order[0] if j == order[-1] else "w%d_0" % j
             by_slot[j] = keep.tile([P, SLOTS], F32, name="dc%d" % j, tag=tag, align_bytes=64)
             nc.vector.tensor_copy(by_slot[j][:], dh[:, start[j] : start[j] + WINDOW].indirect(posn_list[:]))
 
@@ -274,7 +302,7 @@ def tile_attend_gcbow_ns_pl_kernel(tc, eT, wT, ts, ux, y, coffs, posnoffs, sloto
 
         last = order[-1]
         out_codes = keep.tile([P, WORDS], U32, name="out_codes", align_bytes=64)
-        out_scales = keep.tile([P, WORDS], U8, name="out_scales", align_bytes=64)
+        out_scales = keep.tile([P, WORDS // 4], U8, name="out_scales", align_bytes=64)
         words_hbm = out_1[0].rearrange("p c l -> p (c l)").bitcast(I32)
         pieces = [slice(TAIL_CHUNK * n, TAIL_CHUNK * (n + 1)) for n in range(WORDS // TAIL_CHUNK)]
         half = len(pieces) // 2
@@ -284,10 +312,13 @@ def tile_attend_gcbow_ns_pl_kernel(tc, eT, wT, ts, ux, y, coffs, posnoffs, sloto
         for n in range(len(pieces)):
             if n + 1 < half:
                 nc.vector.tensor_copy(out_bf[:, pieces[n + 1], last], grad[last][:, pieces[n + 1]])
-            quantize((out_codes, out_scales), pieces[n], out_bf[:, pieces[n], :], E4M3)
+            nc.vector.quantize_mx(
+                out=out_codes[:, pieces[n]].bitcast(E4M3), scales=out_scales[4 * (n // 2) :, pieces[n % 2]],
+                in_=out_bf[:, pieces[n], :].rearrange("p c l -> p (c l)"))
             if n % 2 == 1:
                 cols = slice(pieces[n - 1].start, pieces[n].stop)
                 nc.sync.dma_start(words_hbm[:, cols], out_codes[:, cols].bitcast(I32))
-        scales_hbm = out_2[0].bitcast(I32)
+        scales_hbm = out_2[0].bitcast(I32).rearrange("f (a c) -> a f c", a=4)
         for quad in range(4):
-            nc.scalar.dma_start(scales_hbm[4 * quad : 4 * quad + 4, :], out_scales[32 * quad : 32 * quad + 4, :].bitcast(I32))
+            nc.scalar.dma_start(
+                scales_hbm[:, 4 * quad : 4 * quad + 4, :], out_scales[32 * quad : 32 * quad + 16, :].bitcast(I32))

@@ -26,7 +26,6 @@ WINDOW = 1376
 TAIL_CHUNK = 256
 RUN = 4
 ROW = 8
-TS_SPLIT = 704
 
 
 def tile_attend_gcbow_ns_pl_kernel(tc, eT, wT, ts, ux, y, coffs, posnoffs, slotoffs, offs, out_0, out_1, out_2):
@@ -44,9 +43,7 @@ def tile_attend_gcbow_ns_pl_kernel(tc, eT, wT, ts, ux, y, coffs, posnoffs, sloto
         e_rows = eT.rearrange("(p t) c -> p t c", t=LANES)
         w_rows = wT.rearrange("(p t) c -> p t c", t=LANES)
         out_rows = out_0.rearrange("(p t) c -> p t c", t=LANES)
-        e_first = [keep.tile([P, WORDS], F32, name="e_lane%d" % t) for t in range(2)]
-        e_last = keep.tile([P, 2 * WORDS], F32, name="e_last")
-        e_lane = [e_first[0][:], e_first[1][:], e_last[:, :WORDS], e_last[:, WORDS:]]
+        e_lane = [keep.tile([P, WORDS], F32, name="e_lane%d" % t)[:] for t in range(LANES)]
         halves = [slice(0, WORDS // 2), slice(WORDS // 2, WORDS)]
         w_part = [
             [keep.tile([P, WORDS // 2], F32, name="w%d_%d" % (t, u), tag="w%d_%d" % (t, u), align_bytes=64) for u in range(2)]
@@ -61,8 +58,10 @@ def tile_attend_gcbow_ns_pl_kernel(tc, eT, wT, ts, ux, y, coffs, posnoffs, sloto
 
         order = [1, 3, 2, 0]
 
-        nc.gpsimd.memset(ts_table[:, TS_SPLIT:], 0.0)
-        nc.vector.memset(ts_table[:, :TS_SPLIT], 0.0)
+        warm = keep.tile([P, 2], F32, name="warm")
+        nc.vector.memset(warm[:, 0:1], 0.0)
+        nc.scalar.activation(warm[:, 1:2], warm[:, 0:1], ACT.Sigmoid)
+        nc.gpsimd.memset(ts_table[:], 0.0)
         make_identity(nc, ident32[:])
         nc.gpsimd.memset(e_c[:, LANES * SLOTS :], 0.0)
         grad = {}
@@ -75,8 +74,6 @@ def tile_attend_gcbow_ns_pl_kernel(tc, eT, wT, ts, ux, y, coffs, posnoffs, sloto
             clear(j, "window%d" % j)
         nc.gpsimd.memset(dh[:, LANES * POS :], 0.0)
 
-        warm = keep.tile([P, 1], F32, name="warm")
-        nc.scalar.activation(warm[:], ident32[:, 0:1], ACT.Sigmoid)
 
         nc.sync.dma_start(ctx_list[:], coffs)
         nc.sync.dma_start(e_lane[0], e_rows[:, 0, :])
@@ -88,14 +85,15 @@ def tile_attend_gcbow_ns_pl_kernel(tc, eT, wT, ts, ux, y, coffs, posnoffs, sloto
         nc.sync.dma_start(e_lane[1], e_rows[:, 1, :])
         nc.sync.dma_start(slot_list[:], slotoffs)
         nc.sync.dma_start(idx_list[:], offs)
-        nc.sync.dma_start(ts_table[0:1, :], ts[0:1, :])
         load_w(0, 0)
         load_w(0, 1)
         load_w(1, 0)
         load_w(1, 1)
-        nc.sync.dma_start(e_last[:], eT.rearrange("(p u t) c -> p u (t c)", u=2, t=2)[:, 1, :])
+        nc.sync.dma_start(e_lane[2], e_rows[:, 2, :])
+        nc.sync.dma_start(ts_table[0:1, :], ts[0:1, :])
         load_w(2, 0)
         load_w(2, 1)
+        nc.sync.dma_start(e_lane[3], e_rows[:, 3, :])
         load_w(3, 0)
         nc.sync.dma_start(
             ux_col[:].rearrange("p (u q) -> p u q", q=2), ux.rearrange("(u p q) o -> p u (q o)", p=P, q=2))
@@ -153,13 +151,15 @@ def tile_attend_gcbow_ns_pl_kernel(tc, eT, wT, ts, ux, y, coffs, posnoffs, sloto
             first = SLOTS * (LANES - 1 - t)
             nc.vector.tensor_copy(pairs[:, t, :], e_c[:, first : first + WINDOW].indirect(slot_list[:]))
 
-        for t in (0, 2):
-            by_context(t)
-            by_context(t + 1)
-            by_position(t)
-            by_position(t + 1)
-            if t == 0:
-                nc.vector.tensor_copy(ts_i[:], ts_table[:].indirect(idx_list[:]))
+        by_context(0)
+        by_context(1)
+        by_position(0)
+        by_position(1)
+        by_context(2)
+        nc.vector.tensor_copy(ts_i[:], ts_table[:].indirect(idx_list[:]))
+        by_position(2)
+        by_context(3)
+        by_position(3)
         w_bf = {}
 
         def cast_w(t, u):

@@ -21,48 +21,49 @@ LANES = 4
 WORDS = 2048
 SLOTS = 1024
 POS = 512
-OUTW = 512
+OUT_SLOTS = 512
+BLOCK_ROWS = 8
 WINDOW = 1376
-TAIL_CHUNK = 256
-RUN = 4
-ROW = 8
+LINE = 4
+PIECE = 256
+ORDER = (1, 3, 2, 0)
 
 
 def tile_attend_gcbow_ns_pl_kernel(tc, eT, wT, ts, ux, y, coffs, posnoffs, slotoffs, offs, out_0, out_1, out_2):
     nc = tc.nc
-    with ExitStack() as ctx:
-        keep = ctx.enter_context(tc.tile_pool(name="keep", bufs=1))
-        ring = ctx.enter_context(tc.tile_pool(name="ring", bufs=2))
-        turn_ps = ctx.enter_context(tc.psum_pool(name="turn", bufs=4))
-        dh_pool = ctx.enter_context(tc.psum_pool(name="dh", bufs=1))
+    with ExitStack() as stack:
+        keep = stack.enter_context(tc.tile_pool(name="keep", bufs=1))
+        ring_ps = stack.enter_context(tc.psum_pool(name="ring", bufs=4))
+        lane_ps = stack.enter_context(tc.psum_pool(name="lanes", bufs=1))
 
         ctx_list = keep.tile([P, SLOTS // 16], U16, name="ctx_list")
         posn_list = keep.tile([P, SLOTS // 16], U16, name="posn_list")
         slot_list = keep.tile([P, SLOTS // 16], U16, name="slot_list")
-        idx_list = keep.tile([P, OUTW // 16], U16, name="idx_list")
+        idx_list = keep.tile([P, OUT_SLOTS // 16], U16, name="idx_list")
         e_rows = eT.rearrange("(p t) c -> p t c", t=LANES)
         w_rows = wT.rearrange("(p t) c -> p t c", t=LANES)
         out_rows = out_0.rearrange("(p t) c -> p t c", t=LANES)
+        y_rows = y.rearrange("(u p q) i -> p u q i", p=P, q=2)
+        ux_rows = ux.rearrange("(u p q) o -> p u (q o)", p=P, q=2)
         e_lane = [keep.tile([P, WORDS], F32, name="e_lane%d" % t)[:] for t in range(LANES)]
         halves = [slice(0, WORDS // 2), slice(WORDS // 2, WORDS)]
         w_part = [
             [keep.tile([P, WORDS // 2], F32, name="w%d_%d" % (t, u), tag="w%d_%d" % (t, u), align_bytes=64) for u in range(2)]
             for t in range(LANES)]
         ts_table = keep.tile([P, WORDS], F32, name="ts_table")
-        y_half = [keep.tile([P, 2, OUTW], F32, name="y_half%d" % u, tag="y_half%d" % u, align_bytes=64) for u in range(2)]
+        y_half = [keep.tile([P, 2, OUT_SLOTS], F32, name="y_half%d" % u, align_bytes=64) for u in range(2)]
         ux_col = keep.tile([P, LANES], F32, name="ux_col")
-        m2ux = keep.tile([P, LANES], F32, name="m2ux")
-        ident32 = keep.tile([P, P], F32, name="ident32")
+        minus_2ux = keep.tile([P, LANES], F32, name="minus_2ux")
+        identity = keep.tile([P, P], F32, name="identity")
         e_c = keep.tile([P, (LANES - 1) * SLOTS + WINDOW], F32, name="e_c")
         dh = keep.tile([P, (LANES - 1) * POS + WINDOW], F32, name="dh")
-
-        order = [1, 3, 2, 0]
 
         warm = keep.tile([P, 2], F32, name="warm")
         nc.vector.memset(warm[:, 0:1], 0.0)
         nc.scalar.activation(warm[:, 1:2], warm[:, 0:1], ACT.Sigmoid)
+
         nc.gpsimd.memset(ts_table[:], 0.0)
-        make_identity(nc, ident32[:])
+        make_identity(nc, identity[:])
         nc.gpsimd.memset(e_c[:, LANES * SLOTS :], 0.0)
         grad = {}
 
@@ -70,96 +71,65 @@ def tile_attend_gcbow_ns_pl_kernel(tc, eT, wT, ts, ux, y, coffs, posnoffs, sloto
             grad[j] = keep.tile([P, WORDS], F32, name="grad%d" % j, tag=tag, align_bytes=64)
             nc.gpsimd.memset(grad[j][:], 0.0)
 
-        for j in order:
+        for j in ORDER[:-1]:
             clear(j, "window%d" % j)
         nc.gpsimd.memset(dh[:, LANES * POS :], 0.0)
-
-
-        nc.sync.dma_start(ctx_list[:], coffs)
-        nc.sync.dma_start(e_lane[0], e_rows[:, 0, :])
-        y_rows = y.rearrange("(u p q) i -> p u q i", p=P, q=2)
 
         def load_w(t, u):
             nc.sync.dma_start(w_part[t][u][:], w_rows[:, t, halves[u]])
 
+        nc.sync.dma_start(ctx_list[:], coffs)
+        nc.sync.dma_start(e_lane[0], e_rows[:, 0, :])
         nc.sync.dma_start(e_lane[1], e_rows[:, 1, :])
         nc.sync.dma_start(slot_list[:], slotoffs)
         nc.sync.dma_start(idx_list[:], offs)
-        load_w(0, 0)
-        load_w(0, 1)
-        load_w(1, 0)
-        load_w(1, 1)
+        for t in range(2):
+            load_w(t, 0)
+            load_w(t, 1)
         nc.sync.dma_start(e_lane[2], e_rows[:, 2, :])
         nc.sync.dma_start(ts_table[0:1, :], ts[0:1, :])
         load_w(2, 0)
         load_w(2, 1)
         nc.sync.dma_start(e_lane[3], e_rows[:, 3, :])
         load_w(3, 0)
-        nc.sync.dma_start(
-            ux_col[:].rearrange("p (u q) -> p u q", q=2), ux.rearrange("(u p q) o -> p u (q o)", p=P, q=2))
+        nc.sync.dma_start(ux_col[:].rearrange("p (u q) -> p u q", q=2), ux_rows)
         nc.sync.dma_start(y_half[0][:], y_rows[:, 0, :, :])
         load_w(3, 1)
         nc.sync.dma_start(y_half[1][:], y_rows[:, 1, :, :])
         nc.sync.dma_start(posn_list[:], posnoffs)
 
-        nc.gpsimd.tensor_scalar(m2ux[:], ux_col[:], -2.0, 0.0, ALU.mult, ALU.add)
+        nc.gpsimd.tensor_scalar(minus_2ux[:], ux_col[:], -2.0, 0.0, ALU.mult, ALU.add)
 
-        pairs = keep.tile([P, LANES, SLOTS], F32, name="pairs", tag="pairs_out", align_bytes=64)
-        w_by_d = keep.tile([P, OUTW, LANES], BF16, name="w_by_d", tag="w_by_d", align_bytes=64)
-        ts_i = keep.tile([P, OUTW], F32, name="ts_i")
-        signed_ux = [keep.tile([P, OUTW], F32, name="signed_ux%d" % q) for q in range(POS // P)]
+        pairs = keep.tile([P, LANES, SLOTS], F32, name="pairs", tag="pairs_then_out", align_bytes=64)
+        w_by_d = keep.tile([P, OUT_SLOTS, LANES], BF16, name="w_by_d", align_bytes=64)
+        ts_i = keep.tile([P, OUT_SLOTS], F32, name="ts_i")
+        signed_ux = [keep.tile([P, OUT_SLOTS], F32, name="signed_ux%d" % n) for n in range(POS // P)]
         factor = [keep.tile([P, LANES, POS // 2], F32, name="factor%d" % u) for u in range(2)]
-        column = {}
 
         def listed(row):
-            return row.rearrange("p (b r a) -> p b r a", r=LANES, a=ROW)
+            return row.rearrange("p (n r a) -> p n r a", r=LANES, a=BLOCK_ROWS)
 
         def dealt(row):
-            return row.rearrange("p (r b a) -> p b r a", r=LANES, a=ROW)
+            return row.rearrange("p (r n a) -> p n r a", r=LANES, a=BLOCK_ROWS)
 
-        def sign_labels(q):
-            nc.gpsimd.tensor_scalar(
-                dealt(signed_ux[q][:]), listed(y_half[q // 2][:, q % 2, :]), m2ux[:, q : q + 1], ux_col[:, q : q + 1],
-                ALU.mult, ALU.add)
-
-        def turn_scales():
-            ts_dealt = keep.tile([P, OUTW], F32, name="ts_dealt")
-            nc.gpsimd.tensor_scalar(dealt(ts_dealt[:]), listed(ts_i[:]), 1.0, 0.0, ALU.mult, ALU.add)
-            ts_ps = turn_ps.tile([P, LANES, P], F32, name="ts_ps", tag="turn")
-            for r in range(LANES):
-                nc.tensor.transpose(ts_ps[:, r, :], ts_dealt[:, P * r : P * (r + 1)], ident32[:])
-            column["ts"] = keep.tile([P, LANES], F32, name="ts_col", tag="w3_1", align_bytes=64)
-            nc.scalar.copy(column["ts"][:], ts_ps[:, :, 0])
-
-        def turn_factors(u):
-            for r0 in range(0, LANES, 2):
-                f_ps = turn_ps.tile([P, 2, 2, P], F32, name="f_ps", tag="turn")
-                for r in range(2):
-                    for q in range(2):
-                        nc.tensor.transpose(
-                            f_ps[:, r, q, :], signed_ux[2 * u + q][:, P * (r0 + r) : P * (r0 + r + 1)], ident32[:])
-                for r in range(2):
-                    nc.scalar.activation(
-                        factor[u][:, r0 + r, :].rearrange("s (p q) -> s p q", q=2), f_ps[:, r, :, :].rearrange("s q p -> s p q"), ACT.Copy,
-                        scale=column["ts"][:, r0 + r : r0 + r + 1])
-
-        def by_context(t):
+        def gather_context(t):
             first = SLOTS * (LANES - 1 - t)
             nc.vector.tensor_copy(e_c[:, first : first + SLOTS], e_lane[t].indirect(ctx_list[:]))
 
-        def by_position(t):
+        def gather_pairs(t):
             first = SLOTS * (LANES - 1 - t)
             nc.vector.tensor_copy(pairs[:, t, :], e_c[:, first : first + WINDOW].indirect(slot_list[:]))
 
-        by_context(0)
-        by_context(1)
-        by_position(0)
-        by_position(1)
-        by_context(2)
+        gather_context(0)
+        gather_context(1)
+        gather_pairs(0)
+        gather_pairs(1)
+        gather_context(2)
         nc.vector.tensor_copy(ts_i[:], ts_table[:].indirect(idx_list[:]))
-        by_position(2)
-        by_context(3)
-        by_position(3)
+        gather_pairs(2)
+        gather_context(3)
+        gather_pairs(3)
+
         w_bf = {}
 
         def cast_w(t, u):
@@ -174,23 +144,37 @@ def tile_attend_gcbow_ns_pl_kernel(tc, eT, wT, ts, ux, y, coffs, posnoffs, sloto
                 cast_w(t + 1, 0)
             nc.scalar.activation(dealt(w_by_d[:, :, t]), w_bf[t][:].indirect(idx_list[:]), ACT.Copy)
 
-        turn_scales()
+        ts_dealt = keep.tile([P, OUT_SLOTS], F32, name="ts_dealt")
+        nc.gpsimd.tensor_scalar(dealt(ts_dealt[:]), listed(ts_i[:]), 1.0, 0.0, ALU.mult, ALU.add)
+        ts_ps = ring_ps.tile([P, LANES, P], F32, name="ts_ps", tag="ring")
+        for r in range(LANES):
+            nc.tensor.transpose(ts_ps[:, r, :], ts_dealt[:, P * r : P * (r + 1)], identity[:])
+        ts_col = keep.tile([P, LANES], F32, name="ts_col", tag="w3_1", align_bytes=64)
+        nc.scalar.copy(ts_col[:], ts_ps[:, :, 0])
+
         for u in range(2):
-            sign_labels(2 * u)
-            sign_labels(2 * u + 1)
-            turn_factors(u)
+            for q in range(2):
+                n = 2 * u + q
+                nc.gpsimd.tensor_scalar(
+                    dealt(signed_ux[n][:]), listed(y_half[u][:, q, :]), minus_2ux[:, n : n + 1], ux_col[:, n : n + 1],
+                    ALU.mult, ALU.add)
+            for r0 in range(0, LANES, 2):
+                f_ps = ring_ps.tile([P, 2, 2, P], F32, name="f_ps", tag="ring")
+                for r in range(2):
+                    for q in range(2):
+                        nc.tensor.transpose(
+                            f_ps[:, r, q, :], signed_ux[2 * u + q][:, P * (r0 + r) : P * (r0 + r + 1)], identity[:])
+                for r in range(2):
+                    nc.scalar.activation(
+                        factor[u][:, r0 + r, :].rearrange("s (p q) -> s p q", q=2),
+                        f_ps[:, r, :, :].rearrange("s q p -> s p q"), ACT.Copy, scale=ts_col[:, r0 + r : r0 + r + 1])
 
         w_words = w_by_d[:].rearrange("p c t -> p (c t)").bitcast(F32)
-        w_by_i = {}
         w_ps = {}
-        for u in range(2):
-            w_ps[u] = dh_pool.tile([P, LANES, P], F32, name="w_ps%d" % u, tag="bank%d" % order[2 + u])
+        for v in range(2):
+            w_ps[v] = lane_ps.tile([P, LANES, P], F32, name="w_ps%d" % v, tag="bank%d" % ORDER[2 + v])
             for r in range(LANES):
-                nc.tensor.transpose(w_ps[u][:, r, :], w_words[:, 2 * P * r + u : 2 * P * (r + 1) : 2], ident32[:])
-
-        def lay_w(t):
-            codes = w_ps[t // 2][:].rearrange("s r p -> s (r p)").bitcast(BF16).rearrange("s (r p e) -> s p r e", r=LANES, e=2)
-            nc.scalar.copy(w_by_i[t], codes[:, :, :, t % 2])
+                nc.tensor.transpose(w_ps[v][:, r, :], w_words[:, 2 * P * r + v : 2 * P * (r + 1) : 2], identity[:])
 
         def mx_tiles(name, width):
             codes = keep.tile([P, width], U32, name=name + "_codes", align_bytes=64)
@@ -201,124 +185,121 @@ def tile_attend_gcbow_ns_pl_kernel(tc, eT, wT, ts, ux, y, coffs, posnoffs, sloto
             nc.vector.quantize_mx(
                 out=operand[0][:, cols].bitcast(fmt), scales=operand[1][:, cols], in_=grouped.rearrange("p c l -> p (c l)"))
 
-        h_mx = mx_tiles("h", POS)
+        s_mx = mx_tiles("s", POS)
         g_mx = mx_tiles("g", POS)
-        wd_mx = mx_tiles("wd", OUTW)
-        wi_mx = mx_tiles("wi", OUTW)
-        h_bf = keep.tile([P, POS, LANES], BF16, name="h_bf", tag="w_bf1", align_bytes=64)
+        wd_mx = mx_tiles("wd", OUT_SLOTS)
+        wi_mx = mx_tiles("wi", LANES * P)
+        s_bf = keep.tile([P, POS, LANES], BF16, name="s_bf", tag="w_bf1", align_bytes=64)
         g_bf = keep.tile([P, POS, LANES], BF16, name="g_bf", align_bytes=64)
-        chunks = [slice(P * c, P * (c + 1)) for c in range(POS // P)]
+        chunks = [slice(P * c, P * (c + 1)) for c in range(LANES)]
         pair_view = pairs[:].rearrange("p t (k i j) -> p k t i j", i=2, j=2)
 
         def pair_sum(c):
-            ks = slice(64 * c, 64 * (c + 1))
+            ks = slice(P // 2 * c, P // 2 * (c + 1))
             nc.vector.tensor_tensor(
-                h_bf[:, chunks[c], :].rearrange("p (k i) t -> p k t i", i=2),
+                s_bf[:, chunks[c], :].rearrange("p (k i) t -> p k t i", i=2),
                 pair_view[:, ks, :, :, 0], pair_view[:, ks, :, :, 1], ALU.add)
 
-        def quantize_h(c):
-            quantize(h_mx, chunks[c], h_bf[:, chunks[c], :], E4M3)
+        def quantize_s(c):
+            quantize(s_mx, chunks[c], s_bf[:, chunks[c], :], E4M3)
 
         sig = {}
 
         def score(c):
-            a_ps = turn_ps.tile([P, LANES, P], F32, name="a_ps", tag="turn")
+            a_ps = ring_ps.tile([P, LANES, P], F32, name="a_ps", tag="ring")
             for r in range(LANES):
-                cols = slice(P * r, P * (r + 1))
                 nc.tensor.matmul_mx(
-                    out=a_ps[:, r, :], lhsT=wd_mx[0][:, cols].bitcast(E4M3), lhsT_scale=wd_mx[1][:, cols],
-                    rhs=h_mx[0][:, chunks[c]].bitcast(E4M3), rhs_scale=h_mx[1][:, chunks[c]], start=True, stop=True)
+                    out=a_ps[:, r, :], lhsT=wd_mx[0][:, chunks[r]].bitcast(E4M3), lhsT_scale=wd_mx[1][:, chunks[r]],
+                    rhs=s_mx[0][:, chunks[c]].bitcast(E4M3), rhs_scale=s_mx[1][:, chunks[c]], start=True, stop=True)
             z = keep.tile([P, LANES, P], F32, name="z%d" % c, tag="z%d" % (c % 2), align_bytes=64)
             nc.vector.tensor_tensor(z[:], a_ps[:], factor[c // 2][:, :, chunks[c % 2]], ALU.mult)
-            sig[c] = keep.tile([P, LANES, P], F32, name="sig%d" % c, tag="w%d_1" % c if c < 3 else "sig3", align_bytes=64)
+            tag = "w%d_1" % c if c + 1 < LANES else "sig_last"
+            sig[c] = keep.tile([P, LANES, P], F32, name="sig%d" % c, tag=tag, align_bytes=64)
             nc.scalar.activation(sig[c][:], z[:], ACT.Sigmoid, scale=0.5)
 
         def loss_gradient(c):
             nc.vector.tensor_tensor(
-                g_bf[:, chunks[c], :].rearrange("s (k i) r -> s k r i", i=RUN),
-                sig[c][:].rearrange("s r (k i) -> s k r i", i=RUN),
-                factor[c // 2][:, :, chunks[c % 2]].rearrange("s r (k i) -> s k r i", i=RUN), ALU.mult)
+                g_bf[:, chunks[c], :].rearrange("s (k i) r -> s k r i", i=LINE),
+                sig[c][:].rearrange("s r (k i) -> s k r i", i=LINE),
+                factor[c // 2][:, :, chunks[c % 2]].rearrange("s r (k i) -> s k r i", i=LINE), ALU.mult)
 
-        quantize(wd_mx, slice(0, OUTW), w_by_d[:], E4M3)
+        quantize(wd_mx, slice(0, OUT_SLOTS), w_by_d[:], E4M3)
         pair_sum(0)
-        pair_sum(1)
-        quantize_h(0)
-        pair_sum(2)
-        quantize_h(1)
-        pair_sum(3)
-        quantize_h(2)
+        for c in range(1, LANES):
+            pair_sum(c)
+            quantize_s(c - 1)
         score(0)
-        quantize_h(3)
+        quantize_s(3)
         score(1)
         loss_gradient(0)
         score(2)
         loss_gradient(1)
         score(3)
+
         w_first = keep.tile([P, P, LANES], BF16, name="w_first", tag="w3_1", align_bytes=64)
         w_rest = keep.tile([P, LANES - 1, P, LANES], BF16, name="w_rest", tag="z1", align_bytes=64)
-        for n, t in enumerate(order):
+        w_by_i = {}
+        for n, t in enumerate(ORDER):
             w_by_i[t] = w_first[:] if n == 0 else w_rest[:, n - 1, :, :]
-            lay_w(t)
-        quantize(wi_mx, chunks[order[0]], w_by_i[order[0]], E4M3)
+            turned = w_ps[t // 2][:].rearrange("s r p -> s (r p)").bitcast(BF16).rearrange("s (r p e) -> s p r e", r=LANES, e=2)
+            nc.scalar.copy(w_by_i[t], turned[:, :, :, t % 2])
+        quantize(wi_mx, chunks[ORDER[0]], w_by_i[ORDER[0]], E4M3)
         loss_gradient(2)
         quantize(g_mx, slice(0, 2 * P), g_bf[:, 0 : 2 * P, :], E5M2)
         loss_gradient(3)
         quantize(g_mx, chunks[2], g_bf[:, chunks[2], :], E5M2)
         quantize(g_mx, chunks[3], g_bf[:, chunks[3], :], E5M2)
-        for j in order[1:]:
+        for j in ORDER[1:]:
             quantize(wi_mx, chunks[j], w_by_i[j], E4M3)
 
         dh_ps = {}
-        for j in order:
-            cols = slice(P * j, P * (j + 1))
-            dh_ps[j] = dh_pool.tile([P, POS], F32, name="dh_ps%d" % j, tag="bank%d" % j)
+        for j in ORDER:
+            dh_ps[j] = lane_ps.tile([P, POS], F32, name="dh_ps%d" % j, tag="bank%d" % j)
             nc.tensor.matmul_mx(
-                out=dh_ps[j][:], lhsT=wi_mx[0][:, cols].bitcast(E4M3), lhsT_scale=wi_mx[1][:, cols],
+                out=dh_ps[j][:], lhsT=wi_mx[0][:, chunks[j]].bitcast(E4M3), lhsT_scale=wi_mx[1][:, chunks[j]],
                 rhs=g_mx[0][:].bitcast(E5M2), rhs_scale=g_mx[1][:], start=True, stop=True)
-        start = {j: POS * (LANES - 1 - n) for n, j in enumerate(order)}
-        for j in order:
-            nc.scalar.activation(dh[:, start[j] : start[j] + POS], dh_ps[j][:], ACT.Copy, scale=0.5)
+        dh_first = {j: POS * (LANES - 1 - n) for n, j in enumerate(ORDER)}
+        for j in ORDER:
+            nc.scalar.activation(dh[:, dh_first[j] : dh_first[j] + POS], dh_ps[j][:], ACT.Copy, scale=0.5)
 
-        out_bf = keep.tile([P, WORDS, LANES], BF16, name="out_bf", tag="pairs_out", align_bytes=64)
-        by_slot = {}
+        out_bf = keep.tile([P, WORDS, LANES], BF16, name="out_bf", tag="pairs_then_out", align_bytes=64)
+        de = {}
 
         def look_up(j):
-            tag = "window%d" % order[0] if j == order[-1] else "w%d_0" % j
-            by_slot[j] = keep.tile([P, SLOTS], F32, name="dc%d" % j, tag=tag, align_bytes=64)
-            nc.vector.tensor_copy(by_slot[j][:], dh[:, start[j] : start[j] + WINDOW].indirect(posn_list[:]))
+            de[j] = keep.tile([P, SLOTS], F32, name="de%d" % j, tag="w%d_0" % j, align_bytes=64)
+            nc.vector.tensor_copy(de[j][:], dh[:, dh_first[j] : dh_first[j] + WINDOW].indirect(posn_list[:]))
 
         def place(j):
-            nc.vector.tensor_copy(grad[j][:].indirect(ctx_list[:]), by_slot[j][:])
+            nc.vector.tensor_copy(grad[j][:].indirect(ctx_list[:]), de[j][:])
             nc.sync.dma_start(out_rows[:, j, :], grad[j][:])
 
-        look_up(order[0])
-        for n, j in enumerate(order[:-1]):
-            if n + 2 < LANES:
-                look_up(order[n + 1])
+        look_up(ORDER[0])
+        for n, j in enumerate(ORDER[:-1]):
+            look_up(ORDER[n + 1])
             place(j)
             nc.scalar.copy(out_bf[:, :, j], grad[j][:])
-        look_up(order[-1])
-        place(order[-1])
+        last = ORDER[-1]
+        clear(last, "window%d" % ORDER[0])
+        place(last)
 
-        last = order[-1]
         out_codes = keep.tile([P, WORDS], U32, name="out_codes", align_bytes=64)
         out_scales = keep.tile([P, WORDS // 4], U8, name="out_scales", align_bytes=64)
         words_hbm = out_1[0].rearrange("p c l -> p (c l)").bitcast(I32)
-        pieces = [slice(TAIL_CHUNK * n, TAIL_CHUNK * (n + 1)) for n in range(WORDS // TAIL_CHUNK)]
+        pieces = [slice(PIECE * n, PIECE * (n + 1)) for n in range(WORDS // PIECE)]
         half = len(pieces) // 2
-        for n in range(half):
-            nc.scalar.copy(out_bf[:, pieces[half + n], last], grad[last][:, pieces[half + n]])
+        for cols in pieces[half:]:
+            nc.scalar.copy(out_bf[:, cols, last], grad[last][:, cols])
         nc.vector.tensor_copy(out_bf[:, pieces[0], last], grad[last][:, pieces[0]])
-        for n in range(len(pieces)):
+        for n, cols in enumerate(pieces):
             if n + 1 < half:
                 nc.vector.tensor_copy(out_bf[:, pieces[n + 1], last], grad[last][:, pieces[n + 1]])
             nc.vector.quantize_mx(
-                out=out_codes[:, pieces[n]].bitcast(E4M3), scales=out_scales[4 * (n // 2) :, pieces[n % 2]],
-                in_=out_bf[:, pieces[n], :].rearrange("p c l -> p (c l)"))
+                out=out_codes[:, cols].bitcast(E4M3), scales=out_scales[4 * (n // 2) :, pieces[n % 2]],
+                in_=out_bf[:, cols, :].rearrange("p c l -> p (c l)"))
             if n % 2 == 1:
-                cols = slice(pieces[n - 1].start, pieces[n].stop)
-                nc.sync.dma_start(words_hbm[:, cols], out_codes[:, cols].bitcast(I32))
+                quarter = slice(pieces[n - 1].start, cols.stop)
+                nc.sync.dma_start(words_hbm[:, quarter], out_codes[:, quarter].bitcast(I32))
         scales_hbm = out_2[0].bitcast(I32).rearrange("f (a c) -> a f c", a=4)
-        for quad in range(4):
+        for group in range(4):
             nc.scalar.dma_start(
-                scales_hbm[:, 4 * quad : 4 * quad + 4, :], out_scales[32 * quad : 32 * quad + 16, :].bitcast(I32))
+                scales_hbm[:, 4 * group : 4 * group + 4, :], out_scales[32 * group : 32 * group + 16, :].bitcast(I32))

@@ -33,8 +33,7 @@ def tile_attend_gcbow_ns_pl_kernel(tc, eT, wT, ts, ux, y, coffs, posnoffs, sloto
     nc = tc.nc
     with ExitStack() as stack:
         keep = stack.enter_context(tc.tile_pool(name="keep", bufs=1))
-        ring_ps = stack.enter_context(tc.psum_pool(name="ring", bufs=4))
-        lane_ps = stack.enter_context(tc.psum_pool(name="lanes", bufs=1))
+        banks = stack.enter_context(tc.psum_pool(name="banks", bufs=1))
 
         ctx_list = keep.tile([P, SLOTS // 16], U16, name="ctx_list")
         posn_list = keep.tile([P, SLOTS // 16], U16, name="posn_list")
@@ -55,16 +54,16 @@ def tile_attend_gcbow_ns_pl_kernel(tc, eT, wT, ts, ux, y, coffs, posnoffs, sloto
         ux_col = keep.tile([P, LANES], F32, name="ux_col")
         minus_2ux = keep.tile([P, LANES], F32, name="minus_2ux")
         identity = keep.tile([P, P], F32, name="identity")
-        e_c = keep.tile([P, (LANES - 1) * SLOTS + WINDOW], F32, name="e_c")
+        e_c = keep.tile([P, LANES * SLOTS], F32, name="e_c")
         dh = keep.tile([P, (LANES - 1) * POS + WINDOW], F32, name="dh")
 
+        nc.scalar.dma_start(ts_table[P - 1 : P, :], ts[0:1, :])
         warm = keep.tile([P, 2], F32, name="warm")
         nc.vector.memset(warm[:, 0:1], 0.0)
         nc.scalar.activation(warm[:, 1:2], warm[:, 0:1], ACT.Sigmoid)
 
-        nc.gpsimd.memset(ts_table[:], 0.0)
+        nc.gpsimd.memset(ts_table[0 : P - 1, :], 0.0)
         make_identity(nc, identity[:])
-        nc.gpsimd.memset(e_c[:, LANES * SLOTS :], 0.0)
         grad = {}
 
         def clear(j, tag):
@@ -78,23 +77,17 @@ def tile_attend_gcbow_ns_pl_kernel(tc, eT, wT, ts, ux, y, coffs, posnoffs, sloto
         def load_w(t, u):
             nc.sync.dma_start(w_part[t][u][:], w_rows[:, t, halves[u]])
 
-        nc.sync.dma_start(ctx_list[:], coffs)
-        nc.sync.dma_start(e_lane[0], e_rows[:, 0, :])
-        nc.sync.dma_start(e_lane[1], e_rows[:, 1, :])
-        nc.sync.dma_start(slot_list[:], slotoffs)
         nc.sync.dma_start(idx_list[:], offs)
-        for t in range(2):
+        nc.sync.dma_start(e_lane[0], e_rows[:, 0, :])
+        nc.sync.dma_start(ctx_list[:], coffs)
+        nc.sync.dma_start(slot_list[:], slotoffs)
+        for t in range(LANES):
             load_w(t, 0)
             load_w(t, 1)
-        nc.sync.dma_start(e_lane[2], e_rows[:, 2, :])
-        nc.sync.dma_start(ts_table[0:1, :], ts[0:1, :])
-        load_w(2, 0)
-        load_w(2, 1)
-        nc.sync.dma_start(e_lane[3], e_rows[:, 3, :])
-        load_w(3, 0)
+            if t + 1 < LANES:
+                nc.sync.dma_start(e_lane[t + 1], e_rows[:, t + 1, :])
         nc.sync.dma_start(ux_col[:].rearrange("p (u q) -> p u q", q=2), ux_rows)
         nc.sync.dma_start(y_half[0][:], y_rows[:, 0, :, :])
-        load_w(3, 1)
         nc.sync.dma_start(y_half[1][:], y_rows[:, 1, :, :])
         nc.sync.dma_start(posn_list[:], posnoffs)
 
@@ -112,23 +105,28 @@ def tile_attend_gcbow_ns_pl_kernel(tc, eT, wT, ts, ux, y, coffs, posnoffs, sloto
         def dealt(row):
             return row.rearrange("p (r n a) -> p n r a", r=LANES, a=BLOCK_ROWS)
 
-        def gather_context(t):
-            first = SLOTS * (LANES - 1 - t)
-            nc.vector.tensor_copy(e_c[:, first : first + SLOTS], e_lane[t].indirect(ctx_list[:]))
+        def gather_context(t, start, stop):
+            first = SLOTS * ((t - 1) % LANES)
+            nc.vector.tensor_copy(
+                e_c[:, first + start : first + stop], e_lane[t].indirect(ctx_list[:, start // 16 : stop // 16]))
 
-        def gather_pairs(t):
-            first = SLOTS * (LANES - 1 - t)
-            nc.vector.tensor_copy(pairs[:, t, :], e_c[:, first : first + WINDOW].indirect(slot_list[:]))
+        def gather_pairs(t, start, stop, window):
+            first = SLOTS * ((t - 1) % LANES)
+            nc.vector.tensor_copy(
+                pairs[:, t, start:stop], e_c[:, first : first + window].indirect(slot_list[:, start // 16 : stop // 16]))
 
-        gather_context(0)
-        gather_context(1)
-        gather_pairs(0)
-        gather_pairs(1)
-        gather_context(2)
         nc.vector.tensor_copy(ts_i[:], ts_table[:].indirect(idx_list[:]))
-        gather_pairs(2)
-        gather_context(3)
-        gather_pairs(3)
+        middle = SLOTS // 2
+        gather_context(0, 0, SLOTS)
+        gather_pairs(0, 0, middle, SLOTS)
+        gather_pairs(0, middle, SLOTS, SLOTS)
+        gather_context(1, 0, SLOTS)
+        for t in range(1, LANES - 1):
+            gather_pairs(t, 0, middle, SLOTS)
+            gather_context(t + 1, 0, middle)
+            gather_context(t + 1, middle, SLOTS)
+            gather_pairs(t, middle, SLOTS, WINDOW)
+        gather_pairs(LANES - 1, 0, SLOTS, WINDOW)
 
         w_bf = {}
 
@@ -137,20 +135,18 @@ def tile_attend_gcbow_ns_pl_kernel(tc, eT, wT, ts, ux, y, coffs, posnoffs, sloto
                 w_bf[t] = keep.tile([P, WORDS], BF16, name="w_bf%d" % t, tag="w_bf%d" % (t % 2), align_bytes=64)
             nc.scalar.copy(w_bf[t][:, halves[u]], w_part[t][u][:])
 
-        cast_w(0, 0)
         for t in range(LANES):
+            cast_w(t, 0)
             cast_w(t, 1)
-            if t + 1 < LANES:
-                cast_w(t + 1, 0)
             nc.scalar.activation(dealt(w_by_d[:, :, t]), w_bf[t][:].indirect(idx_list[:]), ACT.Copy)
 
         ts_dealt = keep.tile([P, OUT_SLOTS], F32, name="ts_dealt")
         nc.gpsimd.tensor_scalar(dealt(ts_dealt[:]), listed(ts_i[:]), 1.0, 0.0, ALU.mult, ALU.add)
-        ts_ps = ring_ps.tile([P, LANES, P], F32, name="ts_ps", tag="ring")
+        ts_ps = banks.tile([P, LANES, P], F32, name="ts_ps", tag="bank4")
         for r in range(LANES):
             nc.tensor.transpose(ts_ps[:, r, :], ts_dealt[:, P * r : P * (r + 1)], identity[:])
         ts_col = keep.tile([P, LANES], F32, name="ts_col", tag="w3_1", align_bytes=64)
-        nc.scalar.copy(ts_col[:], ts_ps[:, :, 0])
+        nc.scalar.copy(ts_col[:], ts_ps[:, :, P - 1])
 
         for u in range(2):
             for q in range(2):
@@ -159,7 +155,7 @@ def tile_attend_gcbow_ns_pl_kernel(tc, eT, wT, ts, ux, y, coffs, posnoffs, sloto
                     dealt(signed_ux[n][:]), listed(y_half[u][:, q, :]), minus_2ux[:, n : n + 1], ux_col[:, n : n + 1],
                     ALU.mult, ALU.add)
             for r0 in range(0, LANES, 2):
-                f_ps = ring_ps.tile([P, 2, 2, P], F32, name="f_ps", tag="ring")
+                f_ps = banks.tile([P, 2, 2, P], F32, name="f_ps", tag="bank%d" % (2 * u + r0 // 2))
                 for r in range(2):
                     for q in range(2):
                         nc.tensor.transpose(
@@ -171,10 +167,13 @@ def tile_attend_gcbow_ns_pl_kernel(tc, eT, wT, ts, ux, y, coffs, posnoffs, sloto
 
         w_words = w_by_d[:].rearrange("p c t -> p (c t)").bitcast(F32)
         w_ps = {}
-        for v in range(2):
-            w_ps[v] = lane_ps.tile([P, LANES, P], F32, name="w_ps%d" % v, tag="bank%d" % ORDER[2 + v])
+
+        def turn_w(v):
+            w_ps[v] = banks.tile([P, LANES, P], F32, name="w_ps%d" % v, tag="bank%d" % v)
             for r in range(LANES):
                 nc.tensor.transpose(w_ps[v][:, r, :], w_words[:, 2 * P * r + v : 2 * P * (r + 1) : 2], identity[:])
+
+        turn_w(0)
 
         def mx_tiles(name, width):
             codes = keep.tile([P, width], U32, name=name + "_codes", align_bytes=64)
@@ -206,12 +205,12 @@ def tile_attend_gcbow_ns_pl_kernel(tc, eT, wT, ts, ux, y, coffs, posnoffs, sloto
         sig = {}
 
         def score(c):
-            a_ps = ring_ps.tile([P, LANES, P], F32, name="a_ps", tag="ring")
+            a_ps = banks.tile([P, LANES, P], F32, name="a_ps", tag="bank%d" % (c + 1))
             for r in range(LANES):
                 nc.tensor.matmul_mx(
                     out=a_ps[:, r, :], lhsT=wd_mx[0][:, chunks[r]].bitcast(E4M3), lhsT_scale=wd_mx[1][:, chunks[r]],
                     rhs=s_mx[0][:, chunks[c]].bitcast(E4M3), rhs_scale=s_mx[1][:, chunks[c]], start=True, stop=True)
-            z = keep.tile([P, LANES, P], F32, name="z%d" % c, tag="z%d" % (c % 2), align_bytes=64)
+            z = keep.tile([P, LANES, P], F32, name="z%d" % c, align_bytes=64)
             nc.vector.tensor_tensor(z[:], a_ps[:], factor[c // 2][:, :, chunks[c % 2]], ALU.mult)
             tag = "w%d_1" % c if c + 1 < LANES else "sig_last"
             sig[c] = keep.tile([P, LANES, P], F32, name="sig%d" % c, tag=tag, align_bytes=64)
@@ -231,30 +230,31 @@ def tile_attend_gcbow_ns_pl_kernel(tc, eT, wT, ts, ux, y, coffs, posnoffs, sloto
         score(0)
         quantize_s(3)
         score(1)
-        loss_gradient(0)
         score(2)
-        loss_gradient(1)
         score(3)
+        turn_w(1)
 
         w_first = keep.tile([P, P, LANES], BF16, name="w_first", tag="w3_1", align_bytes=64)
-        w_rest = keep.tile([P, LANES - 1, P, LANES], BF16, name="w_rest", tag="z1", align_bytes=64)
+        w_rest = keep.tile([P, LANES - 1, P, LANES], BF16, name="w_rest", tag="z3", align_bytes=64)
         w_by_i = {}
         for n, t in enumerate(ORDER):
             w_by_i[t] = w_first[:] if n == 0 else w_rest[:, n - 1, :, :]
             turned = w_ps[t // 2][:].rearrange("s r p -> s (r p)").bitcast(BF16).rearrange("s (r p e) -> s p r e", r=LANES, e=2)
             nc.scalar.copy(w_by_i[t], turned[:, :, :, t % 2])
-        quantize(wi_mx, chunks[ORDER[0]], w_by_i[ORDER[0]], E4M3)
+        loss_gradient(0)
+        loss_gradient(1)
         loss_gradient(2)
         quantize(g_mx, slice(0, 2 * P), g_bf[:, 0 : 2 * P, :], E5M2)
         loss_gradient(3)
         quantize(g_mx, chunks[2], g_bf[:, chunks[2], :], E5M2)
+        quantize(wi_mx, chunks[ORDER[0]], w_by_i[ORDER[0]], E4M3)
         quantize(g_mx, chunks[3], g_bf[:, chunks[3], :], E5M2)
         for j in ORDER[1:]:
             quantize(wi_mx, chunks[j], w_by_i[j], E4M3)
 
         dh_ps = {}
-        for j in ORDER:
-            dh_ps[j] = lane_ps.tile([P, POS], F32, name="dh_ps%d" % j, tag="bank%d" % j)
+        for n, j in enumerate(ORDER):
+            dh_ps[j] = banks.tile([P, POS], F32, name="dh_ps%d" % j, tag="bank%d" % (5, 6, 7, 2)[n])
             nc.tensor.matmul_mx(
                 out=dh_ps[j][:], lhsT=wi_mx[0][:, chunks[j]].bitcast(E4M3), lhsT_scale=wi_mx[1][:, chunks[j]],
                 rhs=g_mx[0][:].bitcast(E5M2), rhs_scale=g_mx[1][:], start=True, stop=True)
@@ -290,15 +290,17 @@ def tile_attend_gcbow_ns_pl_kernel(tc, eT, wT, ts, ux, y, coffs, posnoffs, sloto
         for cols in pieces[half:]:
             nc.scalar.copy(out_bf[:, cols, last], grad[last][:, cols])
         nc.vector.tensor_copy(out_bf[:, pieces[0], last], grad[last][:, pieces[0]])
+        stored = 0
         for n, cols in enumerate(pieces):
             if n + 1 < half:
                 nc.vector.tensor_copy(out_bf[:, pieces[n + 1], last], grad[last][:, pieces[n + 1]])
             nc.vector.quantize_mx(
                 out=out_codes[:, cols].bitcast(E4M3), scales=out_scales[4 * (n // 2) :, pieces[n % 2]],
                 in_=out_bf[:, cols, :].rearrange("p c l -> p (c l)"))
-            if n % 2 == 1:
-                quarter = slice(pieces[n - 1].start, cols.stop)
-                nc.sync.dma_start(words_hbm[:, quarter], out_codes[:, quarter].bitcast(I32))
+            if n % 2 == 0 and n > 0 or n + 1 == len(pieces):
+                done = slice(stored, cols.stop)
+                nc.sync.dma_start(words_hbm[:, done], out_codes[:, done].bitcast(I32))
+                stored = cols.stop
         scales_hbm = out_2[0].bitcast(I32).rearrange("f (a c) -> a f c", a=4)
         for group in range(4):
             nc.scalar.dma_start(

@@ -46,9 +46,8 @@ def tile_attend_gcbow_ns_pl_kernel(tc, eT, wT, ts, ux, y, coffs, posnoffs, sloto
         ux_rows = ux.rearrange("(u p q) o -> p u (q o)", p=P, q=2)
         e_lane = [keep.tile([P, WORDS], F32, name="e_lane%d" % t)[:] for t in range(LANES)]
         halves = [slice(0, WORDS // 2), slice(WORDS // 2, WORDS)]
-        w_part = [
-            [keep.tile([P, WORDS // 2], F32, name="w%d_%d" % (t, u), tag="w%d_%d" % (t, u), align_bytes=64) for u in range(2)]
-            for t in range(LANES)]
+        w_lane = [keep.tile([P, WORDS], F32, name="w%d" % t, align_bytes=64) for t in range(LANES - 1)]
+        w_last = [keep.tile([P, WORDS // 2], F32, name="w3_%d" % u, align_bytes=64) for u in range(2)]
         ts_table = keep.tile([P, WORDS], F32, name="ts_table")
         y_half = [keep.tile([P, 2, OUT_SLOTS], F32, name="y_half%d" % u, align_bytes=64) for u in range(2)]
         ux_col = keep.tile([P, LANES], F32, name="ux_col")
@@ -57,12 +56,11 @@ def tile_attend_gcbow_ns_pl_kernel(tc, eT, wT, ts, ux, y, coffs, posnoffs, sloto
         e_c = keep.tile([P, LANES * SLOTS], F32, name="e_c")
         dh = keep.tile([P, (LANES - 1) * POS + WINDOW], F32, name="dh")
 
-        nc.scalar.dma_start(ts_table[P - 1 : P, :], ts[0:1, :])
+        nc.vector.memset(ts_table[0 : P - 1, :], 0.0)
         warm = keep.tile([P, 2], F32, name="warm")
         nc.vector.memset(warm[:, 0:1], 0.0)
         nc.scalar.activation(warm[:, 1:2], warm[:, 0:1], ACT.Sigmoid)
 
-        nc.gpsimd.memset(ts_table[0 : P - 1, :], 0.0)
         make_identity(nc, identity[:])
         grad = {}
 
@@ -74,18 +72,16 @@ def tile_attend_gcbow_ns_pl_kernel(tc, eT, wT, ts, ux, y, coffs, posnoffs, sloto
             clear(j, "window%d" % j)
         nc.gpsimd.memset(dh[:, LANES * POS :], 0.0)
 
-        def load_w(t, u):
-            nc.sync.dma_start(w_part[t][u][:], w_rows[:, t, halves[u]])
-
+        nc.sync.dma_start(ts_table[P - 1 : P, :], ts[0:1, :])
         nc.sync.dma_start(idx_list[:], offs)
         nc.sync.dma_start(e_lane[0], e_rows[:, 0, :])
         nc.sync.dma_start(ctx_list[:], coffs)
         nc.sync.dma_start(slot_list[:], slotoffs)
-        for t in range(LANES):
-            load_w(t, 0)
-            load_w(t, 1)
-            if t + 1 < LANES:
-                nc.sync.dma_start(e_lane[t + 1], e_rows[:, t + 1, :])
+        for t in range(LANES - 1):
+            nc.sync.dma_start(w_lane[t][:], w_rows[:, t, :])
+            nc.sync.dma_start(e_lane[t + 1], e_rows[:, t + 1, :])
+        for u in range(2):
+            nc.sync.dma_start(w_last[u][:], w_rows[:, LANES - 1, halves[u]])
         nc.sync.dma_start(ux_col[:].rearrange("p (u q) -> p u q", q=2), ux_rows)
         nc.sync.dma_start(y_half[0][:], y_rows[:, 0, :, :])
         nc.sync.dma_start(y_half[1][:], y_rows[:, 1, :, :])
@@ -130,14 +126,13 @@ def tile_attend_gcbow_ns_pl_kernel(tc, eT, wT, ts, ux, y, coffs, posnoffs, sloto
 
         w_bf = {}
 
-        def cast_w(t, u):
-            if u == 0:
-                w_bf[t] = keep.tile([P, WORDS], BF16, name="w_bf%d" % t, tag="w_bf%d" % (t % 2), align_bytes=64)
-            nc.scalar.copy(w_bf[t][:, halves[u]], w_part[t][u][:])
-
         for t in range(LANES):
-            cast_w(t, 0)
-            cast_w(t, 1)
+            w_bf[t] = keep.tile([P, WORDS], BF16, name="w_bf%d" % t, tag="w_bf%d" % (t % 2), align_bytes=64)
+            if t + 1 < LANES:
+                nc.scalar.copy(w_bf[t][:], w_lane[t][:])
+            else:
+                for u in range(2):
+                    nc.scalar.copy(w_bf[t][:, halves[u]], w_last[u][:])
             nc.scalar.activation(dealt(w_by_d[:, :, t]), w_bf[t][:].indirect(idx_list[:]), ACT.Copy)
 
         ts_dealt = keep.tile([P, OUT_SLOTS], F32, name="ts_dealt")
@@ -151,9 +146,15 @@ def tile_attend_gcbow_ns_pl_kernel(tc, eT, wT, ts, ux, y, coffs, posnoffs, sloto
         for u in range(2):
             for q in range(2):
                 n = 2 * u + q
-                nc.gpsimd.tensor_scalar(
-                    dealt(signed_ux[n][:]), listed(y_half[u][:, q, :]), minus_2ux[:, n : n + 1], ux_col[:, n : n + 1],
-                    ALU.mult, ALU.add)
+                if u == 0:
+                    nc.gpsimd.tensor_scalar(
+                        dealt(signed_ux[n][:]), listed(y_half[u][:, q, :]), minus_2ux[:, n : n + 1], ux_col[:, n : n + 1],
+                        ALU.mult, ALU.add)
+                else:
+                    nc.scalar.activation(
+                        dealt(signed_ux[n][:]), listed(y_half[u][:, q, :]), ACT.Identity,
+                        scale=minus_2ux[:, n : n + 1], bias=ux_col[:, n : n + 1])
+        for u in range(2):
             for r0 in range(0, LANES, 2):
                 f_ps = banks.tile([P, 2, 2, P], F32, name="f_ps", tag="bank%d" % (2 * u + r0 // 2))
                 for r in range(2):
@@ -212,8 +213,7 @@ def tile_attend_gcbow_ns_pl_kernel(tc, eT, wT, ts, ux, y, coffs, posnoffs, sloto
                     rhs=s_mx[0][:, chunks[c]].bitcast(E4M3), rhs_scale=s_mx[1][:, chunks[c]], start=True, stop=True)
             z = keep.tile([P, LANES, P], F32, name="z%d" % c, align_bytes=64)
             nc.vector.tensor_tensor(z[:], a_ps[:], factor[c // 2][:, :, chunks[c % 2]], ALU.mult)
-            tag = "w%d_1" % c if c + 1 < LANES else "sig_last"
-            sig[c] = keep.tile([P, LANES, P], F32, name="sig%d" % c, tag=tag, align_bytes=64)
+            sig[c] = keep.tile([P, LANES, P], F32, name="sig%d" % c, align_bytes=64)
             nc.scalar.activation(sig[c][:], z[:], ACT.Sigmoid, scale=0.5)
 
         def loss_gradient(c):
@@ -266,7 +266,7 @@ def tile_attend_gcbow_ns_pl_kernel(tc, eT, wT, ts, ux, y, coffs, posnoffs, sloto
         de = {}
 
         def look_up(j):
-            de[j] = keep.tile([P, SLOTS], F32, name="de%d" % j, tag="w%d_0" % j, align_bytes=64)
+            de[j] = keep.tile([P, SLOTS], F32, name="de%d" % j, tag="w%d" % j if j + 1 < LANES else "w3_0", align_bytes=64)
             nc.vector.tensor_copy(de[j][:], dh[:, dh_first[j] : dh_first[j] + WINDOW].indirect(posn_list[:]))
 
         def place(j):

@@ -186,7 +186,10 @@ def tile_attend_gcbow_ns_pl_kernel(tc, eT, wT, ts, ux, y, coffs, posnoffs, sloto
                 out=operand[0][:, cols].bitcast(fmt), scales=operand[1][:, cols], in_=grouped.rearrange("p c l -> p (c l)"))
 
         s_mx = mx_tiles("s", POS)
-        g_mx = mx_tiles("g", POS)
+        g_wide = mx_tiles("g", POS + POS // 2)
+        g_mx = [part[:, POS // 2 :] for part in g_wide]
+        nc.gpsimd.memset(g_wide[0][:, 0 : POS // 2], 0)
+        nc.gpsimd.memset(g_wide[1][:, 0 : POS // 2], 0)
         wd_mx = mx_tiles("wd", OUT_SLOTS)
         wi_mx = mx_tiles("wi", LANES * P)
         s_bf = keep.tile([P, POS, LANES], BF16, name="s_bf", tag="w_bf1", align_bytes=64)
@@ -212,15 +215,22 @@ def tile_attend_gcbow_ns_pl_kernel(tc, eT, wT, ts, ux, y, coffs, posnoffs, sloto
                     out=a_ps[:, r, :], lhsT=wd_mx[0][:, chunks[r]].bitcast(E4M3), lhsT_scale=wd_mx[1][:, chunks[r]],
                     rhs=s_mx[0][:, chunks[c]].bitcast(E4M3), rhs_scale=s_mx[1][:, chunks[c]], start=True, stop=True)
             z = keep.tile([P, LANES, P], F32, name="z%d" % c, align_bytes=64)
-            nc.vector.tensor_tensor(z[:], a_ps[:], factor[c // 2][:, :, chunks[c % 2]], ALU.mult)
             sig[c] = keep.tile([P, LANES, P], F32, name="sig%d" % c, align_bytes=64)
-            nc.scalar.activation(sig[c][:], z[:], ACT.Sigmoid, scale=0.5)
+            step = P // 2 if c == 0 else P
+            for x in range(0, P, step):
+                cols = slice(x, x + step)
+                nc.vector.tensor_tensor(z[:, :, cols], a_ps[:, :, cols], factor[c // 2][:, :, chunks[c % 2]][:, :, cols], ALU.mult)
+                nc.scalar.activation(sig[c][:, :, cols], z[:, :, cols], ACT.Sigmoid, scale=0.5)
 
         def loss_gradient(c):
-            nc.vector.tensor_tensor(
-                g_bf[:, chunks[c], :].rearrange("s (k i) r -> s k r i", i=LINE),
-                sig[c][:].rearrange("s r (k i) -> s k r i", i=LINE),
-                factor[c // 2][:, :, chunks[c % 2]].rearrange("s r (k i) -> s k r i", i=LINE), ALU.mult)
+            engine = nc.gpsimd if c == 0 else nc.vector
+            step = P // 2 if c == 0 else P
+            for x in range(0, P, step):
+                cols = slice(x, x + step)
+                engine.tensor_tensor(
+                    g_bf[:, chunks[c], :][:, cols, :].rearrange("s (k i) r -> s k r i", i=LINE),
+                    sig[c][:, :, cols].rearrange("s r (k i) -> s k r i", i=LINE),
+                    factor[c // 2][:, :, chunks[c % 2]][:, :, cols].rearrange("s r (k i) -> s k r i", i=LINE), ALU.mult)
 
         quantize(wd_mx, slice(0, OUT_SLOTS), w_by_d[:], E4M3)
         pair_sum(0)
@@ -243,24 +253,32 @@ def tile_attend_gcbow_ns_pl_kernel(tc, eT, wT, ts, ux, y, coffs, posnoffs, sloto
             nc.scalar.copy(w_by_i[t], turned[:, :, :, t % 2])
         loss_gradient(0)
         loss_gradient(1)
+        quantize(wi_mx, chunks[ORDER[0]], w_by_i[ORDER[0]], E4M3)
         loss_gradient(2)
         quantize(g_mx, slice(0, 2 * P), g_bf[:, 0 : 2 * P, :], E5M2)
+        dh_first = {j: POS * (LANES - 1 - n) for n, j in enumerate(ORDER)}
+
+        def multiply_dh(j, bank, first):
+            dh_ps = banks.tile([P, POS], F32, name="dh_ps", tag="bank%d" % bank)
+            nc.tensor.matmul_mx(
+                out=dh_ps[:], lhsT=wi_mx[0][:, chunks[j]].bitcast(E4M3), lhsT_scale=wi_mx[1][:, chunks[j]],
+                rhs=g_wide[0][:, first : first + POS].bitcast(E5M2), rhs_scale=g_wide[1][:, first : first + POS], start=True, stop=True)
+            return dh_ps
+
+        def halve_dh(j, columns, start, stop):
+            nc.scalar.activation(dh[:, dh_first[j] + start : dh_first[j] + stop], columns, ACT.Copy, scale=0.5)
+
+        halve_dh(ORDER[0], multiply_dh(ORDER[0], 3, 0)[:, POS // 2 :], 0, POS // 2)
         loss_gradient(3)
         quantize(g_mx, chunks[2], g_bf[:, chunks[2], :], E5M2)
-        quantize(wi_mx, chunks[ORDER[0]], w_by_i[ORDER[0]], E4M3)
+        quantize(wi_mx, chunks[ORDER[1]], w_by_i[ORDER[1]], E4M3)
         quantize(g_mx, chunks[3], g_bf[:, chunks[3], :], E5M2)
-        for j in ORDER[1:]:
+        for j in ORDER[2:]:
             quantize(wi_mx, chunks[j], w_by_i[j], E4M3)
 
-        dh_ps = {}
         for n, j in enumerate(ORDER):
-            dh_ps[j] = banks.tile([P, POS], F32, name="dh_ps%d" % j, tag="bank%d" % (5, 6, 7, 2)[n])
-            nc.tensor.matmul_mx(
-                out=dh_ps[j][:], lhsT=wi_mx[0][:, chunks[j]].bitcast(E4M3), lhsT_scale=wi_mx[1][:, chunks[j]],
-                rhs=g_mx[0][:].bitcast(E5M2), rhs_scale=g_mx[1][:], start=True, stop=True)
-        dh_first = {j: POS * (LANES - 1 - n) for n, j in enumerate(ORDER)}
-        for j in ORDER:
-            nc.scalar.activation(dh[:, dh_first[j] : dh_first[j] + POS], dh_ps[j][:], ACT.Copy, scale=0.5)
+            start = POS // 2 if n == 0 else 0
+            halve_dh(j, multiply_dh(j, (5, 6, 7, 2)[n], POS // 2)[:, start:], start, POS)
 
         out_bf = keep.tile([P, WORDS, LANES], BF16, name="out_bf", tag="pairs_then_out", align_bytes=64)
         de = {}

@@ -124,6 +124,14 @@ def tile_attend_gcbow_ns_pl_kernel(tc, eT, wT, ts, ux, y, coffs, posnoffs, sloto
             gather_pairs(t, middle, SLOTS, WINDOW)
         gather_pairs(LANES - 1, 0, SLOTS, WINDOW)
 
+        w_words = w_by_d[:].rearrange("p c t -> p (c t)").bitcast(F32)
+        w_ps = {}
+
+        def turn_w(v):
+            w_ps[v] = banks.tile([P, LANES, P], F32, name="w_ps%d" % v, tag="bank%d" % (5, 3)[v])
+            for r in range(LANES):
+                nc.tensor.transpose(w_ps[v][:, r, :], w_words[:, 2 * P * r + v : 2 * P * (r + 1) : 2], identity[:])
+
         w_bf = {}
 
         for t in range(LANES):
@@ -134,6 +142,8 @@ def tile_attend_gcbow_ns_pl_kernel(tc, eT, wT, ts, ux, y, coffs, posnoffs, sloto
                 for u in range(2):
                     nc.scalar.copy(w_bf[t][:, halves[u]], w_last[u][:])
             nc.scalar.activation(dealt(w_by_d[:, :, t]), w_bf[t][:].indirect(idx_list[:]), ACT.Copy)
+            if t == 1:
+                turn_w(0)
 
         ts_dealt = keep.tile([P, OUT_SLOTS], F32, name="ts_dealt")
         nc.gpsimd.tensor_scalar(dealt(ts_dealt[:]), listed(ts_i[:]), 1.0, 0.0, ALU.mult, ALU.add)
@@ -165,16 +175,6 @@ def tile_attend_gcbow_ns_pl_kernel(tc, eT, wT, ts, ux, y, coffs, posnoffs, sloto
                     nc.scalar.activation(
                         factor[u][:, r0 + r, :].rearrange("s (p q) -> s p q", q=2),
                         f_ps[:, r, :, :].rearrange("s q p -> s p q"), ACT.Copy, scale=ts_col[:, r0 + r : r0 + r + 1])
-
-        w_words = w_by_d[:].rearrange("p c t -> p (c t)").bitcast(F32)
-        w_ps = {}
-
-        def turn_w(v):
-            w_ps[v] = banks.tile([P, LANES, P], F32, name="w_ps%d" % v, tag="bank%d" % v)
-            for r in range(LANES):
-                nc.tensor.transpose(w_ps[v][:, r, :], w_words[:, 2 * P * r + v : 2 * P * (r + 1) : 2], identity[:])
-
-        turn_w(0)
 
         def mx_tiles(name, width):
             codes = keep.tile([P, width], U32, name=name + "_codes", align_bytes=64)
@@ -209,7 +209,7 @@ def tile_attend_gcbow_ns_pl_kernel(tc, eT, wT, ts, ux, y, coffs, posnoffs, sloto
         sig = {}
 
         def score(c):
-            a_ps = banks.tile([P, LANES, P], F32, name="a_ps", tag="bank%d" % (c + 1))
+            a_ps = banks.tile([P, LANES, P], F32, name="a_ps", tag="bank%d" % (0, 1, 4, 2)[c])
             for r in range(LANES):
                 nc.tensor.matmul_mx(
                     out=a_ps[:, r, :], lhsT=wd_mx[0][:, chunks[r]].bitcast(E4M3), lhsT_scale=wd_mx[1][:, chunks[r]],
@@ -268,7 +268,7 @@ def tile_attend_gcbow_ns_pl_kernel(tc, eT, wT, ts, ux, y, coffs, posnoffs, sloto
         def halve_dh(j, columns, start, stop):
             nc.scalar.activation(dh[:, dh_first[j] + start : dh_first[j] + stop], columns, ACT.Copy, scale=0.5)
 
-        halve_dh(ORDER[0], multiply_dh(ORDER[0], 3, 0)[:, POS // 2 :], 0, POS // 2)
+        halve_dh(ORDER[0], multiply_dh(ORDER[0], 4, 0)[:, POS // 2 :], 0, POS // 2)
         loss_gradient(3)
         quantize(g_mx, chunks[2], g_bf[:, chunks[2], :], E5M2)
         quantize(wi_mx, chunks[ORDER[1]], w_by_i[ORDER[1]], E4M3)
@@ -278,7 +278,7 @@ def tile_attend_gcbow_ns_pl_kernel(tc, eT, wT, ts, ux, y, coffs, posnoffs, sloto
 
         for n, j in enumerate(ORDER):
             start = POS // 2 if n == 0 else 0
-            halve_dh(j, multiply_dh(j, (5, 6, 7, 2)[n], POS // 2)[:, start:], start, POS)
+            halve_dh(j, multiply_dh(j, (6, 7, 0, 1)[n], POS // 2)[:, start:], start, POS)
 
         out_bf = keep.tile([P, WORDS, LANES], BF16, name="out_bf", tag="pairs_then_out", align_bytes=64)
         de = {}

@@ -46,8 +46,9 @@ def tile_attend_gcbow_ns_pl_kernel(tc, eT, wT, ts, ux, y, coffs, posnoffs, sloto
         ux_rows = ux.rearrange("(u p q) o -> p u (q o)", p=P, q=2)
         e_lane = [keep.tile([P, WORDS], F32, name="e_lane%d" % t)[:] for t in range(LANES)]
         halves = [slice(0, WORDS // 2), slice(WORDS // 2, WORDS)]
-        w_lane = [keep.tile([P, WORDS], F32, name="w%d" % t, align_bytes=64) for t in range(LANES - 1)]
-        w_last = [keep.tile([P, WORDS // 2], F32, name="w3_%d" % u, align_bytes=64) for u in range(2)]
+        w_part = [
+            [keep.tile([P, WORDS // 2], F32, name="w%d_%d" % (t, u), align_bytes=64) for u in range(2)]
+            for t in range(LANES)]
         ts_table = keep.tile([P, WORDS], F32, name="ts_table")
         y_half = [keep.tile([P, 2, OUT_SLOTS], F32, name="y_half%d" % u, align_bytes=64) for u in range(2)]
         ux_col = keep.tile([P, LANES], F32, name="ux_col")
@@ -77,17 +78,15 @@ def tile_attend_gcbow_ns_pl_kernel(tc, eT, wT, ts, ux, y, coffs, posnoffs, sloto
         nc.sync.dma_start(e_lane[0], e_rows[:, 0, :])
         nc.sync.dma_start(ctx_list[:], coffs)
         nc.sync.dma_start(slot_list[:], slotoffs)
-        for t in range(LANES - 1):
-            nc.sync.dma_start(w_lane[t][:], w_rows[:, t, :])
-            nc.sync.dma_start(e_lane[t + 1], e_rows[:, t + 1, :])
-        for u in range(2):
-            nc.sync.dma_start(w_last[u][:], w_rows[:, LANES - 1, halves[u]])
+        for t in range(LANES):
+            for u in range(2):
+                nc.sync.dma_start(w_part[t][u][:], w_rows[:, t, halves[u]])
+            if t + 1 < LANES:
+                nc.sync.dma_start(e_lane[t + 1], e_rows[:, t + 1, :])
         nc.sync.dma_start(ux_col[:].rearrange("p (u q) -> p u q", q=2), ux_rows)
         nc.sync.dma_start(y_half[0][:], y_rows[:, 0, :, :])
         nc.sync.dma_start(y_half[1][:], y_rows[:, 1, :, :])
         nc.sync.dma_start(posn_list[:], posnoffs)
-
-        nc.gpsimd.tensor_scalar(minus_2ux[:], ux_col[:], -2.0, 0.0, ALU.mult, ALU.add)
 
         pairs = keep.tile([P, LANES, SLOTS], F32, name="pairs", tag="pairs_then_out", align_bytes=64)
         w_by_d = keep.tile([P, OUT_SLOTS, LANES], BF16, name="w_by_d", align_bytes=64)
@@ -136,17 +135,15 @@ def tile_attend_gcbow_ns_pl_kernel(tc, eT, wT, ts, ux, y, coffs, posnoffs, sloto
 
         for t in range(LANES):
             w_bf[t] = keep.tile([P, WORDS], BF16, name="w_bf%d" % t, tag="w_bf%d" % (t % 2), align_bytes=64)
-            if t + 1 < LANES:
-                nc.scalar.copy(w_bf[t][:], w_lane[t][:])
-            else:
-                for u in range(2):
-                    nc.scalar.copy(w_bf[t][:, halves[u]], w_last[u][:])
+            for u in range(2):
+                nc.scalar.copy(w_bf[t][:, halves[u]], w_part[t][u][:])
             nc.scalar.activation(dealt(w_by_d[:, :, t]), w_bf[t][:].indirect(idx_list[:]), ACT.Copy)
             if t == 1:
                 turn_w(0)
 
         ts_dealt = keep.tile([P, OUT_SLOTS], F32, name="ts_dealt")
-        nc.gpsimd.tensor_scalar(dealt(ts_dealt[:]), listed(ts_i[:]), 1.0, 0.0, ALU.mult, ALU.add)
+        nc.scalar.copy(dealt(ts_dealt[:]), listed(ts_i[:]))
+        nc.scalar.activation(minus_2ux[:], ux_col[:], ACT.Copy, scale=-2.0)
         ts_ps = banks.tile([P, LANES, P], F32, name="ts_ps", tag="bank4")
         for r in range(LANES):
             nc.tensor.transpose(ts_ps[:, r, :], ts_dealt[:, P * r : P * (r + 1)], identity[:])
@@ -156,14 +153,9 @@ def tile_attend_gcbow_ns_pl_kernel(tc, eT, wT, ts, ux, y, coffs, posnoffs, sloto
         for u in range(2):
             for q in range(2):
                 n = 2 * u + q
-                if u == 0:
-                    nc.gpsimd.tensor_scalar(
-                        dealt(signed_ux[n][:]), listed(y_half[u][:, q, :]), minus_2ux[:, n : n + 1], ux_col[:, n : n + 1],
-                        ALU.mult, ALU.add)
-                else:
-                    nc.scalar.activation(
-                        dealt(signed_ux[n][:]), listed(y_half[u][:, q, :]), ACT.Identity,
-                        scale=minus_2ux[:, n : n + 1], bias=ux_col[:, n : n + 1])
+                nc.scalar.activation(
+                    dealt(signed_ux[n][:]), listed(y_half[u][:, q, :]), ACT.Identity,
+                    scale=minus_2ux[:, n : n + 1], bias=ux_col[:, n : n + 1])
         for u in range(2):
             for r0 in range(0, LANES, 2):
                 f_ps = banks.tile([P, 2, 2, P], F32, name="f_ps", tag="bank%d" % (2 * u + r0 // 2))
@@ -284,7 +276,7 @@ def tile_attend_gcbow_ns_pl_kernel(tc, eT, wT, ts, ux, y, coffs, posnoffs, sloto
         de = {}
 
         def look_up(j):
-            de[j] = keep.tile([P, SLOTS], F32, name="de%d" % j, tag="w%d" % j if j + 1 < LANES else "w3_0", align_bytes=64)
+            de[j] = keep.tile([P, SLOTS], F32, name="de%d" % j, tag="w%d_0" % j, align_bytes=64)
             nc.vector.tensor_copy(de[j][:], dh[:, dh_first[j] : dh_first[j] + WINDOW].indirect(posn_list[:]))
 
         def place(j):

@@ -26,7 +26,9 @@ BLOCK_ROWS = 8
 WINDOW = 1376
 LINE = 4
 PIECE = 256
-ORDER = (1, 3, 2, 0)
+ORDER = (2, 3, 1, 0)
+CUTS = (0, 384, 768, 1024)
+SPLIT = 1024
 
 
 def tile_attend_gcbow_ns_pl_kernel(tc, eT, wT, ts, ux, y, coffs, posnoffs, slotoffs, offs, out_0, out_1, out_2):
@@ -54,8 +56,8 @@ def tile_attend_gcbow_ns_pl_kernel(tc, eT, wT, ts, ux, y, coffs, posnoffs, sloto
         ux_col = keep.tile([P, LANES], F32, name="ux_col")
         minus_2ux = keep.tile([P, LANES], F32, name="minus_2ux")
         identity = keep.tile([P, P], F32, name="identity")
-        e_c = keep.tile([P, LANES * SLOTS], F32, name="e_c")
-        dh = keep.tile([P, (LANES - 1) * POS + WINDOW], F32, name="dh")
+        e_c = keep.tile([P, LANES * SLOTS], F32, name="e_c", tag="e_c_then_lanes", align_bytes=64)
+        dh = [keep.tile([P, POS], F32, name="dh%d" % t, align_bytes=64) for t in range(LANES)]
 
         nc.vector.memset(ts_table[0 : P - 1, :], 0.0)
         warm = keep.tile([P, 2], F32, name="warm")
@@ -69,9 +71,8 @@ def tile_attend_gcbow_ns_pl_kernel(tc, eT, wT, ts, ux, y, coffs, posnoffs, sloto
             grad[j] = keep.tile([P, WORDS], F32, name="grad%d" % j, tag=tag, align_bytes=64)
             nc.gpsimd.memset(grad[j][:], 0.0)
 
-        for j in ORDER[:-1]:
+        for j in ORDER:
             clear(j, "window%d" % j)
-        nc.gpsimd.memset(dh[:, LANES * POS :], 0.0)
 
         nc.sync.dma_start(ts_table[P - 1 : P, :], ts[0:1, :])
         nc.sync.dma_start(idx_list[:], offs)
@@ -248,7 +249,6 @@ def tile_attend_gcbow_ns_pl_kernel(tc, eT, wT, ts, ux, y, coffs, posnoffs, sloto
         quantize(wi_mx, chunks[ORDER[0]], w_by_i[ORDER[0]], E4M3)
         loss_gradient(2)
         quantize(g_mx, slice(0, 2 * P), g_bf[:, 0 : 2 * P, :], E5M2)
-        dh_first = {j: POS * (LANES - 1 - n) for n, j in enumerate(ORDER)}
 
         def multiply_dh(j, bank, first):
             dh_ps = banks.tile([P, POS], F32, name="dh_ps", tag="bank%d" % bank)
@@ -258,7 +258,7 @@ def tile_attend_gcbow_ns_pl_kernel(tc, eT, wT, ts, ux, y, coffs, posnoffs, sloto
             return dh_ps
 
         def halve_dh(j, columns, start, stop):
-            nc.scalar.activation(dh[:, dh_first[j] + start : dh_first[j] + stop], columns, ACT.Copy, scale=0.5)
+            nc.scalar.activation(dh[j][:, start:stop], columns, ACT.Copy, scale=0.5)
 
         halve_dh(ORDER[0], multiply_dh(ORDER[0], 4, 0)[:, POS // 2 :], 0, POS // 2)
         loss_gradient(3)
@@ -268,42 +268,73 @@ def tile_attend_gcbow_ns_pl_kernel(tc, eT, wT, ts, ux, y, coffs, posnoffs, sloto
         for j in ORDER[2:]:
             quantize(wi_mx, chunks[j], w_by_i[j], E4M3)
 
-        for n, j in enumerate(ORDER):
-            start = POS // 2 if n == 0 else 0
-            halve_dh(j, multiply_dh(j, (6, 7, 0, 1)[n], POS // 2)[:, start:], start, POS)
-
+        a, b, c, d = ORDER
+        dh_ps = {j: multiply_dh(j, (6, 7, 0, 1)[n], POS // 2) for n, j in enumerate(ORDER)}
         out_bf = keep.tile([P, WORDS, LANES], BF16, name="out_bf", tag="pairs_then_out", align_bytes=64)
-        de = {}
+        lanes_bf = keep.tile([P, LANES, WORDS], BF16, name="lanes_bf", tag="e_c_then_lanes", align_bytes=64)
+        de = {j: keep.tile([P, SLOTS], F32, name="de%d" % j, tag="w%d_0" % j, align_bytes=64) for j in ORDER}
 
-        def look_up(j):
-            de[j] = keep.tile([P, SLOTS], F32, name="de%d" % j, tag="w%d_0" % j, align_bytes=64)
-            nc.vector.tensor_copy(de[j][:], dh[:, dh_first[j] : dh_first[j] + WINDOW].indirect(posn_list[:]))
+        def on_scalar(out, in_):
+            nc.scalar.activation(out, in_, ACT.Copy)
 
-        def place(j):
-            nc.vector.tensor_copy(grad[j][:].indirect(ctx_list[:]), de[j][:])
-            nc.sync.dma_start(out_rows[:, j, :], grad[j][:])
+        on_vector = nc.vector.tensor_copy
 
-        look_up(ORDER[0])
-        for n, j in enumerate(ORDER[:-1]):
-            look_up(ORDER[n + 1])
-            place(j)
-            nc.scalar.copy(out_bf[:, :, j], grad[j][:])
-        last = ORDER[-1]
-        clear(last, "window%d" % ORDER[0])
-        place(last)
+        def look_up(move, j, n):
+            lo, hi = CUTS[n], CUTS[n + 1]
+            move(de[j][:, lo:hi], dh[j][:].indirect(posn_list[:, lo // 16 : hi // 16]))
+
+        def place(move, j, n):
+            lo, hi = CUTS[n], CUTS[n + 1]
+            move(grad[j][:].indirect(ctx_list[:, lo // 16 : hi // 16]), de[j][:, lo:hi])
+
+        def store(queue, j):
+            queue.dma_start(out_rows[:, j, :], grad[j][:])
+
+        def halve_on_vector(j):
+            nc.vector.tensor_scalar(dh[j][:], dh_ps[j][:], 0.5, None, ALU.mult)
+
+        halve_dh(a, dh_ps[a][:, POS // 2 :], POS // 2, POS)
+        halve_on_vector(b)
+        halve_on_vector(c)
+        for n in range(3):
+            look_up(on_scalar, a, n)
+            look_up(on_vector, b, n)
+        for n in range(3):
+            look_up(on_scalar, c, n)
+            place(on_vector, b, n)
+        store(nc.sync, b)
+        nc.gpsimd.tensor_scalar(lanes_bf[:, b, :], grad[b][:], 1.0, 0.0, ALU.mult, ALU.add)
+        for n in range(3):
+            place(on_scalar, a, n)
+        halve_dh(d, dh_ps[d][:], 0, POS)
+        store(nc.scalar, a)
+        nc.gpsimd.tensor_scalar(lanes_bf[:, a, :], grad[a][:], 1.0, 0.0, ALU.mult, ALU.add)
+        for n in range(3):
+            place(on_vector, c, n)
+            look_up(on_scalar, d, n)
+        store(nc.sync, c)
+        for n in range(3):
+            place(on_scalar, d, n)
+        store(nc.sync, d)
+        mine = slice(0, SPLIT)
+        theirs = slice(SPLIT, WORDS)
+        nc.vector.tensor_copy(lanes_bf[:, c, :], grad[c][:])
+        nc.vector.tensor_copy(out_bf[:, theirs, 2:4], lanes_bf[:, 2:4, theirs].rearrange("p t c -> p c t"))
+        nc.vector.tensor_copy(out_bf[:, mine, 1:4], lanes_bf[:, 1:4, mine].rearrange("p t c -> p c t"))
 
         out_codes = keep.tile([P, WORDS], U32, name="out_codes", align_bytes=64)
         out_scales = keep.tile([P, WORDS // 4], U8, name="out_scales", align_bytes=64)
         words_hbm = out_1[0].rearrange("p c l -> p (c l)").bitcast(I32)
         pieces = [slice(PIECE * n, PIECE * (n + 1)) for n in range(WORDS // PIECE)]
-        half = len(pieces) // 2
+        half = SPLIT // PIECE
         for cols in pieces[half:]:
-            nc.scalar.copy(out_bf[:, cols, last], grad[last][:, cols])
-        nc.vector.tensor_copy(out_bf[:, pieces[0], last], grad[last][:, pieces[0]])
+            nc.scalar.copy(lanes_bf[:, d, cols], grad[d][:, cols])
+            nc.scalar.copy(out_bf[:, cols, 0:2], lanes_bf[:, 0:2, cols].rearrange("p t c -> p c t"))
+        nc.vector.tensor_copy(out_bf[:, pieces[0], d], grad[d][:, pieces[0]])
         stored = 0
         for n, cols in enumerate(pieces):
             if n + 1 < half:
-                nc.vector.tensor_copy(out_bf[:, pieces[n + 1], last], grad[last][:, pieces[n + 1]])
+                nc.vector.tensor_copy(out_bf[:, pieces[n + 1], d], grad[d][:, pieces[n + 1]])
             nc.vector.quantize_mx(
                 out=out_codes[:, cols].bitcast(E4M3), scales=out_scales[4 * (n // 2) :, pieces[n % 2]],
                 in_=out_bf[:, cols, :].rearrange("p c l -> p (c l)"))

@@ -23,12 +23,12 @@ SLOTS = 1024
 POS = 512
 OUT_SLOTS = 512
 BLOCK_ROWS = 8
-WINDOW = 1376
+WINDOW = 1040
 LINE = 4
 PIECE = 256
-ORDER = (2, 3, 1, 0)
+ORDER = (0, 1, 2, 3)
 CUTS = (0, 384, 768, 1024)
-SPLIT = 1024
+SPLIT = 1280
 
 
 def tile_attend_gcbow_ns_pl_kernel(tc, eT, wT, ts, ux, y, coffs, posnoffs, slotoffs, offs, out_0, out_1, out_2):
@@ -46,18 +46,15 @@ def tile_attend_gcbow_ns_pl_kernel(tc, eT, wT, ts, ux, y, coffs, posnoffs, sloto
         out_rows = out_0.rearrange("(p t) c -> p t c", t=LANES)
         y_rows = y.rearrange("(u p q) i -> p u q i", p=P, q=2)
         ux_rows = ux.rearrange("(u p q) o -> p u (q o)", p=P, q=2)
-        e_lane = [keep.tile([P, WORDS], F32, name="e_lane%d" % t)[:] for t in range(LANES)]
-        halves = [slice(0, WORDS // 2), slice(WORDS // 2, WORDS)]
-        w_part = [
-            [keep.tile([P, WORDS // 2], F32, name="w%d_%d" % (t, u), align_bytes=64) for u in range(2)]
-            for t in range(LANES)]
+        e_lane = [keep.tile([P, WORDS], F32, name="e_lane%d" % t, align_bytes=64)[:] for t in range(LANES)]
+        w_lane = [keep.tile([P, WORDS], F32, name="w_lane%d" % t, align_bytes=64)[:] for t in range(LANES)]
         ts_table = keep.tile([P, WORDS], F32, name="ts_table")
         y_half = [keep.tile([P, 2, OUT_SLOTS], F32, name="y_half%d" % u, align_bytes=64) for u in range(2)]
         ux_col = keep.tile([P, LANES], F32, name="ux_col")
         minus_2ux = keep.tile([P, LANES], F32, name="minus_2ux")
         identity = keep.tile([P, P], F32, name="identity")
-        e_c = keep.tile([P, LANES * SLOTS], F32, name="e_c", tag="e_c_then_lanes", align_bytes=64)
-        dh = [keep.tile([P, POS], F32, name="dh%d" % t, align_bytes=64) for t in range(LANES)]
+        e_c = [keep.tile([P, SLOTS], F32, name="e_c%d" % t, align_bytes=64) for t in range(LANES)]
+        dh = [keep.tile([P, WINDOW], F32, name="dh%d" % t, align_bytes=64) for t in range(LANES)]
 
         nc.vector.memset(ts_table[0 : P - 1, :], 0.0)
         warm = keep.tile([P, 2], F32, name="warm")
@@ -73,18 +70,18 @@ def tile_attend_gcbow_ns_pl_kernel(tc, eT, wT, ts, ux, y, coffs, posnoffs, sloto
 
         for j in ORDER:
             clear(j, "window%d" % j)
+            nc.gpsimd.memset(dh[j][:, POS:], 0.0)
 
         nc.sync.dma_start(ts_table[P - 1 : P, :], ts[0:1, :])
         nc.sync.dma_start(idx_list[:], offs)
         nc.sync.dma_start(e_lane[0], e_rows[:, 0, :])
         nc.sync.dma_start(ctx_list[:], coffs)
         nc.sync.dma_start(slot_list[:], slotoffs)
-        for t in range(LANES):
-            for u in range(2):
-                nc.sync.dma_start(w_part[t][u][:], w_rows[:, t, halves[u]])
-            if t + 1 < LANES:
-                nc.sync.dma_start(e_lane[t + 1], e_rows[:, t + 1, :])
+        for t in range(1, LANES):
+            nc.sync.dma_start(e_lane[t], e_rows[:, t, :])
         nc.sync.dma_start(ux_col[:].rearrange("p (u q) -> p u q", q=2), ux_rows)
+        for t in range(LANES):
+            nc.sync.dma_start(w_lane[t], w_rows[:, t, :])
         nc.sync.dma_start(y_half[0][:], y_rows[:, 0, :, :])
         nc.sync.dma_start(y_half[1][:], y_rows[:, 1, :, :])
         nc.sync.dma_start(posn_list[:], posnoffs)
@@ -96,81 +93,97 @@ def tile_attend_gcbow_ns_pl_kernel(tc, eT, wT, ts, ux, y, coffs, posnoffs, sloto
         factor = [keep.tile([P, LANES, POS // 2], F32, name="factor%d" % u) for u in range(2)]
 
         def listed(row):
-            return row.rearrange("p (n r a) -> p n r a", r=LANES, a=BLOCK_ROWS)
+            return row.rearrange("p (k i r) -> p k r i", r=LANES, i=LINE)
 
         def dealt(row):
-            return row.rearrange("p (r n a) -> p n r a", r=LANES, a=BLOCK_ROWS)
+            return row.rearrange("p (r k i) -> p k r i", r=LANES, i=LINE)
 
-        def gather_context(t, start, stop):
-            first = SLOTS * ((t - 1) % LANES)
-            nc.vector.tensor_copy(
-                e_c[:, first + start : first + stop], e_lane[t].indirect(ctx_list[:, start // 16 : stop // 16]))
+        def on_scalar(out, in_):
+            nc.scalar.activation(out, in_, ACT.Copy)
 
-        def gather_pairs(t, start, stop, window):
-            first = SLOTS * ((t - 1) % LANES)
-            nc.vector.tensor_copy(
-                pairs[:, t, start:stop], e_c[:, first : first + window].indirect(slot_list[:, start // 16 : stop // 16]))
+        on_vector = nc.vector.tensor_copy
+
+        def gather_context(move, t, u):
+            lo, hi = SLOTS // 2 * u, SLOTS // 2 * (u + 1)
+            move(e_c[t][:, lo:hi], e_lane[t].indirect(ctx_list[:, lo // 16 : hi // 16]))
+
+        def gather_pairs(move, t, u):
+            lo, hi = SLOTS // 2 * u, SLOTS // 2 * (u + 1)
+            move(pairs[:, t, lo:hi], e_c[t][:].indirect(slot_list[:, lo // 16 : hi // 16]))
 
         nc.vector.tensor_copy(ts_i[:], ts_table[:].indirect(idx_list[:]))
-        middle = SLOTS // 2
-        gather_context(0, 0, SLOTS)
-        gather_pairs(0, 0, middle, SLOTS)
-        gather_pairs(0, middle, SLOTS, SLOTS)
-        gather_context(1, 0, SLOTS)
-        for t in range(1, LANES - 1):
-            gather_pairs(t, 0, middle, SLOTS)
-            gather_context(t + 1, 0, middle)
-            gather_context(t + 1, middle, SLOTS)
-            gather_pairs(t, middle, SLOTS, WINDOW)
-        gather_pairs(LANES - 1, 0, SLOTS, WINDOW)
+        for t in range(LANES):
+            gather_context(on_vector, t, 0)
+            gather_context(on_scalar, t, 1)
+            gather_pairs(on_vector, t, 0)
+            gather_pairs(on_scalar, t, 1)
 
-        w_words = w_by_d[:].rearrange("p c t -> p (c t)").bitcast(F32)
+        w_listed = [keep.tile([P, 2, OUT_SLOTS], BF16, name="w_listed%d" % v, align_bytes=64) for v in range(2)]
         w_ps = {}
+        w_by_i = {}
+
+        def gather_w(move, t, lo, hi):
+            move(w_listed[t // 2][:, t % 2, lo:hi], w_lane[t].indirect(idx_list[:, lo // 16 : hi // 16]))
 
         def turn_w(v):
-            w_ps[v] = banks.tile([P, LANES, P], F32, name="w_ps%d" % v, tag="bank%d" % (5, 3)[v])
-            for r in range(LANES):
-                nc.tensor.transpose(w_ps[v][:, r, :], w_words[:, 2 * P * r + v : 2 * P * (r + 1) : 2], identity[:])
+            w_ps[v] = banks.tile([P, 2, 2, P], F32, name="w_ps%d" % v, tag="bank%d" % (5, 6)[v])
+            words = w_listed[v][:].rearrange("p e c -> p (e c)").bitcast(F32)
+            for e in range(2):
+                for u in range(2):
+                    nc.tensor.transpose(w_ps[v][:, e, u, :], words[:, 2 * P * e + u : 2 * P * (e + 1) : 2], identity[:])
 
-        w_bf = {}
+        def lay_w(v, tag):
+            w_by_i[v] = keep.tile([P, 2 * P, LANES], BF16, name="w_by_i%d" % v, tag=tag, align_bytes=64)
+            words = w_by_i[v][:].rearrange("s c r -> s (c r)").bitcast(F32)
+            nc.scalar.copy(words.rearrange("s (e p u) -> s e p u", e=2, u=2), w_ps[v][:].rearrange("s e u p -> s e p u"))
 
-        for t in range(LANES):
-            w_bf[t] = keep.tile([P, WORDS], BF16, name="w_bf%d" % t, tag="w_bf%d" % (t % 2), align_bytes=64)
-            for u in range(2):
-                nc.scalar.copy(w_bf[t][:, halves[u]], w_part[t][u][:])
-            nc.scalar.activation(dealt(w_by_d[:, :, t]), w_bf[t][:].indirect(idx_list[:]), ACT.Copy)
-            if t == 1:
-                turn_w(0)
+        def weave_w(v):
+            nc.vector.tensor_copy(
+                w_by_d[:, :, 2 * v : 2 * v + 2].rearrange("p (r k i) e -> p k r i e", r=LANES, i=2),
+                w_listed[v][:].rearrange("p e (k i r) -> p k r i e", r=LANES, i=2))
+
+        for t in range(LANES - 1):
+            gather_w(on_scalar, t, 0, OUT_SLOTS)
+        turn_w(0)
 
         ts_dealt = keep.tile([P, OUT_SLOTS], F32, name="ts_dealt")
         nc.scalar.copy(dealt(ts_dealt[:]), listed(ts_i[:]))
-        nc.scalar.activation(minus_2ux[:], ux_col[:], ACT.Copy, scale=-2.0)
+        nc.gpsimd.tensor_scalar(minus_2ux[:], ux_col[:], -2.0, 0.0, ALU.mult, ALU.add)
         ts_ps = banks.tile([P, LANES, P], F32, name="ts_ps", tag="bank4")
         for r in range(LANES):
             nc.tensor.transpose(ts_ps[:, r, :], ts_dealt[:, P * r : P * (r + 1)], identity[:])
-        ts_col = keep.tile([P, LANES], F32, name="ts_col", tag="w3_1", align_bytes=64)
+        ts_col = keep.tile([P, LANES], F32, name="ts_col")
         nc.scalar.copy(ts_col[:], ts_ps[:, :, P - 1])
 
-        for u in range(2):
+        def sign_labels(u):
             for q in range(2):
                 n = 2 * u + q
-                nc.scalar.activation(
-                    dealt(signed_ux[n][:]), listed(y_half[u][:, q, :]), ACT.Identity,
-                    scale=minus_2ux[:, n : n + 1], bias=ux_col[:, n : n + 1])
-        for u in range(2):
-            for r0 in range(0, LANES, 2):
-                f_ps = banks.tile([P, 2, 2, P], F32, name="f_ps", tag="bank%d" % (2 * u + r0 // 2))
-                for r in range(2):
-                    for q in range(2):
-                        nc.tensor.transpose(
-                            f_ps[:, r, q, :], signed_ux[2 * u + q][:, P * (r0 + r) : P * (r0 + r + 1)], identity[:])
-                for r in range(2):
-                    nc.scalar.activation(
-                        factor[u][:, r0 + r, :].rearrange("s (p q) -> s p q", q=2),
-                        f_ps[:, r, :, :].rearrange("s q p -> s p q"), ACT.Copy, scale=ts_col[:, r0 + r : r0 + r + 1])
+                nc.vector.tensor_scalar(
+                    dealt(signed_ux[n][:]), listed(y_half[u][:, q, :]), minus_2ux[:, n : n + 1], ux_col[:, n : n + 1],
+                    ALU.mult, ALU.add)
 
-        def mx_tiles(name, width):
-            codes = keep.tile([P, width], U32, name=name + "_codes", align_bytes=64)
+        f_ps = {}
+
+        def turn_labels(u):
+            for v in range(2):
+                f_ps[u, v] = banks.tile([P, 2, 2, P], F32, name="f_ps", tag="bank%d" % (2 * u + v))
+                for e in range(2):
+                    for q in range(2):
+                        r = 2 * v + e
+                        nc.tensor.transpose(f_ps[u, v][:, e, q, :], signed_ux[2 * u + q][:, P * r : P * (r + 1)], identity[:])
+
+        def copy_factor(u, v):
+            for e in range(2):
+                r = 2 * v + e
+                target = factor[u][:, r, :].rearrange("s (p q) -> s p q", q=2)
+                source = f_ps[u, v][:, e, :, :].rearrange("s q p -> s p q")
+                if v == 0:
+                    nc.scalar.activation(target, source, ACT.Copy, scale=ts_col[:, r : r + 1])
+                else:
+                    nc.vector.tensor_scalar(target, source, ts_col[:, r : r + 1], None, ALU.mult)
+
+        def mx_tiles(name, width, tag=None):
+            codes = keep.tile([P, width], U32, name=name + "_codes", tag=tag or name + "_codes", align_bytes=64)
             scales = keep.tile([P, width], U8, name=name + "_scales", align_bytes=64)
             return codes, scales
 
@@ -179,13 +192,8 @@ def tile_attend_gcbow_ns_pl_kernel(tc, eT, wT, ts, ux, y, coffs, posnoffs, sloto
                 out=operand[0][:, cols].bitcast(fmt), scales=operand[1][:, cols], in_=grouped.rearrange("p c l -> p (c l)"))
 
         s_mx = mx_tiles("s", POS)
-        g_wide = mx_tiles("g", POS + POS // 2)
-        g_mx = [part[:, POS // 2 :] for part in g_wide]
-        nc.gpsimd.memset(g_wide[0][:, 0 : POS // 2], 0)
-        nc.gpsimd.memset(g_wide[1][:, 0 : POS // 2], 0)
-        wd_mx = mx_tiles("wd", OUT_SLOTS)
-        wi_mx = mx_tiles("wi", LANES * P)
-        s_bf = keep.tile([P, POS, LANES], BF16, name="s_bf", tag="w_bf1", align_bytes=64)
+        g_mx = mx_tiles("g", POS)
+        s_bf = keep.tile([P, POS, LANES], BF16, name="s_bf", align_bytes=64)
         g_bf = keep.tile([P, POS, LANES], BF16, name="g_bf", align_bytes=64)
         chunks = [slice(P * c, P * (c + 1)) for c in range(LANES)]
         pair_view = pairs[:].rearrange("p t (k i j) -> p k t i j", i=2, j=2)
@@ -202,7 +210,7 @@ def tile_attend_gcbow_ns_pl_kernel(tc, eT, wT, ts, ux, y, coffs, posnoffs, sloto
         sig = {}
 
         def score(c):
-            a_ps = banks.tile([P, LANES, P], F32, name="a_ps", tag="bank%d" % (0, 1, 4, 2)[c])
+            a_ps = banks.tile([P, LANES, P], F32, name="a_ps", tag="bank%d" % (4, 0, 1, 2)[c])
             for r in range(LANES):
                 nc.tensor.matmul_mx(
                     out=a_ps[:, r, :], lhsT=wd_mx[0][:, chunks[r]].bitcast(E4M3), lhsT_scale=wd_mx[1][:, chunks[r]],
@@ -225,102 +233,105 @@ def tile_attend_gcbow_ns_pl_kernel(tc, eT, wT, ts, ux, y, coffs, posnoffs, sloto
                     sig[c][:, :, cols].rearrange("s r (k i) -> s k r i", i=LINE),
                     factor[c // 2][:, :, chunks[c % 2]][:, :, cols].rearrange("s r (k i) -> s k r i", i=LINE), ALU.mult)
 
-        quantize(wd_mx, slice(0, OUT_SLOTS), w_by_d[:], E4M3)
         pair_sum(0)
         for c in range(1, LANES):
             pair_sum(c)
             quantize_s(c - 1)
-        score(0)
+        weave_w(0)
         quantize_s(3)
+        gather_w(on_vector, LANES - 1, 0, OUT_SLOTS // 2)
+        gather_w(on_scalar, LANES - 1, OUT_SLOTS // 2, OUT_SLOTS)
+        weave_w(1)
+        lay_w(0, "w_lane3")
+        wi_mx = mx_tiles("wi", LANES * P)
+        sign_labels(0)
+        wd_mx = mx_tiles("wd", OUT_SLOTS, "y_half0")
+        quantize(wd_mx, slice(0, OUT_SLOTS), w_by_d[:], E4M3)
+        sign_labels(1)
+        turn_labels(0)
+        copy_factor(0, 0)
+        copy_factor(0, 1)
+        quantize(wi_mx, slice(0, 2 * P), w_by_i[0][:], E4M3)
+        score(0)
+        turn_labels(1)
+        copy_factor(1, 0)
         score(1)
+        copy_factor(1, 1)
         score(2)
         score(3)
         turn_w(1)
-
-        w_first = keep.tile([P, P, LANES], BF16, name="w_first", tag="w3_1", align_bytes=64)
-        w_rest = keep.tile([P, LANES - 1, P, LANES], BF16, name="w_rest", tag="z3", align_bytes=64)
-        w_by_i = {}
-        for n, t in enumerate(ORDER):
-            w_by_i[t] = w_first[:] if n == 0 else w_rest[:, n - 1, :, :]
-            turned = w_ps[t // 2][:].rearrange("s r p -> s (r p)").bitcast(BF16).rearrange("s (r p e) -> s p r e", r=LANES, e=2)
-            nc.scalar.copy(w_by_i[t], turned[:, :, :, t % 2])
+        lay_w(1, "z3")
         loss_gradient(0)
         loss_gradient(1)
-        quantize(wi_mx, chunks[ORDER[0]], w_by_i[ORDER[0]], E4M3)
         loss_gradient(2)
         quantize(g_mx, slice(0, 2 * P), g_bf[:, 0 : 2 * P, :], E5M2)
 
-        def multiply_dh(j, bank, first):
-            dh_ps = banks.tile([P, POS], F32, name="dh_ps", tag="bank%d" % bank)
+        a, b, c, d = ORDER
+
+        def half_of_dh(j, u, bank, on_act):
+            cols = slice(POS // 2 * u, POS // 2 * (u + 1))
+            dh_ps = banks.tile([P, POS // 2], F32, name="dh_ps", tag="bank%d" % bank)
             nc.tensor.matmul_mx(
                 out=dh_ps[:], lhsT=wi_mx[0][:, chunks[j]].bitcast(E4M3), lhsT_scale=wi_mx[1][:, chunks[j]],
-                rhs=g_wide[0][:, first : first + POS].bitcast(E5M2), rhs_scale=g_wide[1][:, first : first + POS], start=True, stop=True)
-            return dh_ps
+                rhs=g_mx[0][:, cols].bitcast(E5M2), rhs_scale=g_mx[1][:, cols], start=True, stop=True)
+            if on_act:
+                nc.scalar.activation(dh[j][:, cols], dh_ps[:], ACT.Copy, scale=0.5)
+            else:
+                nc.vector.tensor_scalar(dh[j][:, cols], dh_ps[:], 0.5, None, ALU.mult)
 
-        def halve_dh(j, columns, start, stop):
-            nc.scalar.activation(dh[j][:, start:stop], columns, ACT.Copy, scale=0.5)
-
-        halve_dh(ORDER[0], multiply_dh(ORDER[0], 4, 0)[:, POS // 2 :], 0, POS // 2)
+        half_of_dh(a, 0, 4, True)
+        half_of_dh(b, 0, 5, True)
         loss_gradient(3)
         quantize(g_mx, chunks[2], g_bf[:, chunks[2], :], E5M2)
-        quantize(wi_mx, chunks[ORDER[1]], w_by_i[ORDER[1]], E4M3)
         quantize(g_mx, chunks[3], g_bf[:, chunks[3], :], E5M2)
-        for j in ORDER[2:]:
-            quantize(wi_mx, chunks[j], w_by_i[j], E4M3)
-
-        a, b, c, d = ORDER
-        dh_ps = {j: multiply_dh(j, (6, 7, 0, 1)[n], POS // 2) for n, j in enumerate(ORDER)}
+        quantize(wi_mx, slice(2 * P, 4 * P), w_by_i[1][:], E4M3)
+        half_of_dh(b, 1, 7, False)
+        half_of_dh(a, 1, 3, True)
+        whole = {}
+        for j, bank in ((c, 0), (d, 1)):
+            whole[j] = banks.tile([P, POS], F32, name="dh_whole", tag="bank%d" % bank)
+            nc.tensor.matmul_mx(
+                out=whole[j][:], lhsT=wi_mx[0][:, chunks[j]].bitcast(E4M3), lhsT_scale=wi_mx[1][:, chunks[j]],
+                rhs=g_mx[0][:].bitcast(E5M2), rhs_scale=g_mx[1][:], start=True, stop=True)
         out_bf = keep.tile([P, WORDS, LANES], BF16, name="out_bf", tag="pairs_then_out", align_bytes=64)
-        lanes_bf = keep.tile([P, LANES, WORDS], BF16, name="lanes_bf", tag="e_c_then_lanes", align_bytes=64)
-        de = {j: keep.tile([P, SLOTS], F32, name="de%d" % j, tag="w%d_0" % j, align_bytes=64) for j in ORDER}
+        lanes_bf = keep.tile([P, LANES, WORDS], BF16, name="lanes_bf", tag="e_lane0", align_bytes=64)
+        de = {j: keep.tile([P, SLOTS], F32, name="de%d" % j, tag="e_c%d" % j, align_bytes=64) for j in ORDER}
 
-        def on_scalar(out, in_):
-            nc.scalar.activation(out, in_, ACT.Copy)
-
-        on_vector = nc.vector.tensor_copy
-
-        def look_up(move, j, n):
-            lo, hi = CUTS[n], CUTS[n + 1]
+        def look_up(move, j, lo, hi):
             move(de[j][:, lo:hi], dh[j][:].indirect(posn_list[:, lo // 16 : hi // 16]))
 
-        def place(move, j, n):
-            lo, hi = CUTS[n], CUTS[n + 1]
+        def place(move, j, first, last):
+            lo, hi = CUTS[first], CUTS[last]
             move(grad[j][:].indirect(ctx_list[:, lo // 16 : hi // 16]), de[j][:, lo:hi])
 
         def store(queue, j):
             queue.dma_start(out_rows[:, j, :], grad[j][:])
 
-        def halve_on_vector(j):
-            nc.vector.tensor_scalar(dh[j][:], dh_ps[j][:], 0.5, None, ALU.mult)
-
-        halve_dh(a, dh_ps[a][:, POS // 2 :], POS // 2, POS)
-        halve_on_vector(b)
-        halve_on_vector(c)
-        for n in range(3):
-            look_up(on_scalar, a, n)
-            look_up(on_vector, b, n)
-        for n in range(3):
-            look_up(on_scalar, c, n)
-            place(on_vector, b, n)
+        look_up(on_scalar, a, 0, SLOTS)
+        look_up(on_vector, b, 0, SLOTS // 2)
+        look_up(on_vector, b, SLOTS // 2, SLOTS)
+        nc.vector.tensor_scalar(dh[c][:, 0:POS], whole[c][:], 0.5, None, ALU.mult)
+        place(on_vector, b, 0, 3)
         store(nc.sync, b)
         nc.gpsimd.tensor_scalar(lanes_bf[:, b, :], grad[b][:], 1.0, 0.0, ALU.mult, ALU.add)
-        for n in range(3):
-            place(on_scalar, a, n)
-        halve_dh(d, dh_ps[d][:], 0, POS)
+        place(on_scalar, a, 0, 1)
+        look_up(on_scalar, c, 0, SLOTS)
+        place(on_scalar, a, 1, 2)
+        nc.scalar.activation(dh[d][:, 0:POS], whole[d][:], ACT.Copy, scale=0.5)
+        place(on_scalar, a, 2, 3)
         store(nc.scalar, a)
         nc.gpsimd.tensor_scalar(lanes_bf[:, a, :], grad[a][:], 1.0, 0.0, ALU.mult, ALU.add)
-        for n in range(3):
-            place(on_vector, c, n)
-            look_up(on_scalar, d, n)
+        place(on_vector, c, 0, 3)
         store(nc.sync, c)
+        look_up(on_scalar, d, 0, SLOTS)
         for n in range(3):
-            place(on_scalar, d, n)
+            place(on_scalar, d, n, n + 1)
         store(nc.sync, d)
         mine = slice(0, SPLIT)
         theirs = slice(SPLIT, WORDS)
         nc.vector.tensor_copy(lanes_bf[:, c, :], grad[c][:])
-        nc.vector.tensor_copy(out_bf[:, theirs, 2:4], lanes_bf[:, 2:4, theirs].rearrange("p t c -> p c t"))
-        nc.vector.tensor_copy(out_bf[:, mine, 1:4], lanes_bf[:, 1:4, mine].rearrange("p t c -> p c t"))
+        nc.vector.tensor_copy(out_bf[:, theirs, 0:2], lanes_bf[:, 0:2, theirs].rearrange("p t c -> p c t"))
+        nc.vector.tensor_copy(out_bf[:, mine, 0:3], lanes_bf[:, 0:3, mine].rearrange("p t c -> p c t"))
 
         out_codes = keep.tile([P, WORDS], U32, name="out_codes", align_bytes=64)
         out_scales = keep.tile([P, WORDS // 4], U8, name="out_scales", align_bytes=64)
@@ -329,7 +340,7 @@ def tile_attend_gcbow_ns_pl_kernel(tc, eT, wT, ts, ux, y, coffs, posnoffs, sloto
         half = SPLIT // PIECE
         for cols in pieces[half:]:
             nc.scalar.copy(lanes_bf[:, d, cols], grad[d][:, cols])
-            nc.scalar.copy(out_bf[:, cols, 0:2], lanes_bf[:, 0:2, cols].rearrange("p t c -> p c t"))
+            nc.scalar.copy(out_bf[:, cols, 2:4], lanes_bf[:, 2:4, cols].rearrange("p t c -> p c t"))
         nc.vector.tensor_copy(out_bf[:, pieces[0], d], grad[d][:, pieces[0]])
         stored = 0
         for n, cols in enumerate(pieces):

@@ -158,9 +158,14 @@ def tile_attend_gcbow_ns_pl_kernel(tc, eT, wT, ts, ux, y, coffs, posnoffs, sloto
         def sign_labels(u):
             for q in range(2):
                 n = 2 * u + q
-                nc.vector.tensor_scalar(
-                    dealt(signed_ux[n][:]), listed(y_half[u][:, q, :]), minus_2ux[:, n : n + 1], ux_col[:, n : n + 1],
-                    ALU.mult, ALU.add)
+                if u == 1:
+                    nc.vector.tensor_scalar(
+                        dealt(signed_ux[n][:]), listed(y_half[u][:, q, :]), minus_2ux[:, n : n + 1], ux_col[:, n : n + 1],
+                        ALU.mult, ALU.add)
+                else:
+                    nc.scalar.activation(
+                        dealt(signed_ux[n][:]), listed(y_half[u][:, q, :]), ACT.Identity,
+                        scale=minus_2ux[:, n : n + 1], bias=ux_col[:, n : n + 1])
 
         f_ps = {}
 
@@ -239,19 +244,19 @@ def tile_attend_gcbow_ns_pl_kernel(tc, eT, wT, ts, ux, y, coffs, posnoffs, sloto
             quantize_s(c - 1)
         weave_w(0)
         quantize_s(3)
+        lay_w(0, "w_lane2")
         gather_w(on_vector, LANES - 1, 0, OUT_SLOTS // 2)
         gather_w(on_scalar, LANES - 1, OUT_SLOTS // 2, OUT_SLOTS)
+        wi_mx = {0: mx_tiles("wi0", 2 * P, "w_lane3")}
+        quantize(wi_mx[0], slice(0, 2 * P), w_by_i[0][:], E4M3)
         weave_w(1)
-        lay_w(0, "w_lane3")
-        wi_mx = mx_tiles("wi", LANES * P)
         sign_labels(0)
+        sign_labels(1)
         wd_mx = mx_tiles("wd", OUT_SLOTS, "y_half0")
         quantize(wd_mx, slice(0, OUT_SLOTS), w_by_d[:], E4M3)
-        sign_labels(1)
         turn_labels(0)
         copy_factor(0, 0)
         copy_factor(0, 1)
-        quantize(wi_mx, slice(0, 2 * P), w_by_i[0][:], E4M3)
         score(0)
         turn_labels(1)
         copy_factor(1, 0)
@@ -272,7 +277,7 @@ def tile_attend_gcbow_ns_pl_kernel(tc, eT, wT, ts, ux, y, coffs, posnoffs, sloto
             cols = slice(POS // 2 * u, POS // 2 * (u + 1))
             dh_ps = banks.tile([P, POS // 2], F32, name="dh_ps", tag="bank%d" % bank)
             nc.tensor.matmul_mx(
-                out=dh_ps[:], lhsT=wi_mx[0][:, chunks[j]].bitcast(E4M3), lhsT_scale=wi_mx[1][:, chunks[j]],
+                out=dh_ps[:], lhsT=wi_mx[j // 2][0][:, chunks[j % 2]].bitcast(E4M3), lhsT_scale=wi_mx[j // 2][1][:, chunks[j % 2]],
                 rhs=g_mx[0][:, cols].bitcast(E5M2), rhs_scale=g_mx[1][:, cols], start=True, stop=True)
             if on_act:
                 nc.scalar.activation(dh[j][:, cols], dh_ps[:], ACT.Copy, scale=0.5)
@@ -284,14 +289,15 @@ def tile_attend_gcbow_ns_pl_kernel(tc, eT, wT, ts, ux, y, coffs, posnoffs, sloto
         loss_gradient(3)
         quantize(g_mx, chunks[2], g_bf[:, chunks[2], :], E5M2)
         quantize(g_mx, chunks[3], g_bf[:, chunks[3], :], E5M2)
-        quantize(wi_mx, slice(2 * P, 4 * P), w_by_i[1][:], E4M3)
+        wi_mx[1] = mx_tiles("wi1", 2 * P, "sig3")
+        quantize(wi_mx[1], slice(0, 2 * P), w_by_i[1][:], E4M3)
         half_of_dh(b, 1, 7, False)
         half_of_dh(a, 1, 3, True)
         whole = {}
         for j, bank in ((c, 0), (d, 1)):
             whole[j] = banks.tile([P, POS], F32, name="dh_whole", tag="bank%d" % bank)
             nc.tensor.matmul_mx(
-                out=whole[j][:], lhsT=wi_mx[0][:, chunks[j]].bitcast(E4M3), lhsT_scale=wi_mx[1][:, chunks[j]],
+                out=whole[j][:], lhsT=wi_mx[j // 2][0][:, chunks[j % 2]].bitcast(E4M3), lhsT_scale=wi_mx[j // 2][1][:, chunks[j % 2]],
                 rhs=g_mx[0][:].bitcast(E5M2), rhs_scale=g_mx[1][:], start=True, stop=True)
         out_bf = keep.tile([P, WORDS, LANES], BF16, name="out_bf", tag="pairs_then_out", align_bytes=64)
         lanes_bf = keep.tile([P, LANES, WORDS], BF16, name="lanes_bf", tag="e_lane0", align_bytes=64)
@@ -307,7 +313,8 @@ def tile_attend_gcbow_ns_pl_kernel(tc, eT, wT, ts, ux, y, coffs, posnoffs, sloto
         def store(queue, j):
             queue.dma_start(out_rows[:, j, :], grad[j][:])
 
-        look_up(on_scalar, a, 0, SLOTS)
+        look_up(on_scalar, a, 0, CUTS[1])
+        look_up(on_scalar, a, CUTS[1], SLOTS)
         look_up(on_vector, b, 0, SLOTS // 2)
         look_up(on_vector, b, SLOTS // 2, SLOTS)
         nc.vector.tensor_scalar(dh[c][:, 0:POS], whole[c][:], 0.5, None, ALU.mult)
@@ -315,17 +322,20 @@ def tile_attend_gcbow_ns_pl_kernel(tc, eT, wT, ts, ux, y, coffs, posnoffs, sloto
         store(nc.sync, b)
         nc.gpsimd.tensor_scalar(lanes_bf[:, b, :], grad[b][:], 1.0, 0.0, ALU.mult, ALU.add)
         place(on_scalar, a, 0, 1)
+        nc.scalar.activation(dh[d][:, 0:POS], whole[d][:], ACT.Copy, scale=0.5)
         look_up(on_scalar, c, 0, SLOTS)
         place(on_scalar, a, 1, 2)
-        nc.scalar.activation(dh[d][:, 0:POS], whole[d][:], ACT.Copy, scale=0.5)
+        look_up(on_scalar, d, CUTS[0], CUTS[1])
         place(on_scalar, a, 2, 3)
+        look_up(on_scalar, d, CUTS[1], CUTS[2])
         store(nc.scalar, a)
         nc.gpsimd.tensor_scalar(lanes_bf[:, a, :], grad[a][:], 1.0, 0.0, ALU.mult, ALU.add)
         place(on_vector, c, 0, 3)
         store(nc.sync, c)
-        look_up(on_scalar, d, 0, SLOTS)
-        for n in range(3):
-            place(on_scalar, d, n, n + 1)
+        place(on_scalar, d, 0, 1)
+        look_up(on_scalar, d, CUTS[2], CUTS[3])
+        place(on_scalar, d, 1, 2)
+        place(on_scalar, d, 2, 3)
         store(nc.sync, d)
         mine = slice(0, SPLIT)
         theirs = slice(SPLIT, WORDS)

@@ -28,7 +28,7 @@ LINE = 4
 PIECE = 256
 ORDER = (0, 1, 2, 3)
 CUTS = (0, 384, 768, 1024)
-SPLIT = 1280
+SPLIT = 1152
 
 
 def tile_attend_gcbow_ns_pl_kernel(tc, eT, wT, ts, ux, y, coffs, posnoffs, slotoffs, offs, out_0, out_1, out_2):
@@ -322,11 +322,11 @@ def tile_attend_gcbow_ns_pl_kernel(tc, eT, wT, ts, ux, y, coffs, posnoffs, sloto
         store(nc.sync, b)
         nc.gpsimd.tensor_scalar(lanes_bf[:, b, :], grad[b][:], 1.0, 0.0, ALU.mult, ALU.add)
         place(on_scalar, a, 0, 1)
-        nc.scalar.activation(dh[d][:, 0:POS], whole[d][:], ACT.Copy, scale=0.5)
         look_up(on_scalar, c, 0, SLOTS)
         place(on_scalar, a, 1, 2)
-        look_up(on_scalar, d, CUTS[0], CUTS[1])
+        nc.scalar.activation(dh[d][:, 0:POS], whole[d][:], ACT.Copy, scale=0.5)
         place(on_scalar, a, 2, 3)
+        look_up(on_scalar, d, CUTS[0], CUTS[1])
         look_up(on_scalar, d, CUTS[1], CUTS[2])
         store(nc.scalar, a)
         nc.gpsimd.tensor_scalar(lanes_bf[:, a, :], grad[a][:], 1.0, 0.0, ALU.mult, ALU.add)
@@ -344,26 +344,34 @@ def tile_attend_gcbow_ns_pl_kernel(tc, eT, wT, ts, ux, y, coffs, posnoffs, sloto
         nc.vector.tensor_copy(out_bf[:, mine, 0:3], lanes_bf[:, 0:3, mine].rearrange("p t c -> p c t"))
 
         out_codes = keep.tile([P, WORDS], U32, name="out_codes", align_bytes=64)
-        out_scales = keep.tile([P, WORDS // 4], U8, name="out_scales", align_bytes=64)
+        out_scales = keep.tile([P, WORDS // 2], U8, name="out_scales", align_bytes=64)
         words_hbm = out_1[0].rearrange("p c l -> p (c l)").bitcast(I32)
-        pieces = [slice(PIECE * n, PIECE * (n + 1)) for n in range(WORDS // PIECE)]
-        half = SPLIT // PIECE
-        for cols in pieces[half:]:
-            nc.scalar.copy(lanes_bf[:, d, cols], grad[d][:, cols])
-            nc.scalar.copy(out_bf[:, cols, 2:4], lanes_bf[:, 2:4, cols].rearrange("p t c -> p c t"))
-        nc.vector.tensor_copy(out_bf[:, pieces[0], d], grad[d][:, pieces[0]])
-        stored = 0
-        for n, cols in enumerate(pieces):
-            if n + 1 < half:
-                nc.vector.tensor_copy(out_bf[:, pieces[n + 1], d], grad[d][:, pieces[n + 1]])
+        quarter = WORDS // 4
+
+        def round_last(lo, hi):
+            nc.vector.tensor_copy(out_bf[:, lo:hi, d], grad[d][:, lo:hi])
+
+        def pack(lo, hi):
+            upper = lo // (WORDS // 2)
+            first = upper * (WORDS // 2)
             nc.vector.quantize_mx(
-                out=out_codes[:, cols].bitcast(E4M3), scales=out_scales[4 * (n // 2) :, pieces[n % 2]],
-                in_=out_bf[:, cols, :].rearrange("p c l -> p (c l)"))
-            if n % 2 == 0 and n > 0 or n + 1 == len(pieces):
-                done = slice(stored, cols.stop)
-                nc.sync.dma_start(words_hbm[:, done], out_codes[:, done].bitcast(I32))
-                stored = cols.stop
-        scales_hbm = out_2[0].bitcast(I32).rearrange("f (a c) -> a f c", a=4)
+                out=out_codes[:, lo:hi].bitcast(E4M3), scales=out_scales[4 * upper :, lo - first : hi - first],
+                in_=out_bf[:, lo:hi, :].rearrange("p c l -> p (c l)"))
+            nc.sync.dma_start(words_hbm[:, lo:hi], out_codes[:, lo:hi].bitcast(I32))
+
+        nc.scalar.copy(lanes_bf[:, d, SPLIT : 3 * quarter], grad[d][:, SPLIT : 3 * quarter])
+        nc.scalar.copy(lanes_bf[:, d, 3 * quarter :], grad[d][:, 3 * quarter :])
+        for lo, hi in ((SPLIT, 3 * quarter), (3 * quarter, WORDS - PIECE), (WORDS - PIECE, WORDS)):
+            nc.scalar.copy(out_bf[:, lo:hi, 2:4], lanes_bf[:, 2:4, lo:hi].rearrange("p t c -> p c t"))
+        round_last(0, quarter)
+        round_last(quarter, 2 * quarter)
+        pack(0, quarter)
+        round_last(2 * quarter, SPLIT)
+        pack(quarter, 2 * quarter)
+        pack(2 * quarter, 3 * quarter)
+        pack(3 * quarter, WORDS - PIECE)
+        pack(WORDS - PIECE, WORDS)
+        scales_hbm = out_2[0].bitcast(I32).rearrange("f (a c) -> a f c", a=2)
         for group in range(4):
             nc.scalar.dma_start(
-                scales_hbm[:, 4 * group : 4 * group + 4, :], out_scales[32 * group : 32 * group + 16, :].bitcast(I32))
+                scales_hbm[:, 4 * group : 4 * group + 4, :], out_scales[32 * group : 32 * group + 8, :].bitcast(I32))

@@ -340,8 +340,10 @@ def tile_attend_gcbow_ns_pl_kernel(tc, eT, wT, ts, ux, y, coffs, posnoffs, sloto
         mine = slice(0, SPLIT)
         theirs = slice(SPLIT, WORDS)
         nc.vector.tensor_copy(lanes_bf[:, c, :], grad[c][:])
-        nc.vector.tensor_copy(out_bf[:, theirs, 0:2], lanes_bf[:, 0:2, theirs].rearrange("p t c -> p c t"))
-        nc.vector.tensor_copy(out_bf[:, mine, 0:3], lanes_bf[:, 0:3, mine].rearrange("p t c -> p c t"))
+        for cols, lanes in ((theirs, slice(0, 2)), (mine, slice(0, 3))):
+            nc.vector.tensor_copy(
+                out_bf[:, cols, lanes].rearrange("p (k i) t -> p k t i", i=LINE),
+                lanes_bf[:, lanes, cols].rearrange("p t (k i) -> p k t i", i=LINE))
 
         out_codes = keep.tile([P, WORDS], U32, name="out_codes", align_bytes=64)
         out_scales = keep.tile([P, WORDS // 2], U8, name="out_scales", align_bytes=64)

@@ -28,7 +28,7 @@ LINE = 4
 PIECE = 256
 ORDER = (0, 1, 2, 3)
 CUTS = (0, 384, 768, 1024)
-SPLIT = 1152
+SPLIT = 1280
 
 
 def tile_attend_gcbow_ns_pl_kernel(tc, eT, wT, ts, ux, y, coffs, posnoffs, slotoffs, offs, out_0, out_1, out_2):
@@ -49,7 +49,7 @@ def tile_attend_gcbow_ns_pl_kernel(tc, eT, wT, ts, ux, y, coffs, posnoffs, sloto
         e_lane = [keep.tile([P, WORDS], F32, name="e_lane%d" % t, align_bytes=64)[:] for t in range(LANES)]
         w_lane = [keep.tile([P, WORDS], F32, name="w_lane%d" % t, align_bytes=64)[:] for t in range(LANES)]
         ts_table = keep.tile([P, WORDS], F32, name="ts_table")
-        y_half = [keep.tile([P, 2, OUT_SLOTS], F32, name="y_half%d" % u, align_bytes=64) for u in range(2)]
+        y_part = [keep.tile([P, OUT_SLOTS], F32, name="y_part%d" % n, align_bytes=64) for n in range(LANES)]
         ux_col = keep.tile([P, LANES], F32, name="ux_col")
         minus_2ux = keep.tile([P, LANES], F32, name="minus_2ux")
         identity = keep.tile([P, P], F32, name="identity")
@@ -82,8 +82,8 @@ def tile_attend_gcbow_ns_pl_kernel(tc, eT, wT, ts, ux, y, coffs, posnoffs, sloto
         nc.sync.dma_start(ux_col[:].rearrange("p (u q) -> p u q", q=2), ux_rows)
         for t in range(LANES):
             nc.sync.dma_start(w_lane[t], w_rows[:, t, :])
-        nc.sync.dma_start(y_half[0][:], y_rows[:, 0, :, :])
-        nc.sync.dma_start(y_half[1][:], y_rows[:, 1, :, :])
+        for n in range(LANES):
+            nc.sync.dma_start(y_part[n][:], y_rows[:, n // 2, n % 2, :])
         nc.sync.dma_start(posn_list[:], posnoffs)
 
         pairs = keep.tile([P, LANES, SLOTS], F32, name="pairs", tag="pairs_then_out", align_bytes=64)
@@ -158,13 +158,13 @@ def tile_attend_gcbow_ns_pl_kernel(tc, eT, wT, ts, ux, y, coffs, posnoffs, sloto
         def sign_labels(u):
             for q in range(2):
                 n = 2 * u + q
-                if u == 1:
+                if n == LANES - 1:
                     nc.vector.tensor_scalar(
-                        dealt(signed_ux[n][:]), listed(y_half[u][:, q, :]), minus_2ux[:, n : n + 1], ux_col[:, n : n + 1],
+                        dealt(signed_ux[n][:]), listed(y_part[n][:]), minus_2ux[:, n : n + 1], ux_col[:, n : n + 1],
                         ALU.mult, ALU.add)
                 else:
                     nc.scalar.activation(
-                        dealt(signed_ux[n][:]), listed(y_half[u][:, q, :]), ACT.Identity,
+                        dealt(signed_ux[n][:]), listed(y_part[n][:]), ACT.Identity,
                         scale=minus_2ux[:, n : n + 1], bias=ux_col[:, n : n + 1])
 
         f_ps = {}
@@ -252,7 +252,7 @@ def tile_attend_gcbow_ns_pl_kernel(tc, eT, wT, ts, ux, y, coffs, posnoffs, sloto
         weave_w(1)
         sign_labels(0)
         sign_labels(1)
-        wd_mx = mx_tiles("wd", OUT_SLOTS, "y_half0")
+        wd_mx = mx_tiles("wd", OUT_SLOTS, "y_part1")
         quantize(wd_mx, slice(0, OUT_SLOTS), w_by_d[:], E4M3)
         turn_labels(0)
         copy_factor(0, 0)
@@ -273,9 +273,9 @@ def tile_attend_gcbow_ns_pl_kernel(tc, eT, wT, ts, ux, y, coffs, posnoffs, sloto
 
         a, b, c, d = ORDER
 
-        def half_of_dh(j, u, bank, on_act):
-            cols = slice(POS // 2 * u, POS // 2 * (u + 1))
-            dh_ps = banks.tile([P, POS // 2], F32, name="dh_ps", tag="bank%d" % bank)
+        def part_of_dh(j, lo, hi, bank, on_act):
+            cols = slice(lo, hi)
+            dh_ps = banks.tile([P, hi - lo], F32, name="dh_ps", tag="bank%d" % bank)
             nc.tensor.matmul_mx(
                 out=dh_ps[:], lhsT=wi_mx[j // 2][0][:, chunks[j % 2]].bitcast(E4M3), lhsT_scale=wi_mx[j // 2][1][:, chunks[j % 2]],
                 rhs=g_mx[0][:, cols].bitcast(E5M2), rhs_scale=g_mx[1][:, cols], start=True, stop=True)
@@ -284,15 +284,17 @@ def tile_attend_gcbow_ns_pl_kernel(tc, eT, wT, ts, ux, y, coffs, posnoffs, sloto
             else:
                 nc.vector.tensor_scalar(dh[j][:, cols], dh_ps[:], 0.5, None, ALU.mult)
 
-        half_of_dh(a, 0, 4, True)
-        half_of_dh(b, 0, 5, True)
+        part_of_dh(a, 0, 2 * P, 4, True)
+        part_of_dh(b, 0, 2 * P, 5, True)
         loss_gradient(3)
         quantize(g_mx, chunks[2], g_bf[:, chunks[2], :], E5M2)
+        part_of_dh(a, 2 * P, 3 * P, 2, True)
+        part_of_dh(b, 2 * P, 3 * P, 6, True)
         quantize(g_mx, chunks[3], g_bf[:, chunks[3], :], E5M2)
-        wi_mx[1] = mx_tiles("wi1", 2 * P, "sig3")
+        wi_mx[1] = mx_tiles("wi1", 2 * P, "g_bf")
         quantize(wi_mx[1], slice(0, 2 * P), w_by_i[1][:], E4M3)
-        half_of_dh(b, 1, 7, False)
-        half_of_dh(a, 1, 3, True)
+        part_of_dh(b, 3 * P, POS, 7, False)
+        part_of_dh(a, 3 * P, POS, 3, True)
         whole = {}
         for j, bank in ((c, 0), (d, 1)):
             whole[j] = banks.tile([P, POS], F32, name="dh_whole", tag="bank%d" % bank)
@@ -318,15 +320,15 @@ def tile_attend_gcbow_ns_pl_kernel(tc, eT, wT, ts, ux, y, coffs, posnoffs, sloto
         look_up(on_vector, b, 0, SLOTS // 2)
         look_up(on_vector, b, SLOTS // 2, SLOTS)
         nc.vector.tensor_scalar(dh[c][:, 0:POS], whole[c][:], 0.5, None, ALU.mult)
+        nc.vector.tensor_scalar(dh[d][:, 0:POS], whole[d][:], 0.5, None, ALU.mult)
         place(on_vector, b, 0, 3)
         store(nc.sync, b)
         nc.gpsimd.tensor_scalar(lanes_bf[:, b, :], grad[b][:], 1.0, 0.0, ALU.mult, ALU.add)
         place(on_scalar, a, 0, 1)
         look_up(on_scalar, c, 0, SLOTS)
         place(on_scalar, a, 1, 2)
-        nc.scalar.activation(dh[d][:, 0:POS], whole[d][:], ACT.Copy, scale=0.5)
-        place(on_scalar, a, 2, 3)
         look_up(on_scalar, d, CUTS[0], CUTS[1])
+        place(on_scalar, a, 2, 3)
         look_up(on_scalar, d, CUTS[1], CUTS[2])
         store(nc.scalar, a)
         nc.gpsimd.tensor_scalar(lanes_bf[:, a, :], grad[a][:], 1.0, 0.0, ALU.mult, ALU.add)
@@ -359,6 +361,8 @@ def tile_attend_gcbow_ns_pl_kernel(tc, eT, wT, ts, ux, y, coffs, posnoffs, sloto
             nc.vector.quantize_mx(
                 out=out_codes[:, lo:hi].bitcast(E4M3), scales=out_scales[4 * upper :, lo - first : hi - first],
                 in_=out_bf[:, lo:hi, :].rearrange("p c l -> p (c l)"))
+
+        def store_words(lo, hi):
             nc.sync.dma_start(words_hbm[:, lo:hi], out_codes[:, lo:hi].bitcast(I32))
 
         nc.scalar.copy(lanes_bf[:, d, SPLIT : 3 * quarter], grad[d][:, SPLIT : 3 * quarter])
@@ -368,11 +372,16 @@ def tile_attend_gcbow_ns_pl_kernel(tc, eT, wT, ts, ux, y, coffs, posnoffs, sloto
         round_last(0, quarter)
         round_last(quarter, 2 * quarter)
         pack(0, quarter)
+        store_words(0, quarter)
         round_last(2 * quarter, SPLIT)
         pack(quarter, 2 * quarter)
+        store_words(quarter, 2 * quarter)
         pack(2 * quarter, 3 * quarter)
+        store_words(2 * quarter, 3 * quarter)
         pack(3 * quarter, WORDS - PIECE)
+        store_words(3 * quarter, WORDS - PIECE)
         pack(WORDS - PIECE, WORDS)
+        store_words(WORDS - PIECE, WORDS)
         scales_hbm = out_2[0].bitcast(I32).rearrange("f (a c) -> a f c", a=2)
         for group in range(4):
             nc.scalar.dma_start(

@@ -22,13 +22,11 @@ WORDS = 2048
 SLOTS = 1024
 POS = 512
 OUT_SLOTS = 512
-BLOCK_ROWS = 8
-WINDOW = 1040
 LINE = 4
+CUTS = (0, 384, 768, SLOTS)
+DH_COLUMNS = (656, 528, 1040, POS)
+SPLIT = 1152
 PIECE = 256
-ORDER = (0, 1, 2, 3)
-CUTS = (0, 384, 768, 1024)
-SPLIT = 1280
 
 
 def tile_attend_gcbow_ns_pl_kernel(tc, eT, wT, ts, ux, y, coffs, posnoffs, slotoffs, offs, out_0, out_1, out_2):
@@ -41,11 +39,11 @@ def tile_attend_gcbow_ns_pl_kernel(tc, eT, wT, ts, ux, y, coffs, posnoffs, sloto
         posn_list = keep.tile([P, SLOTS // 16], U16, name="posn_list")
         slot_list = keep.tile([P, SLOTS // 16], U16, name="slot_list")
         idx_list = keep.tile([P, OUT_SLOTS // 16], U16, name="idx_list")
-        e_rows = eT.rearrange("(p t) c -> p t c", t=LANES)
-        w_rows = wT.rearrange("(p t) c -> p t c", t=LANES)
-        out_rows = out_0.rearrange("(p t) c -> p t c", t=LANES)
+        e_rows = eT.rearrange("(p t) col -> p t col", t=LANES)
+        w_rows = wT.rearrange("(p t) col -> p t col", t=LANES)
+        out_rows = out_0.rearrange("(p t) col -> p t col", t=LANES)
         y_rows = y.rearrange("(u p q) i -> p u q i", p=P, q=2)
-        ux_rows = ux.rearrange("(u p q) o -> p u (q o)", p=P, q=2)
+        ux_rows = ux.rearrange("(u p q) one -> p u (q one)", p=P, q=2)
         e_lane = [keep.tile([P, WORDS], F32, name="e_lane%d" % t, align_bytes=64)[:] for t in range(LANES)]
         w_lane = [keep.tile([P, WORDS], F32, name="w_lane%d" % t, align_bytes=64)[:] for t in range(LANES)]
         ts_table = keep.tile([P, WORDS], F32, name="ts_table")
@@ -54,23 +52,20 @@ def tile_attend_gcbow_ns_pl_kernel(tc, eT, wT, ts, ux, y, coffs, posnoffs, sloto
         minus_2ux = keep.tile([P, LANES], F32, name="minus_2ux")
         identity = keep.tile([P, P], F32, name="identity")
         e_c = [keep.tile([P, SLOTS], F32, name="e_c%d" % t, align_bytes=64) for t in range(LANES)]
-        dh = [keep.tile([P, WINDOW], F32, name="dh%d" % t, align_bytes=64) for t in range(LANES)]
+        dh = [keep.tile([P, DH_COLUMNS[t]], F32, name="dh%d" % t, align_bytes=64) for t in range(LANES)]
+        grad = [keep.tile([P, WORDS], F32, name="grad%d" % t, align_bytes=64) for t in range(LANES)]
 
         nc.vector.memset(ts_table[0 : P - 1, :], 0.0)
+
         warm = keep.tile([P, 2], F32, name="warm")
         nc.vector.memset(warm[:, 0:1], 0.0)
         nc.scalar.activation(warm[:, 1:2], warm[:, 0:1], ACT.Sigmoid)
 
         make_identity(nc, identity[:])
-        grad = {}
-
-        def clear(j, tag):
-            grad[j] = keep.tile([P, WORDS], F32, name="grad%d" % j, tag=tag, align_bytes=64)
-            nc.gpsimd.memset(grad[j][:], 0.0)
-
-        for j in ORDER:
-            clear(j, "window%d" % j)
-            nc.gpsimd.memset(dh[j][:, POS:], 0.0)
+        for t in range(LANES):
+            nc.gpsimd.memset(grad[t][:], 0.0)
+            if DH_COLUMNS[t] > POS:
+                nc.gpsimd.memset(dh[t][:, POS:], 0.0)
 
         nc.sync.dma_start(ts_table[P - 1 : P, :], ts[0:1, :])
         nc.sync.dma_start(idx_list[:], offs)
@@ -80,35 +75,38 @@ def tile_attend_gcbow_ns_pl_kernel(tc, eT, wT, ts, ux, y, coffs, posnoffs, sloto
         for t in range(1, LANES):
             nc.sync.dma_start(e_lane[t], e_rows[:, t, :])
         nc.sync.dma_start(ux_col[:].rearrange("p (u q) -> p u q", q=2), ux_rows)
-        for t in range(LANES):
+        nc.sync.dma_start(w_lane[0], w_rows[:, 0, :])
+        nc.sync.dma_start(w_lane[1], w_rows[:, 1, :])
+        nc.sync.dma_start(y_part[0][:], y_rows[:, 0, 0, :])
+        nc.sync.dma_start(y_part[1][:], y_rows[:, 0, 1, :])
+        for t in range(2, LANES):
             nc.sync.dma_start(w_lane[t], w_rows[:, t, :])
-        for n in range(LANES):
-            nc.sync.dma_start(y_part[n][:], y_rows[:, n // 2, n % 2, :])
+            nc.sync.dma_start(y_part[t][:], y_rows[:, 1, t - 2, :])
         nc.sync.dma_start(posn_list[:], posnoffs)
 
         pairs = keep.tile([P, LANES, SLOTS], F32, name="pairs", tag="pairs_then_out", align_bytes=64)
         w_by_d = keep.tile([P, OUT_SLOTS, LANES], BF16, name="w_by_d", align_bytes=64)
         ts_i = keep.tile([P, OUT_SLOTS], F32, name="ts_i")
         signed_ux = [keep.tile([P, OUT_SLOTS], F32, name="signed_ux%d" % n) for n in range(POS // P)]
-        factor = [keep.tile([P, LANES, POS // 2], F32, name="factor%d" % u) for u in range(2)]
+        factor = {}
 
         def listed(row):
-            return row.rearrange("p (k i r) -> p k r i", r=LANES, i=LINE)
+            return row.rearrange("p (k run r) -> p k r run", r=LANES, run=LINE)
 
         def dealt(row):
-            return row.rearrange("p (r k i) -> p k r i", r=LANES, i=LINE)
+            return row.rearrange("p (r k run) -> p k r run", r=LANES, run=LINE)
 
         def on_scalar(out, in_):
             nc.scalar.activation(out, in_, ACT.Copy)
 
         on_vector = nc.vector.tensor_copy
 
-        def gather_context(move, t, u):
-            lo, hi = SLOTS // 2 * u, SLOTS // 2 * (u + 1)
+        def gather_context(move, t, half):
+            lo, hi = SLOTS // 2 * half, SLOTS // 2 * (half + 1)
             move(e_c[t][:, lo:hi], e_lane[t].indirect(ctx_list[:, lo // 16 : hi // 16]))
 
-        def gather_pairs(move, t, u):
-            lo, hi = SLOTS // 2 * u, SLOTS // 2 * (u + 1)
+        def gather_pairs(move, t, half):
+            lo, hi = SLOTS // 2 * half, SLOTS // 2 * (half + 1)
             move(pairs[:, t, lo:hi], e_c[t][:].indirect(slot_list[:, lo // 16 : hi // 16]))
 
         nc.vector.tensor_copy(ts_i[:], ts_table[:].indirect(idx_list[:]))
@@ -125,26 +123,28 @@ def tile_attend_gcbow_ns_pl_kernel(tc, eT, wT, ts, ux, y, coffs, posnoffs, sloto
         def gather_w(move, t, lo, hi):
             move(w_listed[t // 2][:, t % 2, lo:hi], w_lane[t].indirect(idx_list[:, lo // 16 : hi // 16]))
 
-        def turn_w(v):
-            w_ps[v] = banks.tile([P, 2, 2, P], F32, name="w_ps%d" % v, tag="bank%d" % (5, 6)[v])
-            words = w_listed[v][:].rearrange("p e c -> p (e c)").bitcast(F32)
+        def turn_w(v, bank):
+            w_ps[v] = banks.tile([P, 2, 2, P], F32, name="w_ps%d" % v, tag="bank%d" % bank)
+            words = w_listed[v][:].rearrange("p e col -> p (e col)").bitcast(F32)
             for e in range(2):
-                for u in range(2):
-                    nc.tensor.transpose(w_ps[v][:, e, u, :], words[:, 2 * P * e + u : 2 * P * (e + 1) : 2], identity[:])
+                for odd in range(2):
+                    nc.tensor.transpose(w_ps[v][:, e, odd, :], words[:, 2 * P * e + odd : 2 * P * (e + 1) : 2], identity[:])
 
         def lay_w(v, tag):
             w_by_i[v] = keep.tile([P, 2 * P, LANES], BF16, name="w_by_i%d" % v, tag=tag, align_bytes=64)
-            words = w_by_i[v][:].rearrange("s c r -> s (c r)").bitcast(F32)
-            nc.scalar.copy(words.rearrange("s (e p u) -> s e p u", e=2, u=2), w_ps[v][:].rearrange("s e u p -> s e p u"))
+            words = w_by_i[v][:].rearrange("o col r -> o (col r)").bitcast(F32)
+            nc.scalar.copy(words.rearrange("o (e p odd) -> o e p odd", e=2, odd=2), w_ps[v][:].rearrange("o e odd p -> o e p odd"))
 
         def weave_w(v):
             nc.vector.tensor_copy(
-                w_by_d[:, :, 2 * v : 2 * v + 2].rearrange("p (r k i) e -> p k r i e", r=LANES, i=2),
-                w_listed[v][:].rearrange("p e (k i r) -> p k r i e", r=LANES, i=2))
+                w_by_d[:, :, 2 * v : 2 * v + 2].rearrange("p (r k run) e -> p k r run e", r=LANES, run=2),
+                w_listed[v][:].rearrange("p e (k run r) -> p k r run e", r=LANES, run=2))
 
-        for t in range(LANES - 1):
+        for t in range(2):
             gather_w(on_scalar, t, 0, OUT_SLOTS)
-        turn_w(0)
+        turn_w(0, 5)
+        lay_w(0, "w_by_i0")
+        gather_w(on_scalar, 2, 0, OUT_SLOTS)
 
         ts_dealt = keep.tile([P, OUT_SLOTS], F32, name="ts_dealt")
         nc.scalar.copy(dealt(ts_dealt[:]), listed(ts_i[:]))
@@ -155,37 +155,26 @@ def tile_attend_gcbow_ns_pl_kernel(tc, eT, wT, ts, ux, y, coffs, posnoffs, sloto
         ts_col = keep.tile([P, LANES], F32, name="ts_col")
         nc.scalar.copy(ts_col[:], ts_ps[:, :, P - 1])
 
-        def sign_labels(u):
-            for q in range(2):
-                n = 2 * u + q
-                if n == LANES - 1:
-                    nc.vector.tensor_scalar(
-                        dealt(signed_ux[n][:]), listed(y_part[n][:]), minus_2ux[:, n : n + 1], ux_col[:, n : n + 1],
-                        ALU.mult, ALU.add)
-                else:
-                    nc.scalar.activation(
-                        dealt(signed_ux[n][:]), listed(y_part[n][:]), ACT.Identity,
-                        scale=minus_2ux[:, n : n + 1], bias=ux_col[:, n : n + 1])
+        def sign_labels(n):
+            nc.vector.tensor_scalar(
+                dealt(signed_ux[n][:]), listed(y_part[n][:]), minus_2ux[:, n : n + 1], ux_col[:, n : n + 1], ALU.mult, ALU.add)
 
         f_ps = {}
 
         def turn_labels(u):
             for v in range(2):
                 f_ps[u, v] = banks.tile([P, 2, 2, P], F32, name="f_ps", tag="bank%d" % (2 * u + v))
-                for e in range(2):
-                    for q in range(2):
-                        r = 2 * v + e
-                        nc.tensor.transpose(f_ps[u, v][:, e, q, :], signed_ux[2 * u + q][:, P * r : P * (r + 1)], identity[:])
+            for q in range(2):
+                for r in range(LANES):
+                    nc.tensor.transpose(
+                        f_ps[u, r // 2][:, r % 2, q, :], signed_ux[2 * u + q][:, P * r : P * (r + 1)], identity[:])
 
         def copy_factor(u, v):
             for e in range(2):
                 r = 2 * v + e
-                target = factor[u][:, r, :].rearrange("s (p q) -> s p q", q=2)
-                source = f_ps[u, v][:, e, :, :].rearrange("s q p -> s p q")
-                if v == 0:
-                    nc.scalar.activation(target, source, ACT.Copy, scale=ts_col[:, r : r + 1])
-                else:
-                    nc.vector.tensor_scalar(target, source, ts_col[:, r : r + 1], None, ALU.mult)
+                target = factor[u][:, r, :].rearrange("o (p q) -> o p q", q=2)
+                source = f_ps[u, v][:, e, :, :].rearrange("o q p -> o p q")
+                nc.scalar.activation(target, source, ACT.Copy, scale=ts_col[:, r : r + 1])
 
         def mx_tiles(name, width, tag=None):
             codes = keep.tile([P, width], U32, name=name + "_codes", tag=tag or name + "_codes", align_bytes=64)
@@ -194,195 +183,193 @@ def tile_attend_gcbow_ns_pl_kernel(tc, eT, wT, ts, ux, y, coffs, posnoffs, sloto
 
         def quantize(operand, cols, grouped, fmt):
             nc.vector.quantize_mx(
-                out=operand[0][:, cols].bitcast(fmt), scales=operand[1][:, cols], in_=grouped.rearrange("p c l -> p (c l)"))
+                out=operand[0][:, cols].bitcast(fmt), scales=operand[1][:, cols], in_=grouped.rearrange("p col l -> p (col l)"))
 
         s_mx = mx_tiles("s", POS)
         g_mx = mx_tiles("g", POS)
         s_bf = keep.tile([P, POS, LANES], BF16, name="s_bf", align_bytes=64)
         g_bf = keep.tile([P, POS, LANES], BF16, name="g_bf", align_bytes=64)
-        chunks = [slice(P * c, P * (c + 1)) for c in range(LANES)]
-        pair_view = pairs[:].rearrange("p t (k i j) -> p k t i j", i=2, j=2)
+        chunks = [slice(P * ch, P * (ch + 1)) for ch in range(LANES)]
+        pair_view = pairs[:].rearrange("p t (k run j) -> p k t run j", run=2, j=2)
 
-        def pair_sum(c):
-            ks = slice(P // 2 * c, P // 2 * (c + 1))
+        def pair_sum(ch):
+            ks = slice(P // 2 * ch, P // 2 * (ch + 1))
             nc.vector.tensor_tensor(
-                s_bf[:, chunks[c], :].rearrange("p (k i) t -> p k t i", i=2),
+                s_bf[:, chunks[ch], :].rearrange("p (k run) t -> p k t run", run=2),
                 pair_view[:, ks, :, :, 0], pair_view[:, ks, :, :, 1], ALU.add)
 
-        def quantize_s(c):
-            quantize(s_mx, chunks[c], s_bf[:, chunks[c], :], E4M3)
+        def quantize_s(ch):
+            quantize(s_mx, chunks[ch], s_bf[:, chunks[ch], :], E4M3)
 
         sig = {}
+        scores = {}
 
-        def score(c):
-            a_ps = banks.tile([P, LANES, P], F32, name="a_ps", tag="bank%d" % (4, 0, 1, 2)[c])
+        def score(ch):
+            scores[ch] = banks.tile([P, LANES, P], F32, name="a_ps", tag="bank%d" % (LANES + ch))
             for r in range(LANES):
                 nc.tensor.matmul_mx(
-                    out=a_ps[:, r, :], lhsT=wd_mx[0][:, chunks[r]].bitcast(E4M3), lhsT_scale=wd_mx[1][:, chunks[r]],
-                    rhs=s_mx[0][:, chunks[c]].bitcast(E4M3), rhs_scale=s_mx[1][:, chunks[c]], start=True, stop=True)
-            z = keep.tile([P, LANES, P], F32, name="z%d" % c, align_bytes=64)
-            sig[c] = keep.tile([P, LANES, P], F32, name="sig%d" % c, align_bytes=64)
-            step = P // 2 if c == 0 else P
+                    out=scores[ch][:, r, :], lhsT=wd_mx[0][:, chunks[r]].bitcast(E4M3), lhsT_scale=wd_mx[1][:, chunks[r]],
+                    rhs=s_mx[0][:, chunks[ch]].bitcast(E4M3), rhs_scale=s_mx[1][:, chunks[ch]], start=True, stop=True)
+
+        def squash(ch):
+            z = keep.tile([P, LANES, P], F32, name="z%d" % ch, align_bytes=64)
+            sig[ch] = keep.tile([P, LANES, P], F32, name="sig%d" % ch, align_bytes=64)
+            step = P // 2 if ch == 0 else P
             for x in range(0, P, step):
                 cols = slice(x, x + step)
-                nc.vector.tensor_tensor(z[:, :, cols], a_ps[:, :, cols], factor[c // 2][:, :, chunks[c % 2]][:, :, cols], ALU.mult)
-                nc.scalar.activation(sig[c][:, :, cols], z[:, :, cols], ACT.Sigmoid, scale=0.5)
+                nc.vector.tensor_tensor(
+                    z[:, :, cols], scores[ch][:, :, cols], factor[ch // 2][:, :, chunks[ch % 2]][:, :, cols], ALU.mult)
+                nc.scalar.activation(sig[ch][:, :, cols], z[:, :, cols], ACT.Sigmoid, scale=0.5)
 
-        def loss_gradient(c):
-            engine = nc.gpsimd if c == 0 else nc.vector
-            step = P // 2 if c == 0 else P
+        def loss_gradient(ch):
+            engine = nc.gpsimd if ch == 0 else nc.vector
+            step = P // 2 if ch == 0 else P
             for x in range(0, P, step):
                 cols = slice(x, x + step)
                 engine.tensor_tensor(
-                    g_bf[:, chunks[c], :][:, cols, :].rearrange("s (k i) r -> s k r i", i=LINE),
-                    sig[c][:, :, cols].rearrange("s r (k i) -> s k r i", i=LINE),
-                    factor[c // 2][:, :, chunks[c % 2]][:, :, cols].rearrange("s r (k i) -> s k r i", i=LINE), ALU.mult)
+                    g_bf[:, chunks[ch], :][:, cols, :].rearrange("o (k run) r -> o k r run", run=LINE),
+                    sig[ch][:, :, cols].rearrange("o r (k run) -> o k r run", run=LINE),
+                    factor[ch // 2][:, :, chunks[ch % 2]][:, :, cols].rearrange("o r (k run) -> o k r run", run=LINE), ALU.mult)
 
         pair_sum(0)
-        for c in range(1, LANES):
-            pair_sum(c)
-            quantize_s(c - 1)
-        weave_w(0)
+        for ch in range(1, LANES):
+            pair_sum(ch)
+            quantize_s(ch - 1)
+        sign_labels(0)
         quantize_s(3)
-        lay_w(0, "w_lane2")
+        sign_labels(1)
+        turn_labels(0)
+        weave_w(0)
+        wi_mx = {0: mx_tiles("wi0", 2 * P)}
+        quantize(wi_mx[0], slice(0, 2 * P), w_by_i[0][:], E4M3)
+        sign_labels(2)
         gather_w(on_vector, LANES - 1, 0, OUT_SLOTS // 2)
         gather_w(on_scalar, LANES - 1, OUT_SLOTS // 2, OUT_SLOTS)
-        wi_mx = {0: mx_tiles("wi0", 2 * P, "w_lane3")}
-        quantize(wi_mx[0], slice(0, 2 * P), w_by_i[0][:], E4M3)
-        weave_w(1)
-        sign_labels(0)
-        sign_labels(1)
-        wd_mx = mx_tiles("wd", OUT_SLOTS, "y_part1")
-        quantize(wd_mx, slice(0, OUT_SLOTS), w_by_d[:], E4M3)
-        turn_labels(0)
+        factor[0] = keep.tile([P, LANES, POS // 2], F32, name="factor0", tag="w_lane3", align_bytes=64)
+        factor[1] = keep.tile([P, LANES, POS // 2], F32, name="factor1", align_bytes=64)
         copy_factor(0, 0)
         copy_factor(0, 1)
-        score(0)
+        sign_labels(3)
+        weave_w(1)
         turn_labels(1)
         copy_factor(1, 0)
-        score(1)
         copy_factor(1, 1)
-        score(2)
-        score(3)
-        turn_w(1)
-        lay_w(1, "z3")
+        wd_mx = mx_tiles("wd", OUT_SLOTS)
+        quantize(wd_mx, slice(0, OUT_SLOTS), w_by_d[:], E4M3)
+        for ch in range(LANES):
+            score(ch)
+        squash(0)
+        squash(1)
         loss_gradient(0)
+        squash(2)
+        squash(3)
+        turn_w(1, 3)
+        lay_w(1, "z3")
         loss_gradient(1)
         loss_gradient(2)
         quantize(g_mx, slice(0, 2 * P), g_bf[:, 0 : 2 * P, :], E5M2)
 
-        a, b, c, d = ORDER
-
-        def part_of_dh(j, lo, hi, bank, on_act):
-            cols = slice(lo, hi)
+        def multiply_dh(t, lo, hi, bank):
             dh_ps = banks.tile([P, hi - lo], F32, name="dh_ps", tag="bank%d" % bank)
+            codes, scales = wi_mx[t // 2]
             nc.tensor.matmul_mx(
-                out=dh_ps[:], lhsT=wi_mx[j // 2][0][:, chunks[j % 2]].bitcast(E4M3), lhsT_scale=wi_mx[j // 2][1][:, chunks[j % 2]],
-                rhs=g_mx[0][:, cols].bitcast(E5M2), rhs_scale=g_mx[1][:, cols], start=True, stop=True)
-            if on_act:
-                nc.scalar.activation(dh[j][:, cols], dh_ps[:], ACT.Copy, scale=0.5)
-            else:
-                nc.vector.tensor_scalar(dh[j][:, cols], dh_ps[:], 0.5, None, ALU.mult)
+                out=dh_ps[:], lhsT=codes[:, chunks[t % 2]].bitcast(E4M3), lhsT_scale=scales[:, chunks[t % 2]],
+                rhs=g_mx[0][:, lo:hi].bitcast(E5M2), rhs_scale=g_mx[1][:, lo:hi], start=True, stop=True)
+            return dh[t][:, lo:hi], dh_ps[:]
 
-        part_of_dh(a, 0, 2 * P, 4, True)
-        part_of_dh(b, 0, 2 * P, 5, True)
+        def halve_on_scalar(target, source):
+            nc.scalar.activation(target, source, ACT.Copy, scale=0.5)
+
+        def halve_on_vector(target, source):
+            nc.vector.tensor_scalar(target, source, 0.5, None, ALU.mult)
+
+        halve_on_scalar(*multiply_dh(0, 0, 2 * P, 0))
+        halve_on_scalar(*multiply_dh(1, 0, 2 * P, 1))
         loss_gradient(3)
         quantize(g_mx, chunks[2], g_bf[:, chunks[2], :], E5M2)
-        part_of_dh(a, 2 * P, 3 * P, 2, True)
-        part_of_dh(b, 2 * P, 3 * P, 6, True)
+        halve_on_scalar(*multiply_dh(0, 2 * P, 3 * P, 2))
+        halve_on_scalar(*multiply_dh(1, 2 * P, 3 * P, 4))
         quantize(g_mx, chunks[3], g_bf[:, chunks[3], :], E5M2)
         wi_mx[1] = mx_tiles("wi1", 2 * P, "g_bf")
         quantize(wi_mx[1], slice(0, 2 * P), w_by_i[1][:], E4M3)
-        part_of_dh(b, 3 * P, POS, 7, False)
-        part_of_dh(a, 3 * P, POS, 3, True)
-        whole = {}
-        for j, bank in ((c, 0), (d, 1)):
-            whole[j] = banks.tile([P, POS], F32, name="dh_whole", tag="bank%d" % bank)
-            nc.tensor.matmul_mx(
-                out=whole[j][:], lhsT=wi_mx[j // 2][0][:, chunks[j % 2]].bitcast(E4M3), lhsT_scale=wi_mx[j // 2][1][:, chunks[j % 2]],
-                rhs=g_mx[0][:].bitcast(E5M2), rhs_scale=g_mx[1][:], start=True, stop=True)
+        halve_on_vector(*multiply_dh(1, 3 * P, POS, 5))
+        halve_on_scalar(*multiply_dh(0, 3 * P, POS, 6))
+        dh_lane2 = multiply_dh(2, 0, POS, 7)
+        dh_lane3 = multiply_dh(3, 0, POS, 0)
+
         out_bf = keep.tile([P, WORDS, LANES], BF16, name="out_bf", tag="pairs_then_out", align_bytes=64)
         lanes_bf = keep.tile([P, LANES, WORDS], BF16, name="lanes_bf", tag="e_lane0", align_bytes=64)
-        de = {j: keep.tile([P, SLOTS], F32, name="de%d" % j, tag="e_c%d" % j, align_bytes=64) for j in ORDER}
+        de = [keep.tile([P, SLOTS], F32, name="de%d" % t, tag="e_c%d" % t, align_bytes=64) for t in range(LANES)]
 
-        def look_up(move, j, lo, hi):
-            move(de[j][:, lo:hi], dh[j][:].indirect(posn_list[:, lo // 16 : hi // 16]))
+        def look_up(move, t, lo, hi):
+            move(de[t][:, lo:hi], dh[t][:].indirect(posn_list[:, lo // 16 : hi // 16]))
 
-        def place(move, j, first, last):
-            lo, hi = CUTS[first], CUTS[last]
-            move(grad[j][:].indirect(ctx_list[:, lo // 16 : hi // 16]), de[j][:, lo:hi])
+        def place(move, t, lo, hi):
+            move(grad[t][:].indirect(ctx_list[:, lo // 16 : hi // 16]), de[t][:, lo:hi])
 
-        def store(queue, j):
-            queue.dma_start(out_rows[:, j, :], grad[j][:])
+        def store(queue, t):
+            queue.dma_start(out_rows[:, t, :], grad[t][:])
 
-        look_up(on_scalar, a, 0, CUTS[1])
-        look_up(on_scalar, a, CUTS[1], SLOTS)
-        look_up(on_vector, b, 0, SLOTS // 2)
-        look_up(on_vector, b, SLOTS // 2, SLOTS)
-        nc.vector.tensor_scalar(dh[c][:, 0:POS], whole[c][:], 0.5, None, ALU.mult)
-        nc.vector.tensor_scalar(dh[d][:, 0:POS], whole[d][:], 0.5, None, ALU.mult)
-        place(on_vector, b, 0, 3)
-        store(nc.sync, b)
-        nc.gpsimd.tensor_scalar(lanes_bf[:, b, :], grad[b][:], 1.0, 0.0, ALU.mult, ALU.add)
-        place(on_scalar, a, 0, 1)
-        look_up(on_scalar, c, 0, SLOTS)
-        place(on_scalar, a, 1, 2)
-        look_up(on_scalar, d, CUTS[0], CUTS[1])
-        place(on_scalar, a, 2, 3)
-        look_up(on_scalar, d, CUTS[1], CUTS[2])
-        store(nc.scalar, a)
-        nc.gpsimd.tensor_scalar(lanes_bf[:, a, :], grad[a][:], 1.0, 0.0, ALU.mult, ALU.add)
-        place(on_vector, c, 0, 3)
-        store(nc.sync, c)
-        place(on_scalar, d, 0, 1)
-        look_up(on_scalar, d, CUTS[2], CUTS[3])
-        place(on_scalar, d, 1, 2)
-        place(on_scalar, d, 2, 3)
-        store(nc.sync, d)
-        mine = slice(0, SPLIT)
-        theirs = slice(SPLIT, WORDS)
-        nc.vector.tensor_copy(lanes_bf[:, c, :], grad[c][:])
-        for cols, lanes in ((theirs, slice(0, 2)), (mine, slice(0, 3))):
-            nc.vector.tensor_copy(
-                out_bf[:, cols, lanes].rearrange("p (k i) t -> p k t i", i=LINE),
-                lanes_bf[:, lanes, cols].rearrange("p t (k i) -> p k t i", i=LINE))
+        def round_on_gpsimd(t):
+            nc.gpsimd.tensor_scalar(lanes_bf[:, t, :], grad[t][:], 1.0, 0.0, ALU.mult, ALU.add)
+
+        look_up(on_scalar, 0, CUTS[0], CUTS[1])
+        look_up(on_scalar, 0, CUTS[1], CUTS[3])
+        look_up(on_vector, 1, 0, SLOTS // 2)
+        look_up(on_vector, 1, SLOTS // 2, SLOTS)
+        halve_on_vector(*dh_lane2)
+        place(on_vector, 1, 0, SLOTS)
+        store(nc.sync, 1)
+        round_on_gpsimd(1)
+        place(on_scalar, 0, CUTS[0], CUTS[1])
+        look_up(on_scalar, 2, 0, SLOTS)
+        place(on_scalar, 0, CUTS[1], CUTS[2])
+        halve_on_scalar(*dh_lane3)
+        place(on_scalar, 0, CUTS[2], CUTS[3])
+        look_up(on_scalar, 3, CUTS[0], CUTS[1])
+        look_up(on_scalar, 3, CUTS[1], CUTS[2])
+        store(nc.scalar, 0)
+        round_on_gpsimd(0)
+        place(on_vector, 2, 0, SLOTS)
+        store(nc.sync, 2)
+        place(on_scalar, 3, CUTS[0], CUTS[1])
+        look_up(on_scalar, 3, CUTS[2], CUTS[3])
+        place(on_scalar, 3, CUTS[1], CUTS[2])
+        place(on_scalar, 3, CUTS[2], CUTS[3])
+        store(nc.sync, 3)
+
+        nc.vector.tensor_copy(lanes_bf[:, 2, :], grad[2][:])
+        for cols, lanes in ((slice(SPLIT, WORDS), slice(0, 2)), (slice(0, SPLIT), slice(0, 3))):
+            nc.vector.tensor_copy(out_bf[:, cols, lanes], lanes_bf[:, lanes, cols].rearrange("p t col -> p col t"))
 
         out_codes = keep.tile([P, WORDS], U32, name="out_codes", align_bytes=64)
         out_scales = keep.tile([P, WORDS // 2], U8, name="out_scales", align_bytes=64)
-        words_hbm = out_1[0].rearrange("p c l -> p (c l)").bitcast(I32)
+        words_hbm = out_1[0].rearrange("p col l -> p (col l)").bitcast(I32)
         quarter = WORDS // 4
 
         def round_last(lo, hi):
-            nc.vector.tensor_copy(out_bf[:, lo:hi, d], grad[d][:, lo:hi])
+            nc.vector.tensor_copy(out_bf[:, lo:hi, 3], grad[3][:, lo:hi])
 
-        def pack(lo, hi):
-            upper = lo // (WORDS // 2)
-            first = upper * (WORDS // 2)
+        def pack_and_store(lo, hi):
+            upper, first = divmod(lo, WORDS // 2)
             nc.vector.quantize_mx(
-                out=out_codes[:, lo:hi].bitcast(E4M3), scales=out_scales[4 * upper :, lo - first : hi - first],
-                in_=out_bf[:, lo:hi, :].rearrange("p c l -> p (c l)"))
-
-        def store_words(lo, hi):
+                out=out_codes[:, lo:hi].bitcast(E4M3), scales=out_scales[4 * upper :, first : first + hi - lo],
+                in_=out_bf[:, lo:hi, :].rearrange("p col l -> p (col l)"))
             nc.sync.dma_start(words_hbm[:, lo:hi], out_codes[:, lo:hi].bitcast(I32))
 
-        nc.scalar.copy(lanes_bf[:, d, SPLIT : 3 * quarter], grad[d][:, SPLIT : 3 * quarter])
-        nc.scalar.copy(lanes_bf[:, d, 3 * quarter :], grad[d][:, 3 * quarter :])
+        nc.scalar.copy(lanes_bf[:, 3, SPLIT : 3 * quarter], grad[3][:, SPLIT : 3 * quarter])
+        nc.scalar.copy(lanes_bf[:, 3, 3 * quarter :], grad[3][:, 3 * quarter :])
         for lo, hi in ((SPLIT, 3 * quarter), (3 * quarter, WORDS - PIECE), (WORDS - PIECE, WORDS)):
-            nc.scalar.copy(out_bf[:, lo:hi, 2:4], lanes_bf[:, 2:4, lo:hi].rearrange("p t c -> p c t"))
+            nc.scalar.copy(out_bf[:, lo:hi, 2:4], lanes_bf[:, 2:4, lo:hi].rearrange("p t col -> p col t"))
         round_last(0, quarter)
         round_last(quarter, 2 * quarter)
-        pack(0, quarter)
-        store_words(0, quarter)
+        pack_and_store(0, quarter)
         round_last(2 * quarter, SPLIT)
-        pack(quarter, 2 * quarter)
-        store_words(quarter, 2 * quarter)
-        pack(2 * quarter, 3 * quarter)
-        store_words(2 * quarter, 3 * quarter)
-        pack(3 * quarter, WORDS - PIECE)
-        store_words(3 * quarter, WORDS - PIECE)
-        pack(WORDS - PIECE, WORDS)
-        store_words(WORDS - PIECE, WORDS)
-        scales_hbm = out_2[0].bitcast(I32).rearrange("f (a c) -> a f c", a=2)
+        pack_and_store(quarter, 2 * quarter)
+        pack_and_store(2 * quarter, 3 * quarter)
+        pack_and_store(3 * quarter, WORDS - PIECE)
+        pack_and_store(WORDS - PIECE, WORDS)
+        scales_hbm = out_2[0].bitcast(I32).rearrange("f (upper col) -> upper f col", upper=2)
         for group in range(4):
             nc.scalar.dma_start(
                 scales_hbm[:, 4 * group : 4 * group + 4, :], out_scales[32 * group : 32 * group + 8, :].bitcast(I32))

@@ -24,6 +24,7 @@ POS = 512
 OUT_SLOTS = 512
 LINE = 4
 CUTS = (0, 384, 768, SLOTS)
+LOOK3 = 448
 DH_COLUMNS = (656, 528, 1040, POS)
 SPLIT = 1152
 PIECE = 256
@@ -35,32 +36,44 @@ def tile_attend_gcbow_ns_pl_kernel(tc, eT, wT, ts, ux, y, coffs, posnoffs, sloto
         keep = stack.enter_context(tc.tile_pool(name="keep", bufs=1))
         banks = stack.enter_context(tc.psum_pool(name="banks", bufs=1))
 
-        ctx_list = keep.tile([P, SLOTS // 16], U16, name="ctx_list")
-        posn_list = keep.tile([P, SLOTS // 16], U16, name="posn_list")
-        slot_list = keep.tile([P, SLOTS // 16], U16, name="slot_list")
-        idx_list = keep.tile([P, OUT_SLOTS // 16], U16, name="idx_list")
+        def tile(name, shape, dtype, tag=None):
+            return keep.tile(shape, dtype, name=name, tag=tag or name, align_bytes=64)
+
+        def bank(name, shape, number):
+            return banks.tile(shape, F32, name=name, tag="bank%d" % number)
+
+        def on_scalar(out, in_):
+            nc.scalar.activation(out, in_, ACT.Copy)
+
+        on_vector = nc.vector.tensor_copy
+
+        def entries(offsets, lo, hi):
+            return offsets[:, lo // 16 : hi // 16]
+
+        ctx_list = tile("ctx_list", [P, SLOTS // 16], U16)
+        posn_list = tile("posn_list", [P, SLOTS // 16], U16)
+        slot_list = tile("slot_list", [P, SLOTS // 16], U16)
+        idx_list = tile("idx_list", [P, OUT_SLOTS // 16], U16)
         e_rows = eT.rearrange("(p t) col -> p t col", t=LANES)
         w_rows = wT.rearrange("(p t) col -> p t col", t=LANES)
         out_rows = out_0.rearrange("(p t) col -> p t col", t=LANES)
         y_rows = y.rearrange("(u p q) i -> p u q i", p=P, q=2)
         ux_rows = ux.rearrange("(u p q) one -> p u (q one)", p=P, q=2)
-        e_lane = [keep.tile([P, WORDS], F32, name="e_lane%d" % t, align_bytes=64)[:] for t in range(LANES)]
-        w_lane = [keep.tile([P, WORDS], F32, name="w_lane%d" % t, align_bytes=64)[:] for t in range(LANES)]
-        ts_table = keep.tile([P, WORDS], F32, name="ts_table")
-        y_part = [keep.tile([P, OUT_SLOTS], F32, name="y_part%d" % n, align_bytes=64) for n in range(LANES)]
-        ux_col = keep.tile([P, LANES], F32, name="ux_col")
-        minus_2ux = keep.tile([P, LANES], F32, name="minus_2ux")
-        identity = keep.tile([P, P], F32, name="identity")
-        e_c = [keep.tile([P, SLOTS], F32, name="e_c%d" % t, align_bytes=64) for t in range(LANES)]
-        dh = [keep.tile([P, DH_COLUMNS[t]], F32, name="dh%d" % t, align_bytes=64) for t in range(LANES)]
-        grad = [keep.tile([P, WORDS], F32, name="grad%d" % t, align_bytes=64) for t in range(LANES)]
+        e_lane = [tile("e_lane%d" % t, [P, WORDS], F32) for t in range(LANES)]
+        w_lane = [tile("w_lane%d" % t, [P, WORDS], F32) for t in range(LANES)]
+        ts_table = tile("ts_table", [P, WORDS], F32)
+        y_half = [tile("y_half%d" % u, [P, 2, OUT_SLOTS], F32) for u in range(2)]
+        ux_col = tile("ux_col", [P, LANES], F32)
+        minus_2ux = tile("minus_2ux", [P, LANES], F32)
+        identity = tile("identity", [P, P], F32)
+        e_c = [tile("e_c%d" % t, [P, SLOTS], F32) for t in range(LANES)]
+        dh = [tile("dh%d" % t, [P, DH_COLUMNS[t]], F32) for t in range(LANES)]
+        grad = [tile("grad%d" % t, [P, WORDS], F32) for t in range(LANES)]
 
         nc.vector.memset(ts_table[0 : P - 1, :], 0.0)
-
-        warm = keep.tile([P, 2], F32, name="warm")
+        warm = tile("warm", [P, 2], F32)
         nc.vector.memset(warm[:, 0:1], 0.0)
         nc.scalar.activation(warm[:, 1:2], warm[:, 0:1], ACT.Sigmoid)
-
         make_identity(nc, identity[:])
         for t in range(LANES):
             nc.gpsimd.memset(grad[t][:], 0.0)
@@ -69,211 +82,155 @@ def tile_attend_gcbow_ns_pl_kernel(tc, eT, wT, ts, ux, y, coffs, posnoffs, sloto
 
         nc.sync.dma_start(ts_table[P - 1 : P, :], ts[0:1, :])
         nc.sync.dma_start(idx_list[:], offs)
-        nc.sync.dma_start(e_lane[0], e_rows[:, 0, :])
+        nc.sync.dma_start(e_lane[0][:], e_rows[:, 0, :])
         nc.sync.dma_start(ctx_list[:], coffs)
         nc.sync.dma_start(slot_list[:], slotoffs)
-        for t in range(1, LANES):
-            nc.sync.dma_start(e_lane[t], e_rows[:, t, :])
         nc.sync.dma_start(ux_col[:].rearrange("p (u q) -> p u q", q=2), ux_rows)
-        nc.sync.dma_start(w_lane[0], w_rows[:, 0, :])
-        nc.sync.dma_start(w_lane[1], w_rows[:, 1, :])
-        nc.sync.dma_start(y_part[0][:], y_rows[:, 0, 0, :])
-        nc.sync.dma_start(y_part[1][:], y_rows[:, 0, 1, :])
-        for t in range(2, LANES):
-            nc.sync.dma_start(w_lane[t], w_rows[:, t, :])
-            nc.sync.dma_start(y_part[t][:], y_rows[:, 1, t - 2, :])
+        nc.sync.dma_start(e_lane[1][:], e_rows[:, 1, :])
+        for u in range(2):
+            nc.sync.dma_start(e_lane[2 + u][:], e_rows[:, 2 + u, :])
+            nc.sync.dma_start(y_half[u][:], y_rows[:, u])
+        for t in range(LANES):
+            nc.sync.dma_start(w_lane[t][:], w_rows[:, t, :])
         nc.sync.dma_start(posn_list[:], posnoffs)
 
-        pairs = keep.tile([P, LANES, SLOTS], F32, name="pairs", tag="pairs_then_out", align_bytes=64)
-        w_by_d = keep.tile([P, OUT_SLOTS, LANES], BF16, name="w_by_d", align_bytes=64)
-        ts_i = keep.tile([P, OUT_SLOTS], F32, name="ts_i")
-        signed_ux = [keep.tile([P, OUT_SLOTS], F32, name="signed_ux%d" % n) for n in range(POS // P)]
-        factor = {}
+        ts_i = tile("ts_i", [P, OUT_SLOTS], F32)
+        on_vector(ts_i[:], ts_table[:].indirect(idx_list[:]))
+        ts_ps = bank("ts_ps", [P, LANES, P], 4)
+        for r in range(LANES):
+            nc.tensor.transpose(ts_ps[:, r, :], ts_i[:, r::LANES], identity[:])
+        ts_col = tile("ts_col", [P, LANES], F32)
+        nc.scalar.copy(ts_col[:], ts_ps[:, :, P - 1])
 
-        def listed(row):
-            return row.rearrange("p (k run r) -> p k r run", r=LANES, run=LINE)
-
-        def dealt(row):
-            return row.rearrange("p (r k run) -> p k r run", r=LANES, run=LINE)
-
-        def on_scalar(out, in_):
-            nc.scalar.activation(out, in_, ACT.Copy)
-
-        on_vector = nc.vector.tensor_copy
-
-        def gather_context(move, t, half):
-            lo, hi = SLOTS // 2 * half, SLOTS // 2 * (half + 1)
-            move(e_c[t][:, lo:hi], e_lane[t].indirect(ctx_list[:, lo // 16 : hi // 16]))
-
-        def gather_pairs(move, t, half):
-            lo, hi = SLOTS // 2 * half, SLOTS // 2 * (half + 1)
-            move(pairs[:, t, lo:hi], e_c[t][:].indirect(slot_list[:, lo // 16 : hi // 16]))
-
-        nc.vector.tensor_copy(ts_i[:], ts_table[:].indirect(idx_list[:]))
+        pairs = tile("pairs", [P, LANES, SLOTS], F32, "pairs_then_out")
+        halves = ((on_vector, 0, SLOTS // 2), (on_scalar, SLOTS // 2, SLOTS))
         for t in range(LANES):
-            gather_context(on_vector, t, 0)
-            gather_context(on_scalar, t, 1)
-            gather_pairs(on_vector, t, 0)
-            gather_pairs(on_scalar, t, 1)
+            for move, lo, hi in halves:
+                move(e_c[t][:, lo:hi], e_lane[t][:].indirect(entries(ctx_list, lo, hi)))
+            for move, lo, hi in halves:
+                move(pairs[:, t, lo:hi], e_c[t][:].indirect(entries(slot_list, lo, hi)))
 
-        w_listed = [keep.tile([P, 2, OUT_SLOTS], BF16, name="w_listed%d" % v, align_bytes=64) for v in range(2)]
-        w_ps = {}
+        nc.gpsimd.tensor_scalar(minus_2ux[:], ux_col[:], -2.0, 0.0, ALU.mult, ALU.add)
+        signed_ux = [tile("signed_ux%d" % n, [P, OUT_SLOTS], F32) for n in range(LANES)]
+        factor = [tile("factor%d" % u, [P, LANES, POS // 2], F32) for u in range(2)]
+        for u in range(2):
+            for q in range(2):
+                n = 2 * u + q
+                nc.gpsimd.tensor_scalar(
+                    signed_ux[n][:].rearrange("p (r k run) -> p k r run", r=LANES, run=LINE),
+                    y_half[u][:, q, :].rearrange("p (k run r) -> p k r run", r=LANES, run=LINE),
+                    minus_2ux[:, n : n + 1], ux_col[:, n : n + 1], ALU.mult, ALU.add)
+            f_ps = [bank("f_ps", [P, 2, 2, P], 2 * u + v) for v in range(2)]
+            for q in range(2):
+                for r in range(LANES):
+                    nc.tensor.transpose(f_ps[r // 2][:, r % 2, q, :], signed_ux[2 * u + q][:, P * r : P * (r + 1)], identity[:])
+            for r in range(LANES):
+                nc.scalar.activation(
+                    factor[u][:, r, :].rearrange("o (p q) -> o p q", q=2), f_ps[r // 2][:, r % 2, :, :].rearrange("o q p -> o p q"),
+                    ACT.Copy, scale=ts_col[:, r : r + 1])
+
+        def mx_tiles(name, width, tag=None):
+            return tile(name + "_codes", [P, width], U32, tag), tile(name + "_scales", [P, width], U8)
+
+        def quantize(operand, cols, grouped, fmt):
+            nc.vector.quantize_mx(
+                out=operand[0][:, cols].bitcast(fmt), scales=operand[1][:, cols], in_=grouped.rearrange("p col l -> p (col l)"))
+
+        chunks = [slice(P * ch, P * (ch + 1)) for ch in range(LANES)]
+
+        s_mx = mx_tiles("s", POS)
+        s_bf = tile("s_bf", [P, POS, LANES], BF16)
+        pair_view = pairs[:].rearrange("p t (k run j) -> p k t run j", run=2, j=2)
+        for ch in range(LANES + 1):
+            if ch < LANES:
+                ks = slice(P // 2 * ch, P // 2 * (ch + 1))
+                nc.vector.tensor_tensor(
+                    s_bf[:, chunks[ch], :].rearrange("p (k run) t -> p k t run", run=2),
+                    pair_view[:, ks, :, :, 0], pair_view[:, ks, :, :, 1], ALU.add)
+            if ch > 0:
+                quantize(s_mx, chunks[ch - 1], s_bf[:, chunks[ch - 1], :], E4M3)
+
+        w_listed = [tile("w_listed%d" % v, [P, 2, OUT_SLOTS], BF16) for v in range(2)]
+        w_by_d = tile("w_by_d", [P, OUT_SLOTS, LANES], BF16)
         w_by_i = {}
+        w_ps = {}
+        wi_mx = {0: mx_tiles("wi0", 2 * P)}
+        wd_mx = mx_tiles("wd", OUT_SLOTS)
 
         def gather_w(move, t, lo, hi):
-            move(w_listed[t // 2][:, t % 2, lo:hi], w_lane[t].indirect(idx_list[:, lo // 16 : hi // 16]))
+            move(w_listed[t // 2][:, t % 2, lo:hi], w_lane[t][:].indirect(entries(idx_list, lo, hi)))
 
-        def turn_w(v, bank):
-            w_ps[v] = banks.tile([P, 2, 2, P], F32, name="w_ps%d" % v, tag="bank%d" % bank)
+        def turn_w(v, number):
+            w_ps[v] = bank("w_ps", [P, 2, 2, P], number)
             words = w_listed[v][:].rearrange("p e col -> p (e col)").bitcast(F32)
             for e in range(2):
                 for odd in range(2):
                     nc.tensor.transpose(w_ps[v][:, e, odd, :], words[:, 2 * P * e + odd : 2 * P * (e + 1) : 2], identity[:])
 
         def lay_w(v, tag):
-            w_by_i[v] = keep.tile([P, 2 * P, LANES], BF16, name="w_by_i%d" % v, tag=tag, align_bytes=64)
-            words = w_by_i[v][:].rearrange("o col r -> o (col r)").bitcast(F32)
-            nc.scalar.copy(words.rearrange("o (e p odd) -> o e p odd", e=2, odd=2), w_ps[v][:].rearrange("o e odd p -> o e p odd"))
+            w_by_i[v] = tile("w_by_i%d" % v, [P, 2 * P, LANES], BF16, tag)
+            target = w_by_i[v][:].rearrange("o col r -> o (col r)").bitcast(F32)
+            nc.scalar.copy(target.rearrange("o (e p odd) -> o e p odd", e=2, odd=2), w_ps[v][:].rearrange("o e odd p -> o e p odd"))
 
-        def weave_w(v):
-            nc.vector.tensor_copy(
-                w_by_d[:, :, 2 * v : 2 * v + 2].rearrange("p (r k run) e -> p k r run e", r=LANES, run=2),
-                w_listed[v][:].rearrange("p e (k run r) -> p k r run e", r=LANES, run=2))
+        def weave_w(move, v, rs):
+            move(
+                w_by_d[:, :, 2 * v : 2 * v + 2].rearrange("p (r k run) e -> p k r run e", r=LANES, run=2)[:, :, rs],
+                w_listed[v][:].rearrange("p e (k run r) -> p k r run e", r=LANES, run=2)[:, :, rs])
 
-        for t in range(2):
-            gather_w(on_scalar, t, 0, OUT_SLOTS)
-        turn_w(0, 5)
-        lay_w(0, "w_by_i0")
+        gather_w(on_scalar, 0, 0, OUT_SLOTS)
+        gather_w(on_vector, 1, 0, OUT_SLOTS)
+        turn_w(0, 1)
+        weave_w(on_vector, 0, slice(0, LANES))
         gather_w(on_scalar, 2, 0, OUT_SLOTS)
+        gather_w(on_vector, 3, 0, OUT_SLOTS // 2)
+        gather_w(on_scalar, 3, OUT_SLOTS // 2, OUT_SLOTS)
+        weave_w(on_vector, 1, slice(0, 2))
+        weave_w(on_vector, 1, slice(2, 3))
+        weave_w(nc.scalar.copy, 1, slice(3, 4))
+        for half in range(2):
+            cols = slice(2 * P * half, 2 * P * (half + 1))
+            quantize(wd_mx, cols, w_by_d[:, cols, :], E4M3)
+        turn_w(1, 0)
+        lay_w(0, "w_lane3")
+        lay_w(1, "w_by_i1")
+        quantize(wi_mx[0], slice(0, 2 * P), w_by_i[0][:], E4M3)
 
-        ts_dealt = keep.tile([P, OUT_SLOTS], F32, name="ts_dealt")
-        nc.scalar.copy(dealt(ts_dealt[:]), listed(ts_i[:]))
-        nc.gpsimd.tensor_scalar(minus_2ux[:], ux_col[:], -2.0, 0.0, ALU.mult, ALU.add)
-        ts_ps = banks.tile([P, LANES, P], F32, name="ts_ps", tag="bank4")
-        for r in range(LANES):
-            nc.tensor.transpose(ts_ps[:, r, :], ts_dealt[:, P * r : P * (r + 1)], identity[:])
-        ts_col = keep.tile([P, LANES], F32, name="ts_col")
-        nc.scalar.copy(ts_col[:], ts_ps[:, :, P - 1])
-
-        def sign_labels(n):
-            nc.vector.tensor_scalar(
-                dealt(signed_ux[n][:]), listed(y_part[n][:]), minus_2ux[:, n : n + 1], ux_col[:, n : n + 1], ALU.mult, ALU.add)
-
-        f_ps = {}
-
-        def turn_labels(u):
-            for v in range(2):
-                f_ps[u, v] = banks.tile([P, 2, 2, P], F32, name="f_ps", tag="bank%d" % (2 * u + v))
-            for q in range(2):
-                for r in range(LANES):
-                    nc.tensor.transpose(
-                        f_ps[u, r // 2][:, r % 2, q, :], signed_ux[2 * u + q][:, P * r : P * (r + 1)], identity[:])
-
-        def copy_factor(u, v):
-            for e in range(2):
-                r = 2 * v + e
-                target = factor[u][:, r, :].rearrange("o (p q) -> o p q", q=2)
-                source = f_ps[u, v][:, e, :, :].rearrange("o q p -> o p q")
-                nc.scalar.activation(target, source, ACT.Copy, scale=ts_col[:, r : r + 1])
-
-        def mx_tiles(name, width, tag=None):
-            codes = keep.tile([P, width], U32, name=name + "_codes", tag=tag or name + "_codes", align_bytes=64)
-            scales = keep.tile([P, width], U8, name=name + "_scales", align_bytes=64)
-            return codes, scales
-
-        def quantize(operand, cols, grouped, fmt):
-            nc.vector.quantize_mx(
-                out=operand[0][:, cols].bitcast(fmt), scales=operand[1][:, cols], in_=grouped.rearrange("p col l -> p (col l)"))
-
-        s_mx = mx_tiles("s", POS)
         g_mx = mx_tiles("g", POS)
-        s_bf = keep.tile([P, POS, LANES], BF16, name="s_bf", align_bytes=64)
-        g_bf = keep.tile([P, POS, LANES], BF16, name="g_bf", align_bytes=64)
-        chunks = [slice(P * ch, P * (ch + 1)) for ch in range(LANES)]
-        pair_view = pairs[:].rearrange("p t (k run j) -> p k t run j", run=2, j=2)
-
-        def pair_sum(ch):
-            ks = slice(P // 2 * ch, P // 2 * (ch + 1))
-            nc.vector.tensor_tensor(
-                s_bf[:, chunks[ch], :].rearrange("p (k run) t -> p k t run", run=2),
-                pair_view[:, ks, :, :, 0], pair_view[:, ks, :, :, 1], ALU.add)
-
-        def quantize_s(ch):
-            quantize(s_mx, chunks[ch], s_bf[:, chunks[ch], :], E4M3)
-
-        sig = {}
-        scores = {}
-
-        def score(ch):
-            scores[ch] = banks.tile([P, LANES, P], F32, name="a_ps", tag="bank%d" % (LANES + ch))
+        g_bf = tile("g_bf", [P, POS, LANES], BF16)
+        scores = []
+        for ch in range(LANES):
+            scores.append(bank("a_ps", [P, LANES, P], LANES + ch))
             for r in range(LANES):
                 nc.tensor.matmul_mx(
                     out=scores[ch][:, r, :], lhsT=wd_mx[0][:, chunks[r]].bitcast(E4M3), lhsT_scale=wd_mx[1][:, chunks[r]],
                     rhs=s_mx[0][:, chunks[ch]].bitcast(E4M3), rhs_scale=s_mx[1][:, chunks[ch]], start=True, stop=True)
+        sig = [tile("sig%d" % ch, [P, LANES, P], F32, "signed_ux%d" % ch) for ch in range(LANES)]
+
+        def factor_of(ch, cols):
+            return factor[ch // 2][:, :, chunks[ch % 2]][:, :, cols]
+
+        def pieces(ch):
+            step = P // 2 if ch == 0 else P
+            return [slice(x, x + step) for x in range(0, P, step)]
 
         def squash(ch):
-            z = keep.tile([P, LANES, P], F32, name="z%d" % ch, align_bytes=64)
-            sig[ch] = keep.tile([P, LANES, P], F32, name="sig%d" % ch, align_bytes=64)
-            step = P // 2 if ch == 0 else P
-            for x in range(0, P, step):
-                cols = slice(x, x + step)
-                nc.vector.tensor_tensor(
-                    z[:, :, cols], scores[ch][:, :, cols], factor[ch // 2][:, :, chunks[ch % 2]][:, :, cols], ALU.mult)
+            z = tile("z%d" % ch, [P, LANES, P], F32)
+            for cols in pieces(ch):
+                nc.vector.tensor_tensor(z[:, :, cols], scores[ch][:, :, cols], factor_of(ch, cols), ALU.mult)
                 nc.scalar.activation(sig[ch][:, :, cols], z[:, :, cols], ACT.Sigmoid, scale=0.5)
 
         def loss_gradient(ch):
             engine = nc.gpsimd if ch == 0 else nc.vector
-            step = P // 2 if ch == 0 else P
-            for x in range(0, P, step):
-                cols = slice(x, x + step)
+            for cols in pieces(ch):
                 engine.tensor_tensor(
                     g_bf[:, chunks[ch], :][:, cols, :].rearrange("o (k run) r -> o k r run", run=LINE),
                     sig[ch][:, :, cols].rearrange("o r (k run) -> o k r run", run=LINE),
-                    factor[ch // 2][:, :, chunks[ch % 2]][:, :, cols].rearrange("o r (k run) -> o k r run", run=LINE), ALU.mult)
+                    factor_of(ch, cols).rearrange("o r (k run) -> o k r run", run=LINE), ALU.mult)
 
-        pair_sum(0)
-        for ch in range(1, LANES):
-            pair_sum(ch)
-            quantize_s(ch - 1)
-        sign_labels(0)
-        quantize_s(3)
-        sign_labels(1)
-        turn_labels(0)
-        weave_w(0)
-        wi_mx = {0: mx_tiles("wi0", 2 * P)}
-        quantize(wi_mx[0], slice(0, 2 * P), w_by_i[0][:], E4M3)
-        sign_labels(2)
-        gather_w(on_vector, LANES - 1, 0, OUT_SLOTS // 2)
-        gather_w(on_scalar, LANES - 1, OUT_SLOTS // 2, OUT_SLOTS)
-        factor[0] = keep.tile([P, LANES, POS // 2], F32, name="factor0", tag="w_lane3", align_bytes=64)
-        factor[1] = keep.tile([P, LANES, POS // 2], F32, name="factor1", align_bytes=64)
-        copy_factor(0, 0)
-        copy_factor(0, 1)
-        sign_labels(3)
-        weave_w(1)
-        turn_labels(1)
-        copy_factor(1, 0)
-        copy_factor(1, 1)
-        wd_mx = mx_tiles("wd", OUT_SLOTS)
-        quantize(wd_mx, slice(0, OUT_SLOTS), w_by_d[:], E4M3)
-        for ch in range(LANES):
-            score(ch)
-        squash(0)
-        squash(1)
-        loss_gradient(0)
-        squash(2)
-        squash(3)
-        turn_w(1, 3)
-        lay_w(1, "z3")
-        loss_gradient(1)
-        loss_gradient(2)
-        quantize(g_mx, slice(0, 2 * P), g_bf[:, 0 : 2 * P, :], E5M2)
-
-        def multiply_dh(t, lo, hi, bank):
-            dh_ps = banks.tile([P, hi - lo], F32, name="dh_ps", tag="bank%d" % bank)
-            codes, scales = wi_mx[t // 2]
+        def multiply_dh(t, lo, hi, number):
+            dh_ps = bank("dh_ps", [P, hi - lo], number)
             nc.tensor.matmul_mx(
-                out=dh_ps[:], lhsT=codes[:, chunks[t % 2]].bitcast(E4M3), lhsT_scale=scales[:, chunks[t % 2]],
+                out=dh_ps[:], lhsT=wi_mx[t // 2][0][:, chunks[t % 2]].bitcast(E4M3), lhsT_scale=wi_mx[t // 2][1][:, chunks[t % 2]],
                 rhs=g_mx[0][:, lo:hi].bitcast(E5M2), rhs_scale=g_mx[1][:, lo:hi], start=True, stop=True)
             return dh[t][:, lo:hi], dh_ps[:]
 
@@ -283,36 +240,45 @@ def tile_attend_gcbow_ns_pl_kernel(tc, eT, wT, ts, ux, y, coffs, posnoffs, sloto
         def halve_on_vector(target, source):
             nc.vector.tensor_scalar(target, source, 0.5, None, ALU.mult)
 
+        for ch in range(LANES):
+            squash(ch)
+        for ch in range(3):
+            loss_gradient(ch)
+        quantize(g_mx, slice(0, 2 * P), g_bf[:, 0 : 2 * P, :], E5M2)
         halve_on_scalar(*multiply_dh(0, 0, 2 * P, 0))
         halve_on_scalar(*multiply_dh(1, 0, 2 * P, 1))
         loss_gradient(3)
         quantize(g_mx, chunks[2], g_bf[:, chunks[2], :], E5M2)
         halve_on_scalar(*multiply_dh(0, 2 * P, 3 * P, 2))
-        halve_on_scalar(*multiply_dh(1, 2 * P, 3 * P, 4))
+        halve_on_scalar(*multiply_dh(1, 2 * P, 3 * P, 3))
         quantize(g_mx, chunks[3], g_bf[:, chunks[3], :], E5M2)
         wi_mx[1] = mx_tiles("wi1", 2 * P, "g_bf")
         quantize(wi_mx[1], slice(0, 2 * P), w_by_i[1][:], E4M3)
-        halve_on_vector(*multiply_dh(1, 3 * P, POS, 5))
-        halve_on_scalar(*multiply_dh(0, 3 * P, POS, 6))
-        dh_lane2 = multiply_dh(2, 0, POS, 7)
-        dh_lane3 = multiply_dh(3, 0, POS, 0)
+        halve_on_vector(*multiply_dh(1, 3 * P, POS, 4))
+        halve_on_scalar(*multiply_dh(0, 3 * P, POS, 5))
+        dh_lane2 = multiply_dh(2, 0, POS, 6)
+        dh_lane3 = multiply_dh(3, 0, POS, 7)
 
-        out_bf = keep.tile([P, WORDS, LANES], BF16, name="out_bf", tag="pairs_then_out", align_bytes=64)
-        lanes_bf = keep.tile([P, LANES, WORDS], BF16, name="lanes_bf", tag="e_lane0", align_bytes=64)
-        de = [keep.tile([P, SLOTS], F32, name="de%d" % t, tag="e_c%d" % t, align_bytes=64) for t in range(LANES)]
+        out_bf = tile("out_bf", [P, WORDS, LANES], BF16, "pairs_then_out")
+        lanes_bf = tile("lanes_bf", [P, LANES, WORDS], BF16, "e_lane0")
+        de = [tile("de%d" % t, [P, SLOTS], F32, "e_c%d" % t) for t in range(LANES)]
 
         def look_up(move, t, lo, hi):
-            move(de[t][:, lo:hi], dh[t][:].indirect(posn_list[:, lo // 16 : hi // 16]))
+            move(de[t][:, lo:hi], dh[t][:].indirect(entries(posn_list, lo, hi)))
 
         def place(move, t, lo, hi):
-            move(grad[t][:].indirect(ctx_list[:, lo // 16 : hi // 16]), de[t][:, lo:hi])
+            move(grad[t][:].indirect(entries(ctx_list, lo, hi)), de[t][:, lo:hi])
 
         def store(queue, t):
             queue.dma_start(out_rows[:, t, :], grad[t][:])
 
-        def round_on_gpsimd(t):
-            nc.gpsimd.tensor_scalar(lanes_bf[:, t, :], grad[t][:], 1.0, 0.0, ALU.mult, ALU.add)
+        def on_gpsimd(out, in_):
+            nc.gpsimd.tensor_scalar(out, in_, 1.0, 0.0, ALU.mult, ALU.add)
 
+        def lay(move, lo, hi, lanes):
+            move(out_bf[:, lo:hi, lanes], lanes_bf[:, lanes, lo:hi].rearrange("p t col -> p col t"))
+
+        quarter = WORDS // 4
         look_up(on_scalar, 0, CUTS[0], CUTS[1])
         look_up(on_scalar, 0, CUTS[1], CUTS[3])
         look_up(on_vector, 1, 0, SLOTS // 2)
@@ -320,16 +286,16 @@ def tile_attend_gcbow_ns_pl_kernel(tc, eT, wT, ts, ux, y, coffs, posnoffs, sloto
         halve_on_vector(*dh_lane2)
         place(on_vector, 1, 0, SLOTS)
         store(nc.sync, 1)
-        round_on_gpsimd(1)
+        on_gpsimd(lanes_bf[:, 1, :], grad[1][:])
         place(on_scalar, 0, CUTS[0], CUTS[1])
-        look_up(on_scalar, 2, 0, SLOTS)
-        place(on_scalar, 0, CUTS[1], CUTS[2])
         halve_on_scalar(*dh_lane3)
+        place(on_scalar, 0, CUTS[1], CUTS[2])
+        look_up(on_scalar, 2, 0, SLOTS)
         place(on_scalar, 0, CUTS[2], CUTS[3])
-        look_up(on_scalar, 3, CUTS[0], CUTS[1])
-        look_up(on_scalar, 3, CUTS[1], CUTS[2])
+        look_up(on_vector, 3, 0, LOOK3)
+        look_up(on_scalar, 3, LOOK3, CUTS[2])
         store(nc.scalar, 0)
-        round_on_gpsimd(0)
+        on_gpsimd(lanes_bf[:, 0, :], grad[0][:])
         place(on_vector, 2, 0, SLOTS)
         store(nc.sync, 2)
         place(on_scalar, 3, CUTS[0], CUTS[1])
@@ -337,18 +303,18 @@ def tile_attend_gcbow_ns_pl_kernel(tc, eT, wT, ts, ux, y, coffs, posnoffs, sloto
         place(on_scalar, 3, CUTS[1], CUTS[2])
         place(on_scalar, 3, CUTS[2], CUTS[3])
         store(nc.sync, 3)
+        closing = ((SPLIT, 3 * quarter), (3 * quarter, WORDS - PIECE), (WORDS - PIECE, WORDS))
+        for lo, hi in closing:
+            lay(on_gpsimd, lo, hi, slice(0, 2))
+        on_vector(lanes_bf[:, 2, :], grad[2][:])
+        lay(on_vector, 0, SPLIT, slice(0, 3))
 
-        nc.vector.tensor_copy(lanes_bf[:, 2, :], grad[2][:])
-        for cols, lanes in ((slice(SPLIT, WORDS), slice(0, 2)), (slice(0, SPLIT), slice(0, 3))):
-            nc.vector.tensor_copy(out_bf[:, cols, lanes], lanes_bf[:, lanes, cols].rearrange("p t col -> p col t"))
-
-        out_codes = keep.tile([P, WORDS], U32, name="out_codes", align_bytes=64)
-        out_scales = keep.tile([P, WORDS // 2], U8, name="out_scales", align_bytes=64)
+        out_codes = tile("out_codes", [P, WORDS], U32, "e_lane1")
+        out_scales = tile("out_scales", [P, WORDS // 2], U8)
         words_hbm = out_1[0].rearrange("p col l -> p (col l)").bitcast(I32)
-        quarter = WORDS // 4
 
         def round_last(lo, hi):
-            nc.vector.tensor_copy(out_bf[:, lo:hi, 3], grad[3][:, lo:hi])
+            on_vector(out_bf[:, lo:hi, 3], grad[3][:, lo:hi])
 
         def pack_and_store(lo, hi):
             upper, first = divmod(lo, WORDS // 2)
@@ -359,8 +325,8 @@ def tile_attend_gcbow_ns_pl_kernel(tc, eT, wT, ts, ux, y, coffs, posnoffs, sloto
 
         nc.scalar.copy(lanes_bf[:, 3, SPLIT : 3 * quarter], grad[3][:, SPLIT : 3 * quarter])
         nc.scalar.copy(lanes_bf[:, 3, 3 * quarter :], grad[3][:, 3 * quarter :])
-        for lo, hi in ((SPLIT, 3 * quarter), (3 * quarter, WORDS - PIECE), (WORDS - PIECE, WORDS)):
-            nc.scalar.copy(out_bf[:, lo:hi, 2:4], lanes_bf[:, 2:4, lo:hi].rearrange("p t col -> p col t"))
+        for lo, hi in closing:
+            lay(nc.scalar.copy, lo, hi, slice(2, 4))
         round_last(0, quarter)
         round_last(quarter, 2 * quarter)
         pack_and_store(0, quarter)

@@ -26,6 +26,9 @@ LINE = 4
 CUTS = (0, 384, 768, SLOTS)
 LOOK3 = 448
 DH_COLUMNS = (656, 528, 1040, POS)
+CONTEXT_ON_VECTOR = (512, 768, SLOTS, SLOTS)
+PAIRS_ON_VECTOR = (256, 0, 0, 512)
+SPARE = 16
 SPLIT = 1152
 PIECE = 256
 
@@ -57,16 +60,16 @@ def tile_attend_gcbow_ns_pl_kernel(tc, eT, wT, ts, ux, y, coffs, posnoffs, sloto
         e_rows = eT.rearrange("(p t) col -> p t col", t=LANES)
         w_rows = wT.rearrange("(p t) col -> p t col", t=LANES)
         out_rows = out_0.rearrange("(p t) col -> p t col", t=LANES)
-        y_rows = y.rearrange("(u p q) i -> p u q i", p=P, q=2)
-        ux_rows = ux.rearrange("(u p q) one -> p u (q one)", p=P, q=2)
+        y_rows = y.rearrange("(n p) i -> p n i", p=P)
+        ux_rows = ux.rearrange("(n p) one -> p n one", p=P)
         e_lane = [tile("e_lane%d" % t, [P, WORDS], F32) for t in range(LANES)]
         w_lane = [tile("w_lane%d" % t, [P, WORDS], F32) for t in range(LANES)]
         ts_table = tile("ts_table", [P, WORDS], F32)
-        y_half = [tile("y_half%d" % u, [P, 2, OUT_SLOTS], F32) for u in range(2)]
+        y_part = [tile("y_part%d" % n, [P, OUT_SLOTS], F32) for n in range(LANES)]
         ux_col = tile("ux_col", [P, LANES], F32)
         minus_2ux = tile("minus_2ux", [P, LANES], F32)
         identity = tile("identity", [P, P], F32)
-        e_c = [tile("e_c%d" % t, [P, SLOTS], F32) for t in range(LANES)]
+        e_c = [tile("e_c%d" % t, [P, SLOTS + (0 if PAIRS_ON_VECTOR[t] else SPARE)], F32) for t in range(LANES)]
         dh = [tile("dh%d" % t, [P, DH_COLUMNS[t]], F32) for t in range(LANES)]
         grad = [tile("grad%d" % t, [P, WORDS], F32) for t in range(LANES)]
 
@@ -75,6 +78,9 @@ def tile_attend_gcbow_ns_pl_kernel(tc, eT, wT, ts, ux, y, coffs, posnoffs, sloto
         nc.vector.memset(warm[:, 0:1], 0.0)
         nc.scalar.activation(warm[:, 1:2], warm[:, 0:1], ACT.Sigmoid)
         make_identity(nc, identity[:])
+        for t in range(LANES):
+            if not PAIRS_ON_VECTOR[t]:
+                nc.gpsimd.memset(e_c[t][:, SLOTS:], 0.0)
         for t in range(LANES):
             nc.gpsimd.memset(grad[t][:], 0.0)
             if DH_COLUMNS[t] > POS:
@@ -85,13 +91,15 @@ def tile_attend_gcbow_ns_pl_kernel(tc, eT, wT, ts, ux, y, coffs, posnoffs, sloto
         nc.sync.dma_start(e_lane[0][:], e_rows[:, 0, :])
         nc.sync.dma_start(ctx_list[:], coffs)
         nc.sync.dma_start(slot_list[:], slotoffs)
-        nc.sync.dma_start(ux_col[:].rearrange("p (u q) -> p u q", q=2), ux_rows)
-        nc.sync.dma_start(e_lane[1][:], e_rows[:, 1, :])
-        for u in range(2):
-            nc.sync.dma_start(e_lane[2 + u][:], e_rows[:, 2 + u, :])
-            nc.sync.dma_start(y_half[u][:], y_rows[:, u])
+        with nc.allow_non_contiguous_dma(reason="one scale a position, the positions on the partitions"):
+            nc.sync.dma_start(ux_col[:].rearrange("p (n one) -> p n one", one=1), ux_rows)
+        for t in range(1, LANES):
+            nc.sync.dma_start(e_lane[t][:], e_rows[:, t, :])
+        for n in range(LANES - 1):
+            nc.sync.dma_start(y_part[n][:], y_rows[:, n, :])
         for t in range(LANES):
             nc.sync.dma_start(w_lane[t][:], w_rows[:, t, :])
+        nc.sync.dma_start(y_part[LANES - 1][:], y_rows[:, LANES - 1, :])
         nc.sync.dma_start(posn_list[:], posnoffs)
 
         ts_i = tile("ts_i", [P, OUT_SLOTS], F32)
@@ -103,31 +111,45 @@ def tile_attend_gcbow_ns_pl_kernel(tc, eT, wT, ts, ux, y, coffs, posnoffs, sloto
         nc.scalar.copy(ts_col[:], ts_ps[:, :, P - 1])
 
         pairs = tile("pairs", [P, LANES, SLOTS], F32, "pairs_then_out")
-        halves = ((on_vector, 0, SLOTS // 2), (on_scalar, SLOTS // 2, SLOTS))
         for t in range(LANES):
-            for move, lo, hi in halves:
-                move(e_c[t][:, lo:hi], e_lane[t][:].indirect(entries(ctx_list, lo, hi)))
-            for move, lo, hi in halves:
-                move(pairs[:, t, lo:hi], e_c[t][:].indirect(entries(slot_list, lo, hi)))
+            for move, lo, hi in ((on_vector, 0, CONTEXT_ON_VECTOR[t]), (on_scalar, CONTEXT_ON_VECTOR[t], SLOTS)):
+                if lo < hi:
+                    move(e_c[t][:, lo:hi], e_lane[t][:].indirect(entries(ctx_list, lo, hi)))
+            for move, lo, hi in ((on_vector, 0, PAIRS_ON_VECTOR[t]), (on_scalar, PAIRS_ON_VECTOR[t], SLOTS)):
+                if lo < hi:
+                    move(pairs[:, t, lo:hi], e_c[t][:].indirect(entries(slot_list, lo, hi)))
 
         nc.gpsimd.tensor_scalar(minus_2ux[:], ux_col[:], -2.0, 0.0, ALU.mult, ALU.add)
         signed_ux = [tile("signed_ux%d" % n, [P, OUT_SLOTS], F32) for n in range(LANES)]
-        factor = [tile("factor%d" % u, [P, LANES, POS // 2], F32) for u in range(2)]
-        for u in range(2):
-            for q in range(2):
-                n = 2 * u + q
-                nc.gpsimd.tensor_scalar(
-                    signed_ux[n][:].rearrange("p (r k run) -> p k r run", r=LANES, run=LINE),
-                    y_half[u][:, q, :].rearrange("p (k run r) -> p k r run", r=LANES, run=LINE),
-                    minus_2ux[:, n : n + 1], ux_col[:, n : n + 1], ALU.mult, ALU.add)
-            f_ps = [bank("f_ps", [P, 2, 2, P], 2 * u + v) for v in range(2)]
-            for q in range(2):
-                for r in range(LANES):
-                    nc.tensor.transpose(f_ps[r // 2][:, r % 2, q, :], signed_ux[2 * u + q][:, P * r : P * (r + 1)], identity[:])
+        factor = [tile("factor01", [P, LANES, 2 * P], F32), tile("factor2", [P, LANES, P], F32), tile("factor3", [P, LANES, P], F32)]
+
+        def sign_labels(engine, n):
+            engine.tensor_scalar(
+                signed_ux[n][:].rearrange("p (r k run) -> p k r run", r=LANES, run=LINE),
+                y_part[n][:].rearrange("p (k run r) -> p k r run", r=LANES, run=LINE),
+                minus_2ux[:, n : n + 1], ux_col[:, n : n + 1], ALU.mult, ALU.add)
+
+        def turn_labels(n, target):
             for r in range(LANES):
-                nc.scalar.activation(
-                    factor[u][:, r, :].rearrange("o (p q) -> o p q", q=2), f_ps[r // 2][:, r % 2, :, :].rearrange("o q p -> o p q"),
-                    ACT.Copy, scale=ts_col[:, r : r + 1])
+                nc.tensor.transpose(target(r), signed_ux[n][:, P * r : P * (r + 1)], identity[:])
+
+        def copy_factor(target, source):
+            for r in range(LANES):
+                nc.scalar.activation(target[:, r, :], source(r), ACT.Copy, scale=ts_col[:, r : r + 1])
+
+        f_ps = [bank("f_ps", [P, 2, 2, P], v) for v in range(2)]
+        for n in range(2):
+            sign_labels(nc.gpsimd, n)
+            turn_labels(n, lambda r: f_ps[r // 2][:, r % 2, n, :])
+        copy_factor(factor[0], lambda r: f_ps[r // 2][:, r % 2].rearrange("o n p -> o (n p)"))
+
+        def single_factor(n):
+            one_ps = bank("one_ps", [P, LANES, P], n)
+            turn_labels(n, lambda r: one_ps[:, r, :])
+            copy_factor(factor[n - 1], lambda r: one_ps[:, r, :])
+
+        sign_labels(nc.gpsimd, 2)
+        single_factor(2)
 
         def mx_tiles(name, width, tag=None):
             return tile(name + "_codes", [P, width], U32, tag), tile(name + "_scales", [P, width], U8)
@@ -184,40 +206,42 @@ def tile_attend_gcbow_ns_pl_kernel(tc, eT, wT, ts, ux, y, coffs, posnoffs, sloto
         gather_w(on_scalar, 2, 0, OUT_SLOTS)
         gather_w(on_vector, 3, 0, OUT_SLOTS // 2)
         gather_w(on_scalar, 3, OUT_SLOTS // 2, OUT_SLOTS)
+        sign_labels(nc.vector, 3)
         weave_w(on_vector, 1, slice(0, 2))
         weave_w(on_vector, 1, slice(2, 3))
         weave_w(nc.scalar.copy, 1, slice(3, 4))
+        single_factor(3)
         for half in range(2):
             cols = slice(2 * P * half, 2 * P * (half + 1))
             quantize(wd_mx, cols, w_by_d[:, cols, :], E4M3)
-        turn_w(1, 0)
         lay_w(0, "w_lane3")
-        lay_w(1, "w_by_i1")
         quantize(wi_mx[0], slice(0, 2 * P), w_by_i[0][:], E4M3)
 
         g_mx = mx_tiles("g", POS)
         g_bf = tile("g_bf", [P, POS, LANES], BF16)
-        scores = []
-        for ch in range(LANES):
-            scores.append(bank("a_ps", [P, LANES, P], LANES + ch))
-            for r in range(LANES):
+        def score(number, ch, lanes):
+            a_ps = bank("a_ps", [P, len(lanes), P], number)
+            for place, r in enumerate(lanes):
                 nc.tensor.matmul_mx(
-                    out=scores[ch][:, r, :], lhsT=wd_mx[0][:, chunks[r]].bitcast(E4M3), lhsT_scale=wd_mx[1][:, chunks[r]],
+                    out=a_ps[:, place, :], lhsT=wd_mx[0][:, chunks[r]].bitcast(E4M3), lhsT_scale=wd_mx[1][:, chunks[r]],
                     rhs=s_mx[0][:, chunks[ch]].bitcast(E4M3), rhs_scale=s_mx[1][:, chunks[ch]], start=True, stop=True)
+            return slice(lanes[0], lanes[-1] + 1), a_ps
+
+        scores = [[score(0, 0, (0, 1)), score(4, 0, (2, 3))]] + [[score(4 + ch, ch, range(LANES))] for ch in range(1, LANES)]
         sig = [tile("sig%d" % ch, [P, LANES, P], F32, "signed_ux%d" % ch) for ch in range(LANES)]
 
         def factor_of(ch, cols):
-            return factor[ch // 2][:, :, chunks[ch % 2]][:, :, cols]
+            return factor[0][:, :, chunks[ch]][:, :, cols] if ch < 2 else factor[ch - 1][:, :, cols]
 
         def pieces(ch):
-            step = P // 2 if ch == 0 else P
+            step = P
             return [slice(x, x + step) for x in range(0, P, step)]
 
         def squash(ch):
             z = tile("z%d" % ch, [P, LANES, P], F32)
-            for cols in pieces(ch):
-                nc.vector.tensor_tensor(z[:, :, cols], scores[ch][:, :, cols], factor_of(ch, cols), ALU.mult)
-                nc.scalar.activation(sig[ch][:, :, cols], z[:, :, cols], ACT.Sigmoid, scale=0.5)
+            for rs, a_ps in scores[ch]:
+                nc.vector.tensor_tensor(z[:, rs, :], a_ps[:], factor_of(ch, slice(0, P))[:, rs, :], ALU.mult)
+                nc.scalar.activation(sig[ch][:, rs, :], z[:, rs, :], ACT.Sigmoid, scale=0.5)
 
         def loss_gradient(ch):
             engine = nc.gpsimd if ch == 0 else nc.vector
@@ -242,6 +266,8 @@ def tile_attend_gcbow_ns_pl_kernel(tc, eT, wT, ts, ux, y, coffs, posnoffs, sloto
 
         for ch in range(LANES):
             squash(ch)
+        turn_w(1, 4)
+        lay_w(1, "z3")
         for ch in range(3):
             loss_gradient(ch)
         quantize(g_mx, slice(0, 2 * P), g_bf[:, 0 : 2 * P, :], E5M2)

@@ -61,11 +61,11 @@ def tile_attend_gcbow_ns_pl_kernel(tc, eT, wT, ts, ux, y, coffs, posnoffs, sloto
         w_rows = wT.rearrange("(p t) col -> p t col", t=LANES)
         out_rows = out_0.rearrange("(p t) col -> p t col", t=LANES)
         y_rows = y.rearrange("(n p) i -> p n i", p=P)
-        ux_rows = ux.rearrange("(n p) one -> p n one", p=P)
         e_lane = [tile("e_lane%d" % t, [P, WORDS], F32) for t in range(LANES)]
         w_lane = [tile("w_lane%d" % t, [P, WORDS], F32) for t in range(LANES)]
         ts_table = tile("ts_table", [P, WORDS], F32)
         y_part = [tile("y_part%d" % n, [P, OUT_SLOTS], F32) for n in range(LANES)]
+        ux_row = tile("ux_row", [P, POS], F32)
         ux_col = tile("ux_col", [P, LANES], F32)
         minus_2ux = tile("minus_2ux", [P, LANES], F32)
         identity = tile("identity", [P, P], F32)
@@ -74,6 +74,7 @@ def tile_attend_gcbow_ns_pl_kernel(tc, eT, wT, ts, ux, y, coffs, posnoffs, sloto
         grad = [tile("grad%d" % t, [P, WORDS], F32) for t in range(LANES)]
 
         nc.vector.memset(ts_table[0 : P - 1, :], 0.0)
+        nc.vector.memset(ux_row[0 : P - 1, :], 0.0)
         warm = tile("warm", [P, 2], F32)
         nc.vector.memset(warm[:, 0:1], 0.0)
         nc.scalar.activation(warm[:, 1:2], warm[:, 0:1], ACT.Sigmoid)
@@ -91,8 +92,7 @@ def tile_attend_gcbow_ns_pl_kernel(tc, eT, wT, ts, ux, y, coffs, posnoffs, sloto
         nc.sync.dma_start(e_lane[0][:], e_rows[:, 0, :])
         nc.sync.dma_start(ctx_list[:], coffs)
         nc.sync.dma_start(slot_list[:], slotoffs)
-        with nc.allow_non_contiguous_dma(reason="one scale a position, the positions on the partitions"):
-            nc.sync.dma_start(ux_col[:].rearrange("p (n one) -> p n one", one=1), ux_rows)
+        nc.sync.dma_start(ux_row[P - 1 : P, :], ux.rearrange("x one -> one x"))
         for t in range(1, LANES):
             nc.sync.dma_start(e_lane[t][:], e_rows[:, t, :])
         for n in range(LANES - 1):
@@ -119,6 +119,10 @@ def tile_attend_gcbow_ns_pl_kernel(tc, eT, wT, ts, ux, y, coffs, posnoffs, sloto
                 if lo < hi:
                     move(pairs[:, t, lo:hi], e_c[t][:].indirect(entries(slot_list, lo, hi)))
 
+        ux_ps = bank("ux_ps", [P, LANES, P], 5)
+        for n in range(LANES):
+            nc.tensor.transpose(ux_ps[:, n, :], ux_row[:, P * n : P * (n + 1)], identity[:])
+        nc.scalar.copy(ux_col[:], ux_ps[:, :, P - 1])
         nc.gpsimd.tensor_scalar(minus_2ux[:], ux_col[:], -2.0, 0.0, ALU.mult, ALU.add)
         signed_ux = [tile("signed_ux%d" % n, [P, OUT_SLOTS], F32) for n in range(LANES)]
         factor = [tile("factor01", [P, LANES, 2 * P], F32), tile("factor2", [P, LANES, P], F32), tile("factor3", [P, LANES, P], F32)]
@@ -161,22 +165,25 @@ def tile_attend_gcbow_ns_pl_kernel(tc, eT, wT, ts, ux, y, coffs, posnoffs, sloto
         chunks = [slice(P * ch, P * (ch + 1)) for ch in range(LANES)]
 
         s_mx = mx_tiles("s", POS)
-        s_bf = tile("s_bf", [P, POS, LANES], BF16)
+        s_bf = {}
         pair_view = pairs[:].rearrange("p t (k run j) -> p k t run j", run=2, j=2)
-        for ch in range(LANES + 1):
-            if ch < LANES:
-                ks = slice(P // 2 * ch, P // 2 * (ch + 1))
+
+        def form_s(half, tag):
+            s_bf[half] = tile("s_bf%d" % half, [P, 2 * P, LANES], BF16, tag)
+            for ch in range(2):
+                ks = slice(P // 2 * (2 * half + ch), P // 2 * (2 * half + ch + 1))
                 nc.vector.tensor_tensor(
-                    s_bf[:, chunks[ch], :].rearrange("p (k run) t -> p k t run", run=2),
+                    s_bf[half][:, chunks[ch], :].rearrange("p (k run) t -> p k t run", run=2),
                     pair_view[:, ks, :, :, 0], pair_view[:, ks, :, :, 1], ALU.add)
-            if ch > 0:
-                quantize(s_mx, chunks[ch - 1], s_bf[:, chunks[ch - 1], :], E4M3)
+            for ch in range(2):
+                quantize(s_mx, chunks[2 * half + ch], s_bf[half][:, chunks[ch], :], E4M3)
+
+        form_s(0, "s_bf0")
 
         w_listed = [tile("w_listed%d" % v, [P, 2, OUT_SLOTS], BF16) for v in range(2)]
         w_by_d = tile("w_by_d", [P, OUT_SLOTS, LANES], BF16)
         w_by_i = {}
         w_ps = {}
-        wi_mx = {0: mx_tiles("wi0", 2 * P)}
         wd_mx = mx_tiles("wd", OUT_SLOTS)
 
         def gather_w(move, t, lo, hi):
@@ -202,8 +209,10 @@ def tile_attend_gcbow_ns_pl_kernel(tc, eT, wT, ts, ux, y, coffs, posnoffs, sloto
         gather_w(on_scalar, 0, 0, OUT_SLOTS)
         gather_w(on_vector, 1, 0, OUT_SLOTS)
         turn_w(0, 1)
+        form_s(1, "w_lane1")
         weave_w(on_vector, 0, slice(0, LANES))
         gather_w(on_scalar, 2, 0, OUT_SLOTS)
+        lay_w(0, "w_lane2")
         gather_w(on_vector, 3, 0, OUT_SLOTS // 2)
         gather_w(on_scalar, 3, OUT_SLOTS // 2, OUT_SLOTS)
         sign_labels(nc.vector, 3)
@@ -214,7 +223,7 @@ def tile_attend_gcbow_ns_pl_kernel(tc, eT, wT, ts, ux, y, coffs, posnoffs, sloto
         for half in range(2):
             cols = slice(2 * P * half, 2 * P * (half + 1))
             quantize(wd_mx, cols, w_by_d[:, cols, :], E4M3)
-        lay_w(0, "w_lane3")
+        wi_mx = {0: mx_tiles("wi0", 2 * P, "w_lane3")}
         quantize(wi_mx[0], slice(0, 2 * P), w_by_i[0][:], E4M3)
 
         g_mx = mx_tiles("g", POS)

@@ -71,21 +71,21 @@ def tile_attend_gcbow_ns_pl_kernel(tc, eT, wT, ts, ux, y, coffs, posnoffs, sloto
         identity = tile("identity", [P, P], F32)
         e_c = [tile("e_c%d" % t, [P, SLOTS + (0 if PAIRS_ON_VECTOR[t] else SPARE)], F32) for t in range(LANES)]
         dh = [tile("dh%d" % t, [P, DH_COLUMNS[t]], F32) for t in range(LANES)]
-        grad = [tile("grad%d" % t, [P, WORDS], F32) for t in range(LANES)]
+        grad = [tile("grad%d" % t, [P, WORDS], F32) for t in range(2)]
 
-        nc.vector.memset(ts_table[0 : P - 1, :], 0.0)
-        nc.vector.memset(ux_row[0 : P - 1, :], 0.0)
         warm = tile("warm", [P, 2], F32)
-        nc.vector.memset(warm[:, 0:1], 0.0)
+        nc.gpsimd.memset(warm[:, 0:1], 0.0)
         nc.scalar.activation(warm[:, 1:2], warm[:, 0:1], ACT.Sigmoid)
+        nc.gpsimd.memset(ts_table[0 : P - 1, :], 0.0)
         make_identity(nc, identity[:])
+        nc.gpsimd.memset(ux_row[0 : P - 1, :], 0.0)
         for t in range(LANES):
             if not PAIRS_ON_VECTOR[t]:
                 nc.gpsimd.memset(e_c[t][:, SLOTS:], 0.0)
-        for t in range(LANES):
-            nc.gpsimd.memset(grad[t][:], 0.0)
             if DH_COLUMNS[t] > POS:
                 nc.gpsimd.memset(dh[t][:, POS:], 0.0)
+        for t in range(2):
+            nc.gpsimd.memset(grad[t][:], 0.0)
 
         nc.sync.dma_start(ts_table[P - 1 : P, :], ts[0:1, :])
         nc.sync.dma_start(idx_list[:], offs)
@@ -294,6 +294,9 @@ def tile_attend_gcbow_ns_pl_kernel(tc, eT, wT, ts, ux, y, coffs, posnoffs, sloto
         dh_lane2 = multiply_dh(2, 0, POS, 6)
         dh_lane3 = multiply_dh(3, 0, POS, 7)
 
+        for t, tag in ((2, "z3"), (3, "g_codes")):
+            grad.append(tile("grad%d" % t, [P, WORDS], F32, tag))
+            nc.gpsimd.memset(grad[t][:], 0.0)
         out_bf = tile("out_bf", [P, WORDS, LANES], BF16, "pairs_then_out")
         lanes_bf = tile("lanes_bf", [P, LANES, WORDS], BF16, "e_lane0")
         de = [tile("de%d" % t, [P, SLOTS], F32, "e_c%d" % t) for t in range(LANES)]

@@ -29,6 +29,8 @@ DH_COLUMNS = (656, 528, 1040, POS)
 CONTEXT_ON_VECTOR = (512, 768, SLOTS, SLOTS)
 PAIRS_ON_VECTOR = (256, 0, 0, 512)
 SPARE = 16
+G_ON_GPSIMD = 96
+LAID_BY_GPSIMD = 1280
 SPLIT = 1152
 PIECE = 256
 
@@ -242,23 +244,17 @@ def tile_attend_gcbow_ns_pl_kernel(tc, eT, wT, ts, ux, y, coffs, posnoffs, sloto
         def factor_of(ch, cols):
             return factor[0][:, :, chunks[ch]][:, :, cols] if ch < 2 else factor[ch - 1][:, :, cols]
 
-        def pieces(ch):
-            step = P
-            return [slice(x, x + step) for x in range(0, P, step)]
-
         def squash(ch):
             z = tile("z%d" % ch, [P, LANES, P], F32)
             for rs, a_ps in scores[ch]:
                 nc.vector.tensor_tensor(z[:, rs, :], a_ps[:], factor_of(ch, slice(0, P))[:, rs, :], ALU.mult)
                 nc.scalar.activation(sig[ch][:, rs, :], z[:, rs, :], ACT.Sigmoid, scale=0.5)
 
-        def loss_gradient(ch):
-            engine = nc.gpsimd if ch == 0 else nc.vector
-            for cols in pieces(ch):
-                engine.tensor_tensor(
-                    g_bf[:, chunks[ch], :][:, cols, :].rearrange("o (k run) r -> o k r run", run=LINE),
-                    sig[ch][:, :, cols].rearrange("o r (k run) -> o k r run", run=LINE),
-                    factor_of(ch, cols).rearrange("o r (k run) -> o k r run", run=LINE), ALU.mult)
+        def loss_gradient(engine, ch, cols):
+            engine.tensor_tensor(
+                g_bf[:, chunks[ch], :][:, cols, :].rearrange("o (k run) r -> o k r run", run=LINE),
+                sig[ch][:, :, cols].rearrange("o r (k run) -> o k r run", run=LINE),
+                factor_of(ch, cols).rearrange("o r (k run) -> o k r run", run=LINE), ALU.mult)
 
         def multiply_dh(t, lo, hi, number):
             dh_ps = bank("dh_ps", [P, hi - lo], number)
@@ -277,12 +273,14 @@ def tile_attend_gcbow_ns_pl_kernel(tc, eT, wT, ts, ux, y, coffs, posnoffs, sloto
             squash(ch)
         turn_w(1, 4)
         lay_w(1, "z3")
-        for ch in range(3):
-            loss_gradient(ch)
+        loss_gradient(nc.gpsimd, 0, slice(0, G_ON_GPSIMD))
+        loss_gradient(nc.vector, 0, slice(G_ON_GPSIMD, P))
+        for ch in range(1, 3):
+            loss_gradient(nc.vector, ch, slice(0, P))
         quantize(g_mx, slice(0, 2 * P), g_bf[:, 0 : 2 * P, :], E5M2)
         halve_on_scalar(*multiply_dh(0, 0, 2 * P, 0))
         halve_on_scalar(*multiply_dh(1, 0, 2 * P, 1))
-        loss_gradient(3)
+        loss_gradient(nc.vector, 3, slice(0, P))
         quantize(g_mx, chunks[2], g_bf[:, chunks[2], :], E5M2)
         halve_on_scalar(*multiply_dh(0, 2 * P, 3 * P, 2))
         halve_on_scalar(*multiply_dh(1, 2 * P, 3 * P, 3))
@@ -343,8 +341,9 @@ def tile_attend_gcbow_ns_pl_kernel(tc, eT, wT, ts, ux, y, coffs, posnoffs, sloto
         store(nc.sync, 3)
         closing = ((SPLIT, 3 * quarter), (3 * quarter, WORDS - PIECE), (WORDS - PIECE, WORDS))
         for lo, hi in closing:
-            lay(on_gpsimd, lo, hi, slice(0, 2))
+            lay(on_gpsimd, max(lo, LAID_BY_GPSIMD), hi, slice(0, 2))
         on_vector(lanes_bf[:, 2, :], grad[2][:])
+        lay(on_vector, SPLIT, LAID_BY_GPSIMD, slice(0, 2))
         lay(on_vector, 0, SPLIT, slice(0, 3))
 
         out_codes = tile("out_codes", [P, WORDS], U32, "e_lane1")

@@ -209,7 +209,8 @@ def tile_attend_gcbow_ns_pl_kernel(tc, eT, wT, ts, ux, y, coffs, posnoffs, sloto
                 w_listed[v][:].rearrange("p e (k run r) -> p k r run e", r=LANES, run=2)[:, :, rs])
 
         gather_w(on_scalar, 0, 0, OUT_SLOTS)
-        gather_w(on_vector, 1, 0, OUT_SLOTS)
+        gather_w(on_vector, 1, 0, OUT_SLOTS // 2)
+        gather_w(on_scalar, 1, OUT_SLOTS // 2, OUT_SLOTS)
         turn_w(0, 1)
         form_s(1, "w_lane1")
         weave_w(on_vector, 0, slice(0, LANES))

@@ -29,7 +29,6 @@ DH_COLUMNS = (656, 528, 1040, POS)
 CONTEXT_ON_VECTOR = (512, 768, SLOTS, SLOTS)
 PAIRS_ON_VECTOR = (256, 0, 0, 512)
 SPARE = 16
-G_ON_GPSIMD = 96
 LAID_BY_GPSIMD = 1280
 SPLIT = 1152
 PIECE = 256
@@ -156,6 +155,14 @@ def tile_attend_gcbow_ns_pl_kernel(tc, eT, wT, ts, ux, y, coffs, posnoffs, sloto
 
         sign_labels(nc.gpsimd, 2)
         single_factor(2)
+        there_ps = bank("there_ps", [P, LANES, P], 3)
+        for r in range(LANES):
+            nc.tensor.transpose(there_ps[:, r, :], factor[0][:, r, P:], identity[:])
+        factor_turned = tile("factor_turned", [P, LANES, P], F32, "y_part1")
+        on_vector(factor_turned[:], there_ps[:])
+        factor1_ps = bank("factor1_ps", [P, LANES, P], 2)
+        for r in range(LANES):
+            nc.tensor.transpose(factor1_ps[:, r, :], factor_turned[:, r, :], identity[:])
 
         def mx_tiles(name, width, tag=None):
             return tile(name + "_codes", [P, width], U32, tag), tile(name + "_scales", [P, width], U8)
@@ -251,11 +258,11 @@ def tile_attend_gcbow_ns_pl_kernel(tc, eT, wT, ts, ux, y, coffs, posnoffs, sloto
                 nc.vector.tensor_tensor(z[:, rs, :], a_ps[:], factor_of(ch, slice(0, P))[:, rs, :], ALU.mult)
                 nc.scalar.activation(sig[ch][:, rs, :], z[:, rs, :], ACT.Sigmoid, scale=0.5)
 
-        def loss_gradient(engine, ch, cols):
+        def loss_gradient(engine, ch, factors):
             engine.tensor_tensor(
-                g_bf[:, chunks[ch], :][:, cols, :].rearrange("o (k run) r -> o k r run", run=LINE),
-                sig[ch][:, :, cols].rearrange("o r (k run) -> o k r run", run=LINE),
-                factor_of(ch, cols).rearrange("o r (k run) -> o k r run", run=LINE), ALU.mult)
+                g_bf[:, chunks[ch], :].rearrange("o (k run) r -> o k r run", run=LINE),
+                sig[ch][:].rearrange("o r (k run) -> o k r run", run=LINE),
+                factors.rearrange("o r (k run) -> o k r run", run=LINE), ALU.mult)
 
         def multiply_dh(t, lo, hi, number):
             dh_ps = bank("dh_ps", [P, hi - lo], number)
@@ -274,14 +281,13 @@ def tile_attend_gcbow_ns_pl_kernel(tc, eT, wT, ts, ux, y, coffs, posnoffs, sloto
             squash(ch)
         turn_w(1, 4)
         lay_w(1, "z3")
-        loss_gradient(nc.gpsimd, 0, slice(0, G_ON_GPSIMD))
-        loss_gradient(nc.vector, 0, slice(G_ON_GPSIMD, P))
-        for ch in range(1, 3):
-            loss_gradient(nc.vector, ch, slice(0, P))
+        loss_gradient(nc.gpsimd, 0, factor_of(0, slice(0, P)))
+        loss_gradient(nc.vector, 1, factor1_ps[:])
+        loss_gradient(nc.vector, 2, factor_of(2, slice(0, P)))
         quantize(g_mx, slice(0, 2 * P), g_bf[:, 0 : 2 * P, :], E5M2)
         halve_on_scalar(*multiply_dh(0, 0, 2 * P, 0))
         halve_on_scalar(*multiply_dh(1, 0, 2 * P, 1))
-        loss_gradient(nc.vector, 3, slice(0, P))
+        loss_gradient(nc.vector, 3, factor_of(3, slice(0, P)))
         quantize(g_mx, chunks[2], g_bf[:, chunks[2], :], E5M2)
         halve_on_scalar(*multiply_dh(0, 2 * P, 3 * P, 2))
         halve_on_scalar(*multiply_dh(1, 2 * P, 3 * P, 3))

@@ -321,6 +321,11 @@ def tile_attend_gcbow_ns_pl_kernel(tc, eT, wT, ts, ux, y, coffs, posnoffs, sloto
         def lay(move, lo, hi, lanes):
             move(out_bf[:, lo:hi, lanes], lanes_bf[:, lanes, lo:hi].rearrange("p t col -> p col t"))
 
+        def lay_by_lines(lo, hi, lanes):
+            on_vector(
+                out_bf[:, lo:hi, lanes].rearrange("p (k run) t -> p k t run", run=2),
+                lanes_bf[:, lanes, lo:hi].rearrange("p t (k run) -> p k t run", run=2))
+
         quarter = WORDS // 4
         look_up(on_scalar, 0, CUTS[0], CUTS[1])
         look_up(on_scalar, 0, CUTS[1], CUTS[3])
@@ -350,8 +355,8 @@ def tile_attend_gcbow_ns_pl_kernel(tc, eT, wT, ts, ux, y, coffs, posnoffs, sloto
         for lo, hi in closing:
             lay(on_gpsimd, max(lo, LAID_BY_GPSIMD), hi, slice(0, 2))
         on_vector(lanes_bf[:, 2, :], grad[2][:])
-        lay(on_vector, SPLIT, LAID_BY_GPSIMD, slice(0, 2))
-        lay(on_vector, 0, SPLIT, slice(0, 3))
+        lay_by_lines(SPLIT, LAID_BY_GPSIMD, slice(0, 2))
+        lay_by_lines(0, SPLIT, slice(0, 3))
 
         out_codes = tile("out_codes", [P, WORDS], U32, "e_lane1")
         out_scales = tile("out_scales", [P, WORDS // 2], U8)

@@ -24,13 +24,12 @@ POS = 512
 OUT_SLOTS = 512
 LINE = 4
 CUTS = (0, 384, 768, SLOTS)
-LOOK3 = 448
+LOOK3 = 640
 DH_COLUMNS = (656, 528, 1040, POS)
 CONTEXT_ON_VECTOR = (512, 768, SLOTS, SLOTS)
 PAIRS_ON_VECTOR = (256, 0, 0, 512)
 SPARE = 16
-LAID_BY_GPSIMD = 1280
-SPLIT = 1152
+SPANS = (0, 384, 640, 1024, WORDS)
 PIECE = 256
 
 
@@ -50,6 +49,9 @@ def tile_attend_gcbow_ns_pl_kernel(tc, eT, wT, ts, ux, y, coffs, posnoffs, sloto
             nc.scalar.activation(out, in_, ACT.Copy)
 
         on_vector = nc.vector.tensor_copy
+
+        def on_gpsimd(out, in_):
+            nc.gpsimd.tensor_scalar(out, in_, 1.0, 0.0, ALU.mult, ALU.add)
 
         def entries(offsets, lo, hi):
             return offsets[:, lo // 16 : hi // 16]
@@ -72,7 +74,7 @@ def tile_attend_gcbow_ns_pl_kernel(tc, eT, wT, ts, ux, y, coffs, posnoffs, sloto
         identity = tile("identity", [P, P], F32)
         e_c = [tile("e_c%d" % t, [P, SLOTS + (0 if PAIRS_ON_VECTOR[t] else SPARE)], F32) for t in range(LANES)]
         dh = [tile("dh%d" % t, [P, DH_COLUMNS[t]], F32) for t in range(LANES)]
-        grad = [tile("grad%d" % t, [P, WORDS], F32) for t in range(2)]
+        grad = {t: tile("grad%d" % t, [P, WORDS], F32) for t in (0, 1, 3)}
 
         warm = tile("warm", [P, 2], F32)
         nc.gpsimd.memset(warm[:, 0:1], 0.0)
@@ -85,7 +87,7 @@ def tile_attend_gcbow_ns_pl_kernel(tc, eT, wT, ts, ux, y, coffs, posnoffs, sloto
                 nc.gpsimd.memset(e_c[t][:, SLOTS:], 0.0)
             if DH_COLUMNS[t] > POS:
                 nc.gpsimd.memset(dh[t][:, POS:], 0.0)
-        for t in range(2):
+        for t in (1, 0, 3):
             nc.gpsimd.memset(grad[t][:], 0.0)
 
         nc.sync.dma_start(ts_table[P - 1 : P, :], ts[0:1, :])
@@ -299,12 +301,13 @@ def tile_attend_gcbow_ns_pl_kernel(tc, eT, wT, ts, ux, y, coffs, posnoffs, sloto
         dh_lane2 = multiply_dh(2, 0, POS, 6)
         dh_lane3 = multiply_dh(3, 0, POS, 7)
 
-        for t, tag in ((2, "z3"), (3, "g_codes")):
-            grad.append(tile("grad%d" % t, [P, WORDS], F32, tag))
-            nc.gpsimd.memset(grad[t][:], 0.0)
-        out_bf = tile("out_bf", [P, WORDS, LANES], BF16, "pairs_then_out")
-        lanes_bf = tile("lanes_bf", [P, LANES, WORDS], BF16, "e_lane0")
+        grad[2] = tile("grad2", [P, WORDS], F32, "z3")
+        nc.gpsimd.memset(grad[2][:], 0.0)
         de = [tile("de%d" % t, [P, SLOTS], F32, "e_c%d" % t) for t in range(LANES)]
+        quarter = WORDS // 4
+        tags = ("e_lane0", "e_lane2", "e_lane3", "w_lane0")
+        halves = [tile("halves%d" % k, [P, 2, SPANS[k + 1] - SPANS[k], 2], BF16, tag) for k, tag in enumerate(tags)]
+        out_bf = tile("out_bf", [P, WORDS * LANES], BF16, "pairs_then_out")
 
         def look_up(move, t, lo, hi):
             move(de[t][:, lo:hi], dh[t][:].indirect(entries(posn_list, lo, hi)))
@@ -315,18 +318,17 @@ def tile_attend_gcbow_ns_pl_kernel(tc, eT, wT, ts, ux, y, coffs, posnoffs, sloto
         def store(queue, t):
             queue.dma_start(out_rows[:, t, :], grad[t][:])
 
-        def on_gpsimd(out, in_):
-            nc.gpsimd.tensor_scalar(out, in_, 1.0, 0.0, ALU.mult, ALU.add)
+        def round_lane(move, t, k):
+            move(halves[k][:, t // 2, :, t % 2], grad[t][:, SPANS[k] : SPANS[k + 1]])
 
-        def lay(move, lo, hi, lanes):
-            move(out_bf[:, lo:hi, lanes], lanes_bf[:, lanes, lo:hi].rearrange("p t col -> p col t"))
+        def weave_out(move, word, k, lo=None, hi=None):
+            first = SPANS[k]
+            lo, hi = (lo or first), (hi or SPANS[k + 1])
+            words = halves[k][:].rearrange("p u col e -> p u (col e)").bitcast(word)
+            move(
+                out_bf[:, LANES * lo : LANES * hi].bitcast(word).rearrange("p (col u) -> p col u", u=2),
+                words[:, :, lo - first : hi - first].rearrange("p u col -> p col u"))
 
-        def lay_by_lines(lo, hi, lanes):
-            on_vector(
-                out_bf[:, lo:hi, lanes].rearrange("p (k run) t -> p k t run", run=2),
-                lanes_bf[:, lanes, lo:hi].rearrange("p t (k run) -> p k t run", run=2))
-
-        quarter = WORDS // 4
         look_up(on_scalar, 0, CUTS[0], CUTS[1])
         look_up(on_scalar, 0, CUTS[1], CUTS[3])
         look_up(on_vector, 1, 0, SLOTS // 2)
@@ -334,53 +336,52 @@ def tile_attend_gcbow_ns_pl_kernel(tc, eT, wT, ts, ux, y, coffs, posnoffs, sloto
         halve_on_vector(*dh_lane2)
         place(on_vector, 1, 0, SLOTS)
         store(nc.sync, 1)
-        on_gpsimd(lanes_bf[:, 1, :], grad[1][:])
+        for k in range(len(tags)):
+            round_lane(on_gpsimd, 1, k)
         place(on_scalar, 0, CUTS[0], CUTS[1])
         halve_on_scalar(*dh_lane3)
         place(on_scalar, 0, CUTS[1], CUTS[2])
         look_up(on_scalar, 2, 0, SLOTS)
         place(on_scalar, 0, CUTS[2], CUTS[3])
-        look_up(on_vector, 3, 0, LOOK3)
+        look_up(on_vector, 3, 0, CUTS[1])
+        look_up(on_vector, 3, CUTS[1], LOOK3)
         look_up(on_scalar, 3, LOOK3, CUTS[2])
         store(nc.scalar, 0)
-        on_gpsimd(lanes_bf[:, 0, :], grad[0][:])
+        for k in (1, 2, 0, 3):
+            round_lane(on_gpsimd, 0, k)
         place(on_vector, 2, 0, SLOTS)
         store(nc.sync, 2)
         place(on_scalar, 3, CUTS[0], CUTS[1])
         look_up(on_scalar, 3, CUTS[2], CUTS[3])
         place(on_scalar, 3, CUTS[1], CUTS[2])
+        round_lane(on_scalar, 2, 1)
         place(on_scalar, 3, CUTS[2], CUTS[3])
         store(nc.sync, 3)
-        closing = ((SPLIT, 3 * quarter), (3 * quarter, WORDS - PIECE), (WORDS - PIECE, WORDS))
-        for lo, hi in closing:
-            lay(on_gpsimd, max(lo, LAID_BY_GPSIMD), hi, slice(0, 2))
-        on_vector(lanes_bf[:, 2, :], grad[2][:])
-        lay_by_lines(SPLIT, LAID_BY_GPSIMD, slice(0, 2))
-        lay_by_lines(0, SPLIT, slice(0, 3))
+        for k in (3, 2, 0):
+            round_lane(on_vector, 2, k)
 
         out_codes = tile("out_codes", [P, WORDS], U32, "e_lane1")
         out_scales = tile("out_scales", [P, WORDS // 2], U8)
         words_hbm = out_1[0].rearrange("p col l -> p (col l)").bitcast(I32)
 
-        def round_last(lo, hi):
-            on_vector(out_bf[:, lo:hi, 3], grad[3][:, lo:hi])
-
         def pack_and_store(lo, hi):
             upper, first = divmod(lo, WORDS // 2)
             nc.vector.quantize_mx(
                 out=out_codes[:, lo:hi].bitcast(E4M3), scales=out_scales[4 * upper :, first : first + hi - lo],
-                in_=out_bf[:, lo:hi, :].rearrange("p col l -> p (col l)"))
+                in_=out_bf[:, LANES * lo : LANES * hi])
             nc.sync.dma_start(words_hbm[:, lo:hi], out_codes[:, lo:hi].bitcast(I32))
 
-        nc.scalar.copy(lanes_bf[:, 3, SPLIT : 3 * quarter], grad[3][:, SPLIT : 3 * quarter])
-        nc.scalar.copy(lanes_bf[:, 3, 3 * quarter :], grad[3][:, 3 * quarter :])
-        for lo, hi in closing:
-            lay(nc.scalar.copy, lo, hi, slice(2, 4))
-        round_last(0, quarter)
-        round_last(quarter, 2 * quarter)
-        pack_and_store(0, quarter)
-        round_last(2 * quarter, SPLIT)
+        for k in (2, 0, 3):
+            round_lane(on_vector, 3, k)
+        round_lane(on_scalar, 3, 1)
+        weave_out(nc.scalar.copy, U32, 2)
+        weave_out(nc.scalar.copy, U32, 1)
+        weave_out(nc.scalar.copy, U32, 3, 2 * quarter, 3 * quarter)
+        weave_out(nc.scalar.copy, U32, 3, 3 * quarter, WORDS - PIECE)
+        weave_out(nc.scalar.copy, U32, 3, WORDS - PIECE, WORDS)
+        weave_out(on_vector, I32, 0)
         pack_and_store(quarter, 2 * quarter)
+        pack_and_store(0, quarter)
         pack_and_store(2 * quarter, 3 * quarter)
         pack_and_store(3 * quarter, WORDS - PIECE)
         pack_and_store(WORDS - PIECE, WORDS)

@@ -24,12 +24,12 @@ POS = 512
 OUT_SLOTS = 512
 LINE = 4
 CUTS = (0, 384, 768, SLOTS)
-LOOK3 = 640
+LOOK3 = 704
 DH_COLUMNS = (656, 528, 1040, POS)
 CONTEXT_ON_VECTOR = (512, 768, SLOTS, SLOTS)
 PAIRS_ON_VECTOR = (256, 0, 0, 512)
 SPARE = 16
-SPANS = (0, 384, 640, 1024, WORDS)
+SPANS = (0, 480, 736, 1024, WORDS)
 PIECE = 256
 
 
@@ -387,5 +387,5 @@ def tile_attend_gcbow_ns_pl_kernel(tc, eT, wT, ts, ux, y, coffs, posnoffs, sloto
         pack_and_store(WORDS - PIECE, WORDS)
         scales_hbm = out_2[0].bitcast(I32).rearrange("f (upper col) -> upper f col", upper=2)
         for group in range(4):
-            nc.scalar.dma_start(
+            (nc.scalar if group else nc.sync).dma_start(
                 scales_hbm[:, 4 * group : 4 * group + 4, :], out_scales[32 * group : 32 * group + 8, :].bitcast(I32))

@@ -24,8 +24,9 @@ POS = 512
 OUT_SLOTS = 512
 LINE = 4
 CUTS = (0, 384, 768, SLOTS)
-LOOK3 = 704
-DH_COLUMNS = (656, 528, 1040, POS)
+LOOK3 = 544
+AHEAD = 128
+DH_COLUMNS = (656, 528, 1040, 560)
 CONTEXT_ON_VECTOR = (512, 768, SLOTS, SLOTS)
 PAIRS_ON_VECTOR = (256, 0, 0, 512)
 SPARE = 16
@@ -303,17 +304,19 @@ def tile_attend_gcbow_ns_pl_kernel(tc, eT, wT, ts, ux, y, coffs, posnoffs, sloto
 
         grad[2] = tile("grad2", [P, WORDS], F32, "z3")
         nc.gpsimd.memset(grad[2][:], 0.0)
-        de = [tile("de%d" % t, [P, SLOTS], F32, "e_c%d" % t) for t in range(LANES)]
+        de_wide = tile("de2", [P, AHEAD + SLOTS], F32, "e_c2")
+        de = [de_wide[:, AHEAD:] if t == 2 else tile("de%d" % t, [P, SLOTS], F32, "e_c%d" % t) for t in range(LANES)]
+        de_last = de_wide[:, 0 : CUTS[3] - CUTS[2]]
         quarter = WORDS // 4
         tags = ("e_lane0", "e_lane2", "e_lane3", "w_lane0")
         halves = [tile("halves%d" % k, [P, 2, SPANS[k + 1] - SPANS[k], 2], BF16, tag) for k, tag in enumerate(tags)]
         out_bf = tile("out_bf", [P, WORDS * LANES], BF16, "pairs_then_out")
 
-        def look_up(move, t, lo, hi):
-            move(de[t][:, lo:hi], dh[t][:].indirect(entries(posn_list, lo, hi)))
+        def look_up(move, t, lo, hi, target=None):
+            move(de[t][:, lo:hi] if target is None else target, dh[t][:].indirect(entries(posn_list, lo, hi)))
 
-        def place(move, t, lo, hi):
-            move(grad[t][:].indirect(entries(ctx_list, lo, hi)), de[t][:, lo:hi])
+        def place(move, t, lo, hi, source=None):
+            move(grad[t][:].indirect(entries(ctx_list, lo, hi)), de[t][:, lo:hi] if source is None else source)
 
         def store(queue, t):
             queue.dma_start(out_rows[:, t, :], grad[t][:])
@@ -343,8 +346,7 @@ def tile_attend_gcbow_ns_pl_kernel(tc, eT, wT, ts, ux, y, coffs, posnoffs, sloto
         place(on_scalar, 0, CUTS[1], CUTS[2])
         look_up(on_scalar, 2, 0, SLOTS)
         place(on_scalar, 0, CUTS[2], CUTS[3])
-        look_up(on_vector, 3, 0, CUTS[1])
-        look_up(on_vector, 3, CUTS[1], LOOK3)
+        look_up(on_vector, 3, 0, LOOK3)
         look_up(on_scalar, 3, LOOK3, CUTS[2])
         store(nc.scalar, 0)
         for k in (1, 2, 0, 3):
@@ -352,10 +354,11 @@ def tile_attend_gcbow_ns_pl_kernel(tc, eT, wT, ts, ux, y, coffs, posnoffs, sloto
         place(on_vector, 2, 0, SLOTS)
         store(nc.sync, 2)
         place(on_scalar, 3, CUTS[0], CUTS[1])
-        look_up(on_scalar, 3, CUTS[2], CUTS[3])
+        look_up(on_scalar, 3, CUTS[2], CUTS[2] + AHEAD, de_last[:, :AHEAD])
+        look_up(on_vector, 3, CUTS[2] + AHEAD, CUTS[3], de_last[:, AHEAD:])
         place(on_scalar, 3, CUTS[1], CUTS[2])
         round_lane(on_scalar, 2, 1)
-        place(on_scalar, 3, CUTS[2], CUTS[3])
+        place(on_scalar, 3, CUTS[2], CUTS[3], de_last)
         store(nc.sync, 3)
         for k in (3, 2, 0):
             round_lane(on_vector, 2, k)

@@ -332,6 +332,11 @@ def tile_attend_gcbow_ns_pl_kernel(tc, eT, wT, ts, ux, y, coffs, posnoffs, sloto
                 out_bf[:, LANES * lo : LANES * hi].bitcast(word).rearrange("p (col u) -> p col u", u=2),
                 words[:, :, lo - first : hi - first].rearrange("p u col -> p col u"))
 
+        def weave_pairs(k):
+            on_vector(
+                out_bf[:, LANES * SPANS[k] : LANES * SPANS[k + 1]].rearrange("p (col u e) -> p col u e", u=2, e=2),
+                halves[k][:].rearrange("p u col e -> p col u e"))
+
         look_up(on_scalar, 0, CUTS[0], CUTS[1])
         look_up(on_scalar, 0, CUTS[1], CUTS[3])
         look_up(on_vector, 1, 0, SLOTS // 2)
@@ -382,7 +387,7 @@ def tile_attend_gcbow_ns_pl_kernel(tc, eT, wT, ts, ux, y, coffs, posnoffs, sloto
         weave_out(nc.scalar.copy, U32, 3, 2 * quarter, 3 * quarter)
         weave_out(nc.scalar.copy, U32, 3, 3 * quarter, WORDS - PIECE)
         weave_out(nc.scalar.copy, U32, 3, WORDS - PIECE, WORDS)
-        weave_out(on_vector, I32, 0)
+        weave_pairs(0)
         pack_and_store(quarter, 2 * quarter)
         pack_and_store(0, quarter)
         pack_and_store(2 * quarter, 3 * quarter)

@@ -77,6 +77,8 @@ def tile_attend_gcbow_ns_pl_kernel(tc, eT, wT, ts, ux, y, coffs, posnoffs, sloto
         dh = [tile("dh%d" % t, [P, DH_COLUMNS[t]], F32) for t in range(LANES)]
         grad = {t: tile("grad%d" % t, [P, WORDS], F32) for t in (0, 1, 3)}
 
+        nc.scalar.dma_start(ts_table[P - 1 : P, :], ts[0:1, :])
+        nc.scalar.dma_start(ux_row[P - 1 : P, :], ux.rearrange("x one -> one x"))
         warm = tile("warm", [P, 2], F32)
         nc.gpsimd.memset(warm[:, 0:1], 0.0)
         nc.scalar.activation(warm[:, 1:2], warm[:, 0:1], ACT.Sigmoid)
@@ -91,12 +93,10 @@ def tile_attend_gcbow_ns_pl_kernel(tc, eT, wT, ts, ux, y, coffs, posnoffs, sloto
         for t in (1, 0, 3):
             nc.gpsimd.memset(grad[t][:], 0.0)
 
-        nc.sync.dma_start(ts_table[P - 1 : P, :], ts[0:1, :])
         nc.sync.dma_start(idx_list[:], offs)
         nc.sync.dma_start(e_lane[0][:], e_rows[:, 0, :])
         nc.sync.dma_start(ctx_list[:], coffs)
         nc.sync.dma_start(slot_list[:], slotoffs)
-        nc.sync.dma_start(ux_row[P - 1 : P, :], ux.rearrange("x one -> one x"))
         for t in range(1, LANES):
             nc.sync.dma_start(e_lane[t][:], e_rows[:, t, :])
         for n in range(LANES - 1):
@@ -105,6 +105,12 @@ def tile_attend_gcbow_ns_pl_kernel(tc, eT, wT, ts, ux, y, coffs, posnoffs, sloto
             nc.sync.dma_start(w_lane[t][:], w_rows[:, t, :])
         nc.sync.dma_start(y_part[LANES - 1][:], y_rows[:, LANES - 1, :])
         nc.sync.dma_start(posn_list[:], posnoffs)
+
+        ux_ps = bank("ux_ps", [P, LANES, P], 5)
+        for n in range(LANES):
+            nc.tensor.transpose(ux_ps[:, n, :], ux_row[:, P * n : P * (n + 1)], identity[:])
+        nc.scalar.copy(ux_col[:], ux_ps[:, :, P - 1])
+        nc.gpsimd.tensor_scalar(minus_2ux[:], ux_col[:], -2.0, 0.0, ALU.mult, ALU.add)
 
         ts_i = tile("ts_i", [P, OUT_SLOTS], F32)
         on_vector(ts_i[:], ts_table[:].indirect(idx_list[:]))
@@ -123,11 +129,6 @@ def tile_attend_gcbow_ns_pl_kernel(tc, eT, wT, ts, ux, y, coffs, posnoffs, sloto
                 if lo < hi:
                     move(pairs[:, t, lo:hi], e_c[t][:].indirect(entries(slot_list, lo, hi)))
 
-        ux_ps = bank("ux_ps", [P, LANES, P], 5)
-        for n in range(LANES):
-            nc.tensor.transpose(ux_ps[:, n, :], ux_row[:, P * n : P * (n + 1)], identity[:])
-        nc.scalar.copy(ux_col[:], ux_ps[:, :, P - 1])
-        nc.gpsimd.tensor_scalar(minus_2ux[:], ux_col[:], -2.0, 0.0, ALU.mult, ALU.add)
         signed_ux = [tile("signed_ux%d" % n, [P, OUT_SLOTS], F32) for n in range(LANES)]
         factor = [tile("factor01", [P, LANES, 2 * P], F32), tile("factor2", [P, LANES, P], F32), tile("factor3", [P, LANES, P], F32)]
 

@@ -24,13 +24,13 @@ POS = 512
 OUT_SLOTS = 512
 LINE = 4
 CUTS = (0, 384, 768, SLOTS)
-LOOK3 = 544
+LOOK3 = 480
 AHEAD = 128
-DH_COLUMNS = (656, 528, 1040, 560)
+DH_COLUMNS = (656, 528, 1040, POS)
 CONTEXT_ON_VECTOR = (512, 768, SLOTS, SLOTS)
 PAIRS_ON_VECTOR = (256, 0, 0, 512)
 SPARE = 16
-SPANS = (0, 480, 736, 1024, WORDS)
+SPANS = (0, 416, 672, 1024, WORDS)
 PIECE = 256
 
 
@@ -310,7 +310,11 @@ def tile_attend_gcbow_ns_pl_kernel(tc, eT, wT, ts, ux, y, coffs, posnoffs, sloto
         de_last = de_wide[:, 0 : CUTS[3] - CUTS[2]]
         quarter = WORDS // 4
         tags = ("e_lane0", "e_lane2", "e_lane3", "w_lane0")
-        halves = [tile("halves%d" % k, [P, 2, SPANS[k + 1] - SPANS[k], 2], BF16, tag) for k, tag in enumerate(tags)]
+        widths = [LANES * (SPANS[k + 1] - SPANS[k]) for k in range(len(tags))]
+        room = widths[1] // 2 + 2 * (CUTS[2] - CUTS[1])
+        rows = [tile("halves%d" % k, [P, room if k == 1 else widths[k]], BF16, tag) for k, tag in enumerate(tags)]
+        halves = [row[:, :width].rearrange("p (u col e) -> p u col e", u=2, e=2) for row, width in zip(rows, widths)]
+        de_middle = rows[1][:, widths[1] // 2 :].bitcast(F32)
         out_bf = tile("out_bf", [P, WORDS * LANES], BF16, "pairs_then_out")
 
         def look_up(move, t, lo, hi, target=None):
@@ -328,7 +332,7 @@ def tile_attend_gcbow_ns_pl_kernel(tc, eT, wT, ts, ux, y, coffs, posnoffs, sloto
         def weave_out(move, word, k, lo=None, hi=None):
             first = SPANS[k]
             lo, hi = (lo or first), (hi or SPANS[k + 1])
-            words = halves[k][:].rearrange("p u col e -> p u (col e)").bitcast(word)
+            words = rows[k][:, : widths[k]].bitcast(word).rearrange("p (u col) -> p u col", u=2)
             move(
                 out_bf[:, LANES * lo : LANES * hi].bitcast(word).rearrange("p (col u) -> p col u", u=2),
                 words[:, :, lo - first : hi - first].rearrange("p u col -> p col u"))
@@ -336,7 +340,7 @@ def tile_attend_gcbow_ns_pl_kernel(tc, eT, wT, ts, ux, y, coffs, posnoffs, sloto
         def weave_pairs(k):
             on_vector(
                 out_bf[:, LANES * SPANS[k] : LANES * SPANS[k + 1]].rearrange("p (col u e) -> p col u e", u=2, e=2),
-                halves[k][:].rearrange("p u col e -> p col u e"))
+                halves[k].rearrange("p u col e -> p col u e"))
 
         look_up(on_scalar, 0, CUTS[0], CUTS[1])
         look_up(on_scalar, 0, CUTS[1], CUTS[3])
@@ -352,8 +356,9 @@ def tile_attend_gcbow_ns_pl_kernel(tc, eT, wT, ts, ux, y, coffs, posnoffs, sloto
         place(on_scalar, 0, CUTS[1], CUTS[2])
         look_up(on_scalar, 2, 0, SLOTS)
         place(on_scalar, 0, CUTS[2], CUTS[3])
-        look_up(on_vector, 3, 0, LOOK3)
-        look_up(on_scalar, 3, LOOK3, CUTS[2])
+        look_up(on_vector, 3, CUTS[0], CUTS[1])
+        look_up(on_vector, 3, CUTS[1], LOOK3, de_middle[:, : LOOK3 - CUTS[1]])
+        look_up(on_scalar, 3, LOOK3, CUTS[2], de_middle[:, LOOK3 - CUTS[1] :])
         store(nc.scalar, 0)
         for k in (1, 2, 0, 3):
             round_lane(on_gpsimd, 0, k)
@@ -362,9 +367,9 @@ def tile_attend_gcbow_ns_pl_kernel(tc, eT, wT, ts, ux, y, coffs, posnoffs, sloto
         place(on_scalar, 3, CUTS[0], CUTS[1])
         look_up(on_scalar, 3, CUTS[2], CUTS[2] + AHEAD, de_last[:, :AHEAD])
         look_up(on_vector, 3, CUTS[2] + AHEAD, CUTS[3], de_last[:, AHEAD:])
-        place(on_scalar, 3, CUTS[1], CUTS[2])
-        round_lane(on_scalar, 2, 1)
+        place(on_scalar, 3, CUTS[1], CUTS[2], de_middle)
         place(on_scalar, 3, CUTS[2], CUTS[3], de_last)
+        round_lane(on_scalar, 2, 1)
         store(nc.sync, 3)
         for k in (3, 2, 0):
             round_lane(on_vector, 2, k)

@@ -24,7 +24,7 @@ POS = 512
 OUT_SLOTS = 512
 LINE = 4
 CUTS = (0, 384, 768, SLOTS)
-LOOK3 = 480
+LOOK3 = 544
 AHEAD = 128
 DH_COLUMNS = (656, 528, 1040, POS)
 CONTEXT_ON_VECTOR = (512, 768, SLOTS, SLOTS)
@@ -298,16 +298,15 @@ def tile_attend_gcbow_ns_pl_kernel(tc, eT, wT, ts, ux, y, coffs, posnoffs, sloto
         quantize(g_mx, chunks[3], g_bf[:, chunks[3], :], E5M2)
         wi_mx[1] = mx_tiles("wi1", 2 * P, "g_bf")
         quantize(wi_mx[1], slice(0, 2 * P), w_by_i[1][:], E4M3)
-        halve_on_vector(*multiply_dh(1, 3 * P, POS, 4))
-        halve_on_scalar(*multiply_dh(0, 3 * P, POS, 5))
+        halve_on_vector(*multiply_dh(0, 3 * P, POS, 4))
+        halve_on_scalar(*multiply_dh(1, 3 * P, POS, 5))
         dh_lane2 = multiply_dh(2, 0, POS, 6)
         dh_lane3 = multiply_dh(3, 0, POS, 7)
 
         grad[2] = tile("grad2", [P, WORDS], F32, "z3")
         nc.gpsimd.memset(grad[2][:], 0.0)
-        de_wide = tile("de2", [P, AHEAD + SLOTS], F32, "e_c2")
-        de = [de_wide[:, AHEAD:] if t == 2 else tile("de%d" % t, [P, SLOTS], F32, "e_c%d" % t) for t in range(LANES)]
-        de_last = de_wide[:, 0 : CUTS[3] - CUTS[2]]
+        de = [tile("de%d" % t, [P, SLOTS if t < 3 else CUTS[1]], F32, "e_c%d" % t) for t in range(LANES)]
+        de_last = de[0][:, CUTS[2] :]
         quarter = WORDS // 4
         tags = ("e_lane0", "e_lane2", "e_lane3", "w_lane0")
         widths = [LANES * (SPANS[k + 1] - SPANS[k]) for k in range(len(tags))]

@@ -30,7 +30,7 @@ DH_COLUMNS = (656, 528, 1040, POS)
 CONTEXT_ON_VECTOR = (512, 768, SLOTS, SLOTS)
 PAIRS_ON_VECTOR = (256, 0, 0, 512)
 SPARE = 16
-SPANS = (0, 416, 672, 1024, WORDS)
+SPANS = (0, 256, 560, 1024, WORDS)
 PIECE = 256
 
 
@@ -310,10 +310,10 @@ def tile_attend_gcbow_ns_pl_kernel(tc, eT, wT, ts, ux, y, coffs, posnoffs, sloto
         quarter = WORDS // 4
         tags = ("e_lane0", "e_lane2", "e_lane3", "w_lane0")
         widths = [LANES * (SPANS[k + 1] - SPANS[k]) for k in range(len(tags))]
-        room = widths[1] // 2 + 2 * (CUTS[2] - CUTS[1])
-        rows = [tile("halves%d" % k, [P, room if k == 1 else widths[k]], BF16, tag) for k, tag in enumerate(tags)]
+        room = widths[0] // 2 + 2 * (CUTS[2] - CUTS[1])
+        rows = [tile("halves%d" % k, [P, room if k == 0 else widths[k]], BF16, tag) for k, tag in enumerate(tags)]
         halves = [row[:, :width].rearrange("p (u col e) -> p u col e", u=2, e=2) for row, width in zip(rows, widths)]
-        de_middle = rows[1][:, widths[1] // 2 :].bitcast(F32)
+        de_middle = rows[0][:, widths[0] // 2 :].bitcast(F32)
         out_bf = tile("out_bf", [P, WORDS * LANES], BF16, "pairs_then_out")
 
         def look_up(move, t, lo, hi, target=None):
@@ -359,7 +359,7 @@ def tile_attend_gcbow_ns_pl_kernel(tc, eT, wT, ts, ux, y, coffs, posnoffs, sloto
         look_up(on_vector, 3, CUTS[1], LOOK3, de_middle[:, : LOOK3 - CUTS[1]])
         look_up(on_scalar, 3, LOOK3, CUTS[2], de_middle[:, LOOK3 - CUTS[1] :])
         store(nc.scalar, 0)
-        for k in (1, 2, 0, 3):
+        for k in range(len(tags)):
             round_lane(on_gpsimd, 0, k)
         place(on_vector, 2, 0, SLOTS)
         store(nc.sync, 2)
@@ -368,37 +368,38 @@ def tile_attend_gcbow_ns_pl_kernel(tc, eT, wT, ts, ux, y, coffs, posnoffs, sloto
         look_up(on_vector, 3, CUTS[2] + AHEAD, CUTS[3], de_last[:, AHEAD:])
         place(on_scalar, 3, CUTS[1], CUTS[2], de_middle)
         place(on_scalar, 3, CUTS[2], CUTS[3], de_last)
-        round_lane(on_scalar, 2, 1)
+        round_lane(on_scalar, 2, 0)
         store(nc.sync, 3)
-        for k in (3, 2, 0):
+        for k in (3, 2, 1):
             round_lane(on_vector, 2, k)
 
         out_codes = tile("out_codes", [P, WORDS], U32, "e_lane1")
-        out_scales = tile("out_scales", [P, WORDS // 2], U8)
+        out_scales = tile("out_scales", [P, quarter], U8)
         words_hbm = out_1[0].rearrange("p col l -> p (col l)").bitcast(I32)
 
         def pack_and_store(lo, hi):
-            upper, first = divmod(lo, WORDS // 2)
-            nc.vector.quantize_mx(
-                out=out_codes[:, lo:hi].bitcast(E4M3), scales=out_scales[4 * upper :, first : first + hi - lo],
-                in_=out_bf[:, LANES * lo : LANES * hi])
+            for col in range(lo, hi, PIECE):
+                plane, first = divmod(col, quarter)
+                nc.vector.quantize_mx(
+                    out=out_codes[:, col : col + PIECE].bitcast(E4M3), scales=out_scales[4 * plane :, first : first + PIECE],
+                    in_=out_bf[:, LANES * col : LANES * (col + PIECE)])
             nc.sync.dma_start(words_hbm[:, lo:hi], out_codes[:, lo:hi].bitcast(I32))
 
-        for k in (2, 0, 3):
+        for k in (1, 2, 3):
             round_lane(on_vector, 3, k)
-        round_lane(on_scalar, 3, 1)
-        weave_out(nc.scalar.copy, U32, 2)
+        round_lane(on_scalar, 3, 0)
         weave_out(nc.scalar.copy, U32, 1)
+        weave_out(nc.scalar.copy, U32, 0)
         weave_out(nc.scalar.copy, U32, 3, 2 * quarter, 3 * quarter)
         weave_out(nc.scalar.copy, U32, 3, 3 * quarter, WORDS - PIECE)
         weave_out(nc.scalar.copy, U32, 3, WORDS - PIECE, WORDS)
-        weave_pairs(0)
-        pack_and_store(quarter, 2 * quarter)
+        weave_pairs(2)
         pack_and_store(0, quarter)
+        pack_and_store(quarter, 2 * quarter)
         pack_and_store(2 * quarter, 3 * quarter)
         pack_and_store(3 * quarter, WORDS - PIECE)
         pack_and_store(WORDS - PIECE, WORDS)
-        scales_hbm = out_2[0].bitcast(I32).rearrange("f (upper col) -> upper f col", upper=2)
+        scales_hbm = out_2[0].bitcast(I32).rearrange("f (plane col) -> plane f col", plane=4)
         for group in range(4):
             (nc.scalar if group else nc.sync).dma_start(
-                scales_hbm[:, 4 * group : 4 * group + 4, :], out_scales[32 * group : 32 * group + 8, :].bitcast(I32))
+                scales_hbm[:, 4 * group : 4 * group + 4, :], out_scales[32 * group : 32 * group + 16, :].bitcast(I32))

@@ -24,7 +24,7 @@ POS = 512
 OUT_SLOTS = 512
 LINE = 4
 CUTS = (0, 384, 768, SLOTS)
-LOOK3 = 544
+LOOK3 = 512
 AHEAD = 128
 DH_COLUMNS = (656, 528, 1040, POS)
 CONTEXT_ON_VECTOR = (512, 768, SLOTS, SLOTS)

@@ -132,10 +132,10 @@ def tile_attend_gcbow_ns_pl_kernel(tc, eT, wT, ts, ux, y, coffs, posnoffs, sloto
         signed_ux = [tile("signed_ux%d" % n, [P, OUT_SLOTS], F32) for n in range(LANES)]
         factor = [tile("factor01", [P, LANES, 2 * P], F32), tile("factor2", [P, LANES, P], F32), tile("factor3", [P, LANES, P], F32)]
 
-        def sign_labels(engine, n):
+        def sign_labels(engine, n, rs=slice(0, LANES)):
             engine.tensor_scalar(
-                signed_ux[n][:].rearrange("p (r k run) -> p k r run", r=LANES, run=LINE),
-                y_part[n][:].rearrange("p (k run r) -> p k r run", r=LANES, run=LINE),
+                signed_ux[n][:].rearrange("p (r k run) -> p k r run", r=LANES, run=LINE)[:, :, rs],
+                y_part[n][:].rearrange("p (k run r) -> p k r run", r=LANES, run=LINE)[:, :, rs],
                 minus_2ux[:, n : n + 1], ux_col[:, n : n + 1], ALU.mult, ALU.add)
 
         def turn_labels(n, target):
@@ -193,7 +193,7 @@ def tile_attend_gcbow_ns_pl_kernel(tc, eT, wT, ts, ux, y, coffs, posnoffs, sloto
 
         form_s(0, "s_bf0")
 
-        w_listed = [tile("w_listed%d" % v, [P, 2, OUT_SLOTS], BF16) for v in range(2)]
+        w_listed = [tile("w_listed0", [P, 2, OUT_SLOTS], BF16)]
         w_by_d = tile("w_by_d", [P, OUT_SLOTS, LANES], BF16)
         w_by_i = {}
         w_ps = {}
@@ -219,25 +219,26 @@ def tile_attend_gcbow_ns_pl_kernel(tc, eT, wT, ts, ux, y, coffs, posnoffs, sloto
                 w_by_d[:, :, 2 * v : 2 * v + 2].rearrange("p (r k run) e -> p k r run e", r=LANES, run=2)[:, :, rs],
                 w_listed[v][:].rearrange("p e (k run r) -> p k r run e", r=LANES, run=2)[:, :, rs])
 
+        def gather_dealt(move, t, lo, hi):
+            move(
+                w_by_d[:, :, t].rearrange("p (r o) -> p o r", r=LANES)[:, lo // LANES : hi // LANES, :],
+                w_lane[t][:].indirect(entries(idx_list, lo, hi)))
+
         gather_w(on_scalar, 0, 0, OUT_SLOTS)
-        gather_w(on_vector, 1, 0, OUT_SLOTS // 2)
-        gather_w(on_scalar, 1, OUT_SLOTS // 2, OUT_SLOTS)
+        gather_w(on_vector, 1, 0, OUT_SLOTS)
         turn_w(0, 1)
         form_s(1, "w_lane1")
         weave_w(on_vector, 0, slice(0, LANES))
-        gather_w(on_scalar, 2, 0, OUT_SLOTS)
+        gather_dealt(on_scalar, 2, 0, OUT_SLOTS)
         lay_w(0, "w_lane2")
-        gather_w(on_vector, 3, 0, OUT_SLOTS // 2)
-        gather_w(on_scalar, 3, OUT_SLOTS // 2, OUT_SLOTS)
-        sign_labels(nc.vector, 3)
-        weave_w(on_vector, 1, slice(0, 2))
-        weave_w(on_vector, 1, slice(2, 3))
-        weave_w(nc.scalar.copy, 1, slice(3, 4))
+        gather_dealt(on_scalar, 3, 0, OUT_SLOTS)
+        sign_labels(nc.vector, 3, slice(0, 2))
+        sign_labels(nc.vector, 3, slice(2, 4))
         single_factor(3)
         for half in range(2):
             cols = slice(2 * P * half, 2 * P * (half + 1))
             quantize(wd_mx, cols, w_by_d[:, cols, :], E4M3)
-        wi_mx = {0: mx_tiles("wi0", 2 * P, "w_lane3")}
+        wi_mx = {0: mx_tiles("wi0", 2 * P, "y_part3")}
         quantize(wi_mx[0], slice(0, 2 * P), w_by_i[0][:], E4M3)
 
         g_mx = mx_tiles("g", POS)
@@ -283,8 +284,14 @@ def tile_attend_gcbow_ns_pl_kernel(tc, eT, wT, ts, ux, y, coffs, posnoffs, sloto
 
         for ch in range(LANES):
             squash(ch)
-        turn_w(1, 4)
-        lay_w(1, "z3")
+        pair_ps = bank("pair_ps", [P, LANES, P], 4)
+        pair_words = w_by_d[:].rearrange("p col l -> p (col l)").bitcast(F32)
+        for r in range(LANES):
+            nc.tensor.transpose(pair_ps[:, r, :], pair_words[:, 2 * P * r + 1 : 2 * P * (r + 1) : 2], identity[:])
+        w_by_i[1] = tile("w_by_i1", [P, 2 * P, LANES], BF16, "z3")
+        nc.scalar.copy(
+            w_by_i[1][:].rearrange("o (e p) r -> o e p r", e=2),
+            pair_ps[:].rearrange("o r p -> o (r p)").bitcast(BF16).rearrange("o (r p e) -> o e p r", r=LANES, e=2))
         loss_gradient(nc.gpsimd, 0, factor_of(0, slice(0, P)))
         loss_gradient(nc.vector, 1, factor1_ps[:])
         loss_gradient(nc.vector, 2, factor_of(2, slice(0, P)))

@@ -43,8 +43,8 @@ def tile_attend_gcbow_ns_pl_kernel(tc, eT, wT, ts, ux, y, coffs, posnoffs, sloto
         def tile(name, shape, dtype, tag=None):
             return keep.tile(shape, dtype, name=name, tag=tag or name, align_bytes=64)
 
-        def bank(name, shape, number):
-            return banks.tile(shape, F32, name=name, tag="bank%d" % number)
+        def bank(name, shape, number, dtype=F32):
+            return banks.tile(shape, dtype, name=name, tag="bank%d" % number)
 
         def on_scalar(out, in_):
             nc.scalar.activation(out, in_, ACT.Copy)
@@ -84,6 +84,8 @@ def tile_attend_gcbow_ns_pl_kernel(tc, eT, wT, ts, ux, y, coffs, posnoffs, sloto
         nc.scalar.activation(warm[:, 1:2], warm[:, 0:1], ACT.Sigmoid)
         nc.gpsimd.memset(ts_table[0 : P - 1, :], 0.0)
         make_identity(nc, identity[:])
+        identity_bf = tile("identity_bf", [P, P], BF16)
+        make_identity(nc, identity_bf[:])
         nc.gpsimd.memset(ux_row[0 : P - 1, :], 0.0)
         for t in range(LANES):
             if not PAIRS_ON_VECTOR[t]:
@@ -209,15 +211,22 @@ def tile_attend_gcbow_ns_pl_kernel(tc, eT, wT, ts, ux, y, coffs, posnoffs, sloto
                 for odd in range(2):
                     nc.tensor.transpose(w_ps[v][:, e, odd, :], words[:, 2 * P * e + odd : 2 * P * (e + 1) : 2], identity[:])
 
-        def lay_w(v, tag):
+        def lay_w(move, v, tag):
             w_by_i[v] = tile("w_by_i%d" % v, [P, 2 * P, LANES], BF16, tag)
             target = w_by_i[v][:].rearrange("o col r -> o (col r)").bitcast(F32)
-            nc.scalar.copy(target.rearrange("o (e p odd) -> o e p odd", e=2, odd=2), w_ps[v][:].rearrange("o e odd p -> o e p odd"))
+            move(target.rearrange("o (e p odd) -> o e p odd", e=2, odd=2), w_ps[v][:].rearrange("o e odd p -> o e p odd"))
 
         def weave_w(move, v, rs):
             move(
                 w_by_d[:, :, 2 * v : 2 * v + 2].rearrange("p (r k run) e -> p k r run e", r=LANES, run=2)[:, :, rs],
                 w_listed[v][:].rearrange("p e (k run r) -> p k r run e", r=LANES, run=2)[:, :, rs])
+
+        def lay_lane(move, t, number, tag):
+            lane_ps = bank("lane_ps", [P, LANES, P], number, BF16)
+            for r in range(LANES):
+                nc.tensor.transpose(lane_ps[:, r, :], w_by_d[:, P * r : P * (r + 1), t], identity_bf[:])
+            w_by_i[t] = tile("w_by_i%d" % t, [P, P, LANES], BF16, tag)
+            move(w_by_i[t][:], lane_ps[:].rearrange("o r p -> o p r"))
 
         def gather_dealt(move, t, lo, hi):
             move(
@@ -229,17 +238,20 @@ def tile_attend_gcbow_ns_pl_kernel(tc, eT, wT, ts, ux, y, coffs, posnoffs, sloto
         turn_w(0, 1)
         form_s(1, "w_lane1")
         weave_w(on_vector, 0, slice(0, LANES))
+        lay_w(on_vector, 0, None)
+        wi_mx = {0: mx_tiles("wi0", 2 * P)}
+        quantize(wi_mx[0], slice(0, 2 * P), w_by_i[0][:], E4M3)
         gather_dealt(on_scalar, 2, 0, OUT_SLOTS)
-        lay_w(0, "w_lane2")
         gather_dealt(on_scalar, 3, 0, OUT_SLOTS)
         sign_labels(nc.vector, 3, slice(0, 2))
         sign_labels(nc.vector, 3, slice(2, 4))
+        lay_lane(on_vector, 2, 6, "y_part3")
         single_factor(3)
         for half in range(2):
             cols = slice(2 * P * half, 2 * P * (half + 1))
             quantize(wd_mx, cols, w_by_d[:, cols, :], E4M3)
-        wi_mx = {0: mx_tiles("wi0", 2 * P, "y_part3")}
-        quantize(wi_mx[0], slice(0, 2 * P), w_by_i[0][:], E4M3)
+        wi_mx[2] = mx_tiles("wi2", P, "w_lane3")
+        quantize(wi_mx[2], slice(0, P), w_by_i[2][:], E4M3)
 
         g_mx = mx_tiles("g", POS)
         g_bf = tile("g_bf", [P, POS, LANES], BF16)
@@ -271,8 +283,9 @@ def tile_attend_gcbow_ns_pl_kernel(tc, eT, wT, ts, ux, y, coffs, posnoffs, sloto
 
         def multiply_dh(t, lo, hi, number):
             dh_ps = bank("dh_ps", [P, hi - lo], number)
+            (codes, scales), cols = (wi_mx[0], chunks[t]) if t < 2 else (wi_mx[t], chunks[0])
             nc.tensor.matmul_mx(
-                out=dh_ps[:], lhsT=wi_mx[t // 2][0][:, chunks[t % 2]].bitcast(E4M3), lhsT_scale=wi_mx[t // 2][1][:, chunks[t % 2]],
+                out=dh_ps[:], lhsT=codes[:, cols].bitcast(E4M3), lhsT_scale=scales[:, cols],
                 rhs=g_mx[0][:, lo:hi].bitcast(E5M2), rhs_scale=g_mx[1][:, lo:hi], start=True, stop=True)
             return dh[t][:, lo:hi], dh_ps[:]
 
@@ -284,14 +297,7 @@ def tile_attend_gcbow_ns_pl_kernel(tc, eT, wT, ts, ux, y, coffs, posnoffs, sloto
 
         for ch in range(LANES):
             squash(ch)
-        pair_ps = bank("pair_ps", [P, LANES, P], 4)
-        pair_words = w_by_d[:].rearrange("p col l -> p (col l)").bitcast(F32)
-        for r in range(LANES):
-            nc.tensor.transpose(pair_ps[:, r, :], pair_words[:, 2 * P * r + 1 : 2 * P * (r + 1) : 2], identity[:])
-        w_by_i[1] = tile("w_by_i1", [P, 2 * P, LANES], BF16, "z3")
-        nc.scalar.copy(
-            w_by_i[1][:].rearrange("o (e p) r -> o e p r", e=2),
-            pair_ps[:].rearrange("o r p -> o (r p)").bitcast(BF16).rearrange("o (r p e) -> o e p r", r=LANES, e=2))
+        lay_lane(nc.scalar.copy, 3, 4, "z3")
         loss_gradient(nc.gpsimd, 0, factor_of(0, slice(0, P)))
         loss_gradient(nc.vector, 1, factor1_ps[:])
         loss_gradient(nc.vector, 2, factor_of(2, slice(0, P)))
@@ -303,8 +309,8 @@ def tile_attend_gcbow_ns_pl_kernel(tc, eT, wT, ts, ux, y, coffs, posnoffs, sloto
         halve_on_scalar(*multiply_dh(0, 2 * P, 3 * P, 2))
         halve_on_scalar(*multiply_dh(1, 2 * P, 3 * P, 3))
         quantize(g_mx, chunks[3], g_bf[:, chunks[3], :], E5M2)
-        wi_mx[1] = mx_tiles("wi1", 2 * P, "g_bf")
-        quantize(wi_mx[1], slice(0, 2 * P), w_by_i[1][:], E4M3)
+        wi_mx[3] = mx_tiles("wi3", P, "g_bf")
+        quantize(wi_mx[3], slice(0, P), w_by_i[3][:], E4M3)
         halve_on_vector(*multiply_dh(0, 3 * P, POS, 4))
         halve_on_scalar(*multiply_dh(1, 3 * P, POS, 5))
         dh_lane2 = multiply_dh(2, 0, POS, 6)

@@ -75,7 +75,7 @@ def tile_attend_gcbow_ns_pl_kernel(tc, eT, wT, ts, ux, y, coffs, posnoffs, sloto
         identity = tile("identity", [P, P], F32)
         e_c = [tile("e_c%d" % t, [P, SLOTS + (0 if PAIRS_ON_VECTOR[t] else SPARE)], F32) for t in range(LANES)]
         dh = [tile("dh%d" % t, [P, DH_COLUMNS[t]], F32) for t in range(LANES)]
-        grad = {t: tile("grad%d" % t, [P, WORDS], F32) for t in (0, 1, 3)}
+        grad = {t: tile("grad%d" % t, [P, WORDS], F32) for t in range(LANES)}
 
         nc.scalar.dma_start(ts_table[P - 1 : P, :], ts[0:1, :])
         nc.scalar.dma_start(ux_row[P - 1 : P, :], ux.rearrange("x one -> one x"))
@@ -94,6 +94,7 @@ def tile_attend_gcbow_ns_pl_kernel(tc, eT, wT, ts, ux, y, coffs, posnoffs, sloto
                 nc.gpsimd.memset(dh[t][:, POS:], 0.0)
         for t in (1, 0, 3):
             nc.gpsimd.memset(grad[t][:], 0.0)
+        nc.vector.memset(grad[2][:], 0.0)
 
         nc.sync.dma_start(idx_list[:], offs)
         nc.sync.dma_start(e_lane[0][:], e_rows[:, 0, :])
@@ -311,13 +312,12 @@ def tile_attend_gcbow_ns_pl_kernel(tc, eT, wT, ts, ux, y, coffs, posnoffs, sloto
         quantize(g_mx, chunks[3], g_bf[:, chunks[3], :], E5M2)
         wi_mx[3] = mx_tiles("wi3", P, "g_bf")
         quantize(wi_mx[3], slice(0, P), w_by_i[3][:], E4M3)
+        halve_on_vector(*multiply_dh(2, 0, 2 * P, 2))
         halve_on_vector(*multiply_dh(0, 3 * P, POS, 4))
         halve_on_scalar(*multiply_dh(1, 3 * P, POS, 5))
-        dh_lane2 = multiply_dh(2, 0, POS, 6)
+        dh_lane2 = multiply_dh(2, 2 * P, POS, 6)
         dh_lane3 = multiply_dh(3, 0, POS, 7)
 
-        grad[2] = tile("grad2", [P, WORDS], F32, "z3")
-        nc.gpsimd.memset(grad[2][:], 0.0)
         de = [tile("de%d" % t, [P, SLOTS if t < 3 else CUTS[1]], F32, "e_c%d" % t) for t in range(LANES)]
         de_last = de[0][:, CUTS[2] :]
         quarter = WORDS // 4

@@ -75,7 +75,7 @@ def tile_attend_gcbow_ns_pl_kernel(tc, eT, wT, ts, ux, y, coffs, posnoffs, sloto
         identity = tile("identity", [P, P], F32)
         e_c = [tile("e_c%d" % t, [P, SLOTS + (0 if PAIRS_ON_VECTOR[t] else SPARE)], F32) for t in range(LANES)]
         dh = [tile("dh%d" % t, [P, DH_COLUMNS[t]], F32) for t in range(LANES)]
-        grad = {t: tile("grad%d" % t, [P, WORDS], F32) for t in range(LANES)}
+        grad = {t: tile("grad%d" % t, [P, WORDS], F32) for t in (0, 1, 3)}
 
         nc.scalar.dma_start(ts_table[P - 1 : P, :], ts[0:1, :])
         nc.scalar.dma_start(ux_row[P - 1 : P, :], ux.rearrange("x one -> one x"))
@@ -94,7 +94,6 @@ def tile_attend_gcbow_ns_pl_kernel(tc, eT, wT, ts, ux, y, coffs, posnoffs, sloto
                 nc.gpsimd.memset(dh[t][:, POS:], 0.0)
         for t in (1, 0, 3):
             nc.gpsimd.memset(grad[t][:], 0.0)
-        nc.vector.memset(grad[2][:], 0.0)
 
         nc.sync.dma_start(idx_list[:], offs)
         nc.sync.dma_start(e_lane[0][:], e_rows[:, 0, :])
@@ -318,6 +317,8 @@ def tile_attend_gcbow_ns_pl_kernel(tc, eT, wT, ts, ux, y, coffs, posnoffs, sloto
         dh_lane2 = multiply_dh(2, 2 * P, POS, 6)
         dh_lane3 = multiply_dh(3, 0, POS, 7)
 
+        grad[2] = tile("grad2", [P, WORDS], F32, "z3")
+        nc.gpsimd.memset(grad[2][:], 0.0)
         de = [tile("de%d" % t, [P, SLOTS if t < 3 else CUTS[1]], F32, "e_c%d" % t) for t in range(LANES)]
         de_last = de[0][:, CUTS[2] :]
         quarter = WORDS // 4

@@ -32,6 +32,7 @@ PAIRS_ON_VECTOR = (256, 0, 0, 512)
 SPARE = 16
 SPANS = (0, 256, 560, 1024, WORDS)
 PIECE = 256
+EXTRA = 32
 
 
 def tile_attend_gcbow_ns_pl_kernel(tc, eT, wT, ts, ux, y, coffs, posnoffs, slotoffs, offs, out_0, out_1, out_2):
@@ -275,11 +276,11 @@ def tile_attend_gcbow_ns_pl_kernel(tc, eT, wT, ts, ux, y, coffs, posnoffs, sloto
                 nc.vector.tensor_tensor(z[:, rs, :], a_ps[:], factor_of(ch, slice(0, P))[:, rs, :], ALU.mult)
                 nc.scalar.activation(sig[ch][:, rs, :], z[:, rs, :], ACT.Sigmoid, scale=0.5)
 
-        def loss_gradient(engine, ch, factors):
+        def loss_gradient(engine, ch, factors, rs=slice(0, LANES), ks=slice(0, P // LINE)):
             engine.tensor_tensor(
-                g_bf[:, chunks[ch], :].rearrange("o (k run) r -> o k r run", run=LINE),
-                sig[ch][:].rearrange("o r (k run) -> o k r run", run=LINE),
-                factors.rearrange("o r (k run) -> o k r run", run=LINE), ALU.mult)
+                g_bf[:, chunks[ch], :].rearrange("o (k run) r -> o k r run", run=LINE)[:, ks, rs],
+                sig[ch][:].rearrange("o r (k run) -> o k r run", run=LINE)[:, ks, rs],
+                factors.rearrange("o r (k run) -> o k r run", run=LINE)[:, ks, rs], ALU.mult)
 
         def multiply_dh(t, lo, hi, number):
             dh_ps = bank("dh_ps", [P, hi - lo], number)
@@ -298,8 +299,10 @@ def tile_attend_gcbow_ns_pl_kernel(tc, eT, wT, ts, ux, y, coffs, posnoffs, sloto
         for ch in range(LANES):
             squash(ch)
         lay_lane(nc.scalar.copy, 3, 4, "z3")
-        loss_gradient(nc.gpsimd, 0, factor_of(0, slice(0, P)))
-        loss_gradient(nc.vector, 1, factor1_ps[:])
+        loss_gradient(nc.gpsimd, 0, factor_of(0, slice(0, P)), slice(0, 2))
+        loss_gradient(nc.gpsimd, 0, factor_of(0, slice(0, P)), slice(2, 4))
+        loss_gradient(nc.gpsimd, 1, factor_of(1, slice(0, P)), ks=slice(0, EXTRA // LINE))
+        loss_gradient(nc.vector, 1, factor1_ps[:], ks=slice(EXTRA // LINE, P // LINE))
         loss_gradient(nc.vector, 2, factor_of(2, slice(0, P)))
         quantize(g_mx, slice(0, 2 * P), g_bf[:, 0 : 2 * P, :], E5M2)
         halve_on_scalar(*multiply_dh(0, 0, 2 * P, 0))

from contextlib import ExitStack

import concourse.mybir as mybir
from concourse.masks import make_identity

FLOPS = 2 * 2 * 512 * 512 * 512

F32 = mybir.dt.float32
BF16 = mybir.dt.bfloat16
I32 = mybir.dt.int32
U32 = mybir.dt.uint32
U16 = mybir.dt.uint16
U8 = mybir.dt.uint8
E4M3 = mybir.dt.float8_e4m3fn_x4
E5M2 = mybir.dt.float8_e5m2_x4
ALU = mybir.AluOpType
ACT = mybir.ActivationFunctionType

P = 128
LANES = 4
WORDS = 2048
SLOTS = 1024
POS = 512
OUT_SLOTS = 512
LINE = 4
CUTS = (0, 384, 768, SLOTS)
LOOK3 = 512
AHEAD = 128
DH_COLUMNS = (656, 528, 1040, POS)
CONTEXT_ON_VECTOR = (512, 768, SLOTS, SLOTS)
PAIRS_ON_VECTOR = (256, 0, 0, 512)
SPARE = 16
SPANS = (0, 256, 560, 1024, WORDS)
PIECE = 256
EXTRA = 32


def tile_attend_gcbow_ns_pl_kernel(tc, eT, wT, ts, ux, y, coffs, posnoffs, slotoffs, offs, out_0, out_1, out_2):
    nc = tc.nc
    with ExitStack() as stack:
        keep = stack.enter_context(tc.tile_pool(name="keep", bufs=1))
        banks = stack.enter_context(tc.psum_pool(name="banks", bufs=1))

        def tile(name, shape, dtype, tag=None):
            return keep.tile(shape, dtype, name=name, tag=tag or name, align_bytes=64)

        def bank(name, shape, number, dtype=F32):
            return banks.tile(shape, dtype, name=name, tag="bank%d" % number)

        def on_scalar(out, in_):
            nc.scalar.activation(out, in_, ACT.Copy)

        on_vector = nc.vector.tensor_copy

        def on_gpsimd(out, in_):
            nc.gpsimd.tensor_scalar(out, in_, 1.0, 0.0, ALU.mult, ALU.add)

        def entries(offsets, lo, hi):
            return offsets[:, lo // 16 : hi // 16]

        ctx_list = tile("ctx_list", [P, SLOTS // 16], U16)
        posn_list = tile("posn_list", [P, SLOTS // 16], U16)
        slot_list = tile("slot_list", [P, SLOTS // 16], U16)
        idx_list = tile("idx_list", [P, OUT_SLOTS // 16], U16)
        e_rows = eT.rearrange("(p t) col -> p t col", t=LANES)
        w_rows = wT.rearrange("(p t) col -> p t col", t=LANES)
        out_rows = out_0.rearrange("(p t) col -> p t col", t=LANES)
        y_rows = y.rearrange("(n p) i -> p n i", p=P)
        e_lane = [tile("e_lane%d" % t, [P, WORDS], F32) for t in range(LANES)]
        w_lane = [tile("w_lane%d" % t, [P, WORDS], F32) for t in range(LANES)]
        ts_table = tile("ts_table", [P, WORDS], F32)
        y_part = [tile("y_part%d" % n, [P, OUT_SLOTS], F32) for n in range(LANES)]
        ux_row = tile("ux_row", [P, POS], F32)
        ux_col = tile("ux_col", [P, LANES], F32)
        minus_2ux = tile("minus_2ux", [P, LANES], F32)
        identity = tile("identity", [P, P], F32)
        e_c = [tile("e_c%d" % t, [P, SLOTS + (0 if PAIRS_ON_VECTOR[t] else SPARE)], F32) for t in range(LANES)]
        dh = [tile("dh%d" % t, [P, DH_COLUMNS[t]], F32) for t in range(LANES)]
        grad = {t: tile("grad%d" % t, [P, WORDS], F32) for t in (0, 1, 3)}

        nc.scalar.dma_start(ts_table[P - 1 : P, :], ts[0:1, :])
        nc.scalar.dma_start(ux_row[P - 1 : P, :], ux.rearrange("x one -> one x"))
        warm = tile("warm", [P, 2], F32)
        nc.gpsimd.memset(warm[:, 0:1], 0.0)
        nc.scalar.activation(warm[:, 1:2], warm[:, 0:1], ACT.Sigmoid)
        nc.gpsimd.memset(ts_table[0 : P - 1, :], 0.0)
        make_identity(nc, identity[:])
        identity_bf = tile("identity_bf", [P, P], BF16)
        make_identity(nc, identity_bf[:])
        nc.gpsimd.memset(ux_row[0 : P - 1, :], 0.0)
        for t in range(LANES):
            if not PAIRS_ON_VECTOR[t]:
                nc.gpsimd.memset(e_c[t][:, SLOTS:], 0.0)
            if DH_COLUMNS[t] > POS:
                nc.gpsimd.memset(dh[t][:, POS:], 0.0)
        for t in (1, 0, 3):
            nc.gpsimd.memset(grad[t][:], 0.0)

        nc.sync.dma_start(idx_list[:], offs)
        nc.sync.dma_start(e_lane[0][:], e_rows[:, 0, :])
        nc.sync.dma_start(ctx_list[:], coffs)
        nc.sync.dma_start(slot_list[:], slotoffs)
        for t in range(1, LANES):
            nc.sync.dma_start(e_lane[t][:], e_rows[:, t, :])
        for n in range(LANES - 1):
            nc.sync.dma_start(y_part[n][:], y_rows[:, n, :])
        for t in range(LANES):
            nc.sync.dma_start(w_lane[t][:], w_rows[:, t, :])
        nc.sync.dma_start(y_part[LANES - 1][:], y_rows[:, LANES - 1, :])
        nc.sync.dma_start(posn_list[:], posnoffs)

        ux_ps = bank("ux_ps", [P, LANES, P], 5)
        for n in range(LANES):
            nc.tensor.transpose(ux_ps[:, n, :], ux_row[:, P * n : P * (n + 1)], identity[:])
        nc.scalar.copy(ux_col[:], ux_ps[:, :, P - 1])
        nc.gpsimd.tensor_scalar(minus_2ux[:], ux_col[:], -2.0, 0.0, ALU.mult, ALU.add)

        ts_i = tile("ts_i", [P, OUT_SLOTS], F32)
        on_vector(ts_i[:], ts_table[:].indirect(idx_list[:]))
        ts_ps = bank("ts_ps", [P, LANES, P], 4)
        for r in range(LANES):
            nc.tensor.transpose(ts_ps[:, r, :], ts_i[:, r::LANES], identity[:])
        ts_col = tile("ts_col", [P, LANES], F32)
        nc.scalar.copy(ts_col[:], ts_ps[:, :, P - 1])

        pairs = tile("pairs", [P, LANES, SLOTS], F32, "pairs_then_out")
        for t in range(LANES):
            for move, lo, hi in ((on_vector, 0, CONTEXT_ON_VECTOR[t]), (on_scalar, CONTEXT_ON_VECTOR[t], SLOTS)):
                if lo < hi:
                    move(e_c[t][:, lo:hi], e_lane[t][:].indirect(entries(ctx_list, lo, hi)))
            for move, lo, hi in ((on_vector, 0, PAIRS_ON_VECTOR[t]), (on_scalar, PAIRS_ON_VECTOR[t], SLOTS)):
                if lo < hi:
                    move(pairs[:, t, lo:hi], e_c[t][:].indirect(entries(slot_list, lo, hi)))

        signed_ux = [tile("signed_ux%d" % n, [P, OUT_SLOTS], F32) for n in range(LANES)]
        factor = [tile("factor01", [P, LANES, 2 * P], F32), tile("factor2", [P, LANES, P], F32), tile("factor3", [P, LANES, P], F32)]

        def sign_labels(engine, n, rs=slice(0, LANES)):
            engine.tensor_scalar(
                signed_ux[n][:].rearrange("p (r k run) -> p k r run", r=LANES, run=LINE)[:, :, rs],
                y_part[n][:].rearrange("p (k run r) -> p k r run", r=LANES, run=LINE)[:, :, rs],
                minus_2ux[:, n : n + 1], ux_col[:, n : n + 1], ALU.mult, ALU.add)

        def turn_labels(n, target):
            for r in range(LANES):
                nc.tensor.transpose(target(r), signed_ux[n][:, P * r : P * (r + 1)], identity[:])

        def copy_factor(target, source):
            for r in range(LANES):
                nc.scalar.activation(target[:, r, :], source(r), ACT.Copy, scale=ts_col[:, r : r + 1])

        f_ps = [bank("f_ps", [P, 2, 2, P], v) for v in range(2)]
        for n in range(2):
            sign_labels(nc.gpsimd, n)
            turn_labels(n, lambda r: f_ps[r // 2][:, r % 2, n, :])
        copy_factor(factor[0], lambda r: f_ps[r // 2][:, r % 2].rearrange("o n p -> o (n p)"))

        def single_factor(n):
            one_ps = bank("one_ps", [P, LANES, P], n)
            turn_labels(n, lambda r: one_ps[:, r, :])
            copy_factor(factor[n - 1], lambda r: one_ps[:, r, :])

        sign_labels(nc.gpsimd, 2)
        single_factor(2)
        there_ps = bank("there_ps", [P, LANES, P], 3)
        for r in range(LANES):
            nc.tensor.transpose(there_ps[:, r, :], factor[0][:, r, P:], identity[:])
        factor_turned = tile("factor_turned", [P, LANES, P], F32, "y_part1")
        on_vector(factor_turned[:], there_ps[:])
        factor1_ps = bank("factor1_ps", [P, LANES, P], 2)
        for r in range(LANES):
            nc.tensor.transpose(factor1_ps[:, r, :], factor_turned[:, r, :], identity[:])

        def mx_tiles(name, width, tag=None):
            return tile(name + "_codes", [P, width], U32, tag), tile(name + "_scales", [P, width], U8)

        def quantize(operand, cols, grouped, fmt):
            nc.vector.quantize_mx(
                out=operand[0][:, cols].bitcast(fmt), scales=operand[1][:, cols], in_=grouped.rearrange("p col l -> p (col l)"))

        chunks = [slice(P * ch, P * (ch + 1)) for ch in range(LANES)]

        s_mx = mx_tiles("s", POS)
        s_bf = {}
        pair_view = pairs[:].rearrange("p t (k run j) -> p k t run j", run=2, j=2)

        def form_s(half, tag):
            s_bf[half] = tile("s_bf%d" % half, [P, 2 * P, LANES], BF16, tag)
            for ch in range(2):
                ks = slice(P // 2 * (2 * half + ch), P // 2 * (2 * half + ch + 1))
                nc.vector.tensor_tensor(
                    s_bf[half][:, chunks[ch], :].rearrange("p (k run) t -> p k t run", run=2),
                    pair_view[:, ks, :, :, 0], pair_view[:, ks, :, :, 1], ALU.add)
            for ch in range(2):
                quantize(s_mx, chunks[2 * half + ch], s_bf[half][:, chunks[ch], :], E4M3)

        form_s(0, "s_bf0")

        w_listed = [tile("w_listed0", [P, 2, OUT_SLOTS], BF16)]
        w_by_d = tile("w_by_d", [P, OUT_SLOTS, LANES], BF16)
        w_by_i = {}
        w_ps = {}
        wd_mx = mx_tiles("wd", OUT_SLOTS)

        def gather_w(move, t, lo, hi):
            move(w_listed[t // 2][:, t % 2, lo:hi], w_lane[t][:].indirect(entries(idx_list, lo, hi)))

        def turn_w(v, number):
            w_ps[v] = bank("w_ps", [P, 2, 2, P], number)
            words = w_listed[v][:].rearrange("p e col -> p (e col)").bitcast(F32)
            for e in range(2):
                for odd in range(2):
                    nc.tensor.transpose(w_ps[v][:, e, odd, :], words[:, 2 * P * e + odd : 2 * P * (e + 1) : 2], identity[:])

        def lay_w(move, v, tag):
            w_by_i[v] = tile("w_by_i%d" % v, [P, 2 * P, LANES], BF16, tag)
            target = w_by_i[v][:].rearrange("o col r -> o (col r)").bitcast(F32)
            move(target.rearrange("o (e p odd) -> o e p odd", e=2, odd=2), w_ps[v][:].rearrange("o e odd p -> o e p odd"))

        def weave_w(move, v, rs):
            move(
                w_by_d[:, :, 2 * v : 2 * v + 2].rearrange("p (r k run) e -> p k r run e", r=LANES, run=2)[:, :, rs],
                w_listed[v][:].rearrange("p e (k run r) -> p k r run e", r=LANES, run=2)[:, :, rs])

        def lay_lane(move, t, number, tag):
            lane_ps = bank("lane_ps", [P, LANES, P], number, BF16)
            for r in range(LANES):
                nc.tensor.transpose(lane_ps[:, r, :], w_by_d[:, P * r : P * (r + 1), t], identity_bf[:])
            w_by_i[t] = tile("w_by_i%d" % t, [P, P, LANES], BF16, tag)
            move(w_by_i[t][:], lane_ps[:].rearrange("o r p -> o p r"))

        def gather_dealt(move, t, lo, hi):
            move(
                w_by_d[:, :, t].rearrange("p (r o) -> p o r", r=LANES)[:, lo // LANES : hi // LANES, :],
                w_lane[t][:].indirect(entries(idx_list, lo, hi)))

        gather_w(on_scalar, 0, 0, OUT_SLOTS)
        gather_w(on_vector, 1, 0, OUT_SLOTS)
        turn_w(0, 1)
        form_s(1, "w_lane1")
        weave_w(on_vector, 0, slice(0, LANES))
        lay_w(on_vector, 0, None)
        wi_mx = {0: mx_tiles("wi0", 2 * P)}
        quantize(wi_mx[0], slice(0, 2 * P), w_by_i[0][:], E4M3)
        gather_dealt(on_scalar, 2, 0, OUT_SLOTS)
        gather_dealt(on_scalar, 3, 0, OUT_SLOTS)
        sign_labels(nc.vector, 3, slice(0, 2))
        sign_labels(nc.vector, 3, slice(2, 4))
        lay_lane(on_vector, 2, 6, "y_part3")
        single_factor(3)
        for half in range(2):
            cols = slice(2 * P * half, 2 * P * (half + 1))
            quantize(wd_mx, cols, w_by_d[:, cols, :], E4M3)
        wi_mx[2] = mx_tiles("wi2", P, "w_lane3")
        quantize(wi_mx[2], slice(0, P), w_by_i[2][:], E4M3)

        g_mx = mx_tiles("g", POS)
        g_bf = tile("g_bf", [P, POS, LANES], BF16)
        def score(number, ch, lanes):
            a_ps = bank("a_ps", [P, len(lanes), P], number)
            for place, r in enumerate(lanes):
                nc.tensor.matmul_mx(
                    out=a_ps[:, place, :], lhsT=wd_mx[0][:, chunks[r]].bitcast(E4M3), lhsT_scale=wd_mx[1][:, chunks[r]],
                    rhs=s_mx[0][:, chunks[ch]].bitcast(E4M3), rhs_scale=s_mx[1][:, chunks[ch]], start=True, stop=True)
            return slice(lanes[0], lanes[-1] + 1), a_ps

        scores = [[score(0, 0, (0, 1)), score(4, 0, (2, 3))]] + [[score(4 + ch, ch, range(LANES))] for ch in range(1, LANES)]
        sig = [tile("sig%d" % ch, [P, LANES, P], F32, "signed_ux%d" % ch) for ch in range(LANES)]

        def factor_of(ch, cols):
            return factor[0][:, :, chunks[ch]][:, :, cols] if ch < 2 else factor[ch - 1][:, :, cols]

        def squash(ch):
            z = tile("z%d" % ch, [P, LANES, P], F32)
            for rs, a_ps in scores[ch]:
                nc.vector.tensor_tensor(z[:, rs, :], a_ps[:], factor_of(ch, slice(0, P))[:, rs, :], ALU.mult)
                nc.scalar.activation(sig[ch][:, rs, :], z[:, rs, :], ACT.Sigmoid, scale=0.5)

        def loss_gradient(engine, ch, factors, rs=slice(0, LANES), ks=slice(0, P // LINE)):
            engine.tensor_tensor(
                g_bf[:, chunks[ch], :].rearrange("o (k run) r -> o k r run", run=LINE)[:, ks, rs],
                sig[ch][:].rearrange("o r (k run) -> o k r run", run=LINE)[:, ks, rs],
                factors.rearrange("o r (k run) -> o k r run", run=LINE)[:, ks, rs], ALU.mult)

        def multiply_dh(t, lo, hi, number):
            dh_ps = bank("dh_ps", [P, hi - lo], number)
            (codes, scales), cols = (wi_mx[0], chunks[t]) if t < 2 else (wi_mx[t], chunks[0])
            nc.tensor.matmul_mx(
                out=dh_ps[:], lhsT=codes[:, cols].bitcast(E4M3), lhsT_scale=scales[:, cols],
                rhs=g_mx[0][:, lo:hi].bitcast(E5M2), rhs_scale=g_mx[1][:, lo:hi], start=True, stop=True)
            return dh[t][:, lo:hi], dh_ps[:]

        def halve_on_scalar(target, source):
            nc.scalar.activation(target, source, ACT.Copy, scale=0.5)

        def halve_on_vector(target, source):
            nc.vector.tensor_scalar(target, source, 0.5, None, ALU.mult)

        for ch in range(LANES):
            squash(ch)
        lay_lane(nc.scalar.copy, 3, 4, "z3")
        loss_gradient(nc.gpsimd, 0, factor_of(0, slice(0, P)), slice(0, 2))
        loss_gradient(nc.gpsimd, 0, factor_of(0, slice(0, P)), slice(2, 4))
        loss_gradient(nc.gpsimd, 1, factor_of(1, slice(0, P)), ks=slice(0, EXTRA // LINE))
        loss_gradient(nc.vector, 1, factor1_ps[:], ks=slice(EXTRA // LINE, P // LINE))
        loss_gradient(nc.vector, 2, factor_of(2, slice(0, P)))
        quantize(g_mx, slice(0, 2 * P), g_bf[:, 0 : 2 * P, :], E5M2)
        halve_on_scalar(*multiply_dh(0, 0, 2 * P, 0))
        halve_on_scalar(*multiply_dh(1, 0, 2 * P, 1))
        loss_gradient(nc.vector, 3, factor_of(3, slice(0, P)))
        quantize(g_mx, chunks[2], g_bf[:, chunks[2], :], E5M2)
        halve_on_scalar(*multiply_dh(0, 2 * P, 3 * P, 2))
        halve_on_scalar(*multiply_dh(1, 2 * P, 3 * P, 3))
        quantize(g_mx, chunks[3], g_bf[:, chunks[3], :], E5M2)
        wi_mx[3] = mx_tiles("wi3", P, "g_bf")
        quantize(wi_mx[3], slice(0, P), w_by_i[3][:], E4M3)
        halve_on_vector(*multiply_dh(2, 0, 2 * P, 2))
        halve_on_vector(*multiply_dh(0, 3 * P, POS, 4))
        halve_on_scalar(*multiply_dh(1, 3 * P, POS, 5))
        dh_lane2 = multiply_dh(2, 2 * P, POS, 6)
        dh_lane3 = multiply_dh(3, 0, POS, 7)

        grad[2] = tile("grad2", [P, WORDS], F32, "z3")
        nc.gpsimd.memset(grad[2][:], 0.0)
        de = [tile("de%d" % t, [P, SLOTS if t < 3 else CUTS[1]], F32, "e_c%d" % t) for t in range(LANES)]
        de_last = de[0][:, CUTS[2] :]
        quarter = WORDS // 4
        tags = ("e_lane0", "e_lane2", "e_lane3", "w_lane0")
        widths = [LANES * (SPANS[k + 1] - SPANS[k]) for k in range(len(tags))]
        room = widths[0] // 2 + 2 * (CUTS[2] - CUTS[1])
        rows = [tile("halves%d" % k, [P, room if k == 0 else widths[k]], BF16, tag) for k, tag in enumerate(tags)]
        halves = [row[:, :width].rearrange("p (u col e) -> p u col e", u=2, e=2) for row, width in zip(rows, widths)]
        de_middle = rows[0][:, widths[0] // 2 :].bitcast(F32)
        out_bf = tile("out_bf", [P, WORDS * LANES], BF16, "pairs_then_out")

        def look_up(move, t, lo, hi, target=None):
            move(de[t][:, lo:hi] if target is None else target, dh[t][:].indirect(entries(posn_list, lo, hi)))

        def place(move, t, lo, hi, source=None):
            move(grad[t][:].indirect(entries(ctx_list, lo, hi)), de[t][:, lo:hi] if source is None else source)

        def store(queue, t):
            queue.dma_start(out_rows[:, t, :], grad[t][:])

        def round_lane(move, t, k):
            move(halves[k][:, t // 2, :, t % 2], grad[t][:, SPANS[k] : SPANS[k + 1]])

        def weave_out(move, word, k, lo=None, hi=None):
            first = SPANS[k]
            lo, hi = (lo or first), (hi or SPANS[k + 1])
            words = rows[k][:, : widths[k]].bitcast(word).rearrange("p (u col) -> p u col", u=2)
            move(
                out_bf[:, LANES * lo : LANES * hi].bitcast(word).rearrange("p (col u) -> p col u", u=2),
                words[:, :, lo - first : hi - first].rearrange("p u col -> p col u"))

        def weave_pairs(k):
            on_vector(
                out_bf[:, LANES * SPANS[k] : LANES * SPANS[k + 1]].rearrange("p (col u e) -> p col u e", u=2, e=2),
                halves[k].rearrange("p u col e -> p col u e"))

        look_up(on_scalar, 0, CUTS[0], CUTS[1])
        look_up(on_scalar, 0, CUTS[1], CUTS[3])
        look_up(on_vector, 1, 0, SLOTS // 2)
        look_up(on_vector, 1, SLOTS // 2, SLOTS)
        halve_on_vector(*dh_lane2)
        place(on_vector, 1, 0, SLOTS)
        store(nc.sync, 1)
        for k in range(len(tags)):
            round_lane(on_gpsimd, 1, k)
        place(on_scalar, 0, CUTS[0], CUTS[1])
        halve_on_scalar(*dh_lane3)
        place(on_scalar, 0, CUTS[1], CUTS[2])
        look_up(on_scalar, 2, 0, SLOTS)
        place(on_scalar, 0, CUTS[2], CUTS[3])
        look_up(on_vector, 3, CUTS[0], CUTS[1])
        look_up(on_vector, 3, CUTS[1], LOOK3, de_middle[:, : LOOK3 - CUTS[1]])
        look_up(on_scalar, 3, LOOK3, CUTS[2], de_middle[:, LOOK3 - CUTS[1] :])
        store(nc.scalar, 0)
        for k in range(len(tags)):
            round_lane(on_gpsimd, 0, k)
        place(on_vector, 2, 0, SLOTS)
        store(nc.sync, 2)
        place(on_scalar, 3, CUTS[0], CUTS[1])
        look_up(on_scalar, 3, CUTS[2], CUTS[2] + AHEAD, de_last[:, :AHEAD])
        look_up(on_vector, 3, CUTS[2] + AHEAD, CUTS[3], de_last[:, AHEAD:])
        place(on_scalar, 3, CUTS[1], CUTS[2], de_middle)
        place(on_scalar, 3, CUTS[2], CUTS[3], de_last)
        round_lane(on_scalar, 2, 0)
        store(nc.sync, 3)
        for k in (3, 2, 1):
            round_lane(on_vector, 2, k)

        out_codes = tile("out_codes", [P, WORDS], U32, "e_lane1")
        out_scales = tile("out_scales", [P, quarter], U8)
        words_hbm = out_1[0].rearrange("p col l -> p (col l)").bitcast(I32)

        def pack_and_store(lo, hi):
            for col in range(lo, hi, PIECE):
                plane, first = divmod(col, quarter)
                nc.vector.quantize_mx(
                    out=out_codes[:, col : col + PIECE].bitcast(E4M3), scales=out_scales[4 * plane :, first : first + PIECE],
                    in_=out_bf[:, LANES * col : LANES * (col + PIECE)])
            nc.sync.dma_start(words_hbm[:, lo:hi], out_codes[:, lo:hi].bitcast(I32))

        for k in (1, 2, 3):
            round_lane(on_vector, 3, k)
        round_lane(on_scalar, 3, 0)
        weave_out(nc.scalar.copy, U32, 1)
        weave_out(nc.scalar.copy, U32, 0)
        weave_out(nc.scalar.copy, U32, 3, 2 * quarter, 3 * quarter)
        weave_out(nc.scalar.copy, U32, 3, 3 * quarter, WORDS - PIECE)
        weave_out(nc.scalar.copy, U32, 3, WORDS - PIECE, WORDS)
        weave_pairs(2)
        pack_and_store(0, quarter)
        pack_and_store(quarter, 2 * quarter)
        pack_and_store(2 * quarter, 3 * quarter)
        pack_and_store(3 * quarter, WORDS - PIECE)
        pack_and_store(WORDS - PIECE, WORDS)
        scales_hbm = out_2[0].bitcast(I32).rearrange("f (plane col) -> plane f col", plane=4)
        for group in range(4):
            (nc.scalar if group else nc.sync).dma_start(
                scales_hbm[:, 4 * group : 4 * group + 4, :], out_scales[32 * group : 32 * group + 16, :].bitcast(I32))
